import numpy as np, ml_dtypes
CORES = [16,17,18,19,32,33,34,35]
N = 8
BF = ml_dtypes.bfloat16
V, M, C, B, VIS, H, ST = 4096, 256, 1024, 16, 4, 8, 3
def pack(v, words, rel, om, th):
    return {"x": np.ascontiguousarray(v.reshape(N, 128, V)).astype(np.float32).astype(BF), "wd": np.ascontiguousarray(words.reshape(N, 128, M)).astype(np.int32),
            "rt": np.ascontiguousarray(rel.reshape(N, 128, C)).astype(np.int32), "wt": np.ascontiguousarray(om.reshape(N, 128, 1)).astype(np.int32), "th": np.ascontiguousarray(th.reshape(N, 128, 1)).astype(np.int32)}
def setup_inputs(rng):
    return pack(rng.integers(0, 256, (N, 8, 16, V)), rng.integers(0, V, (N, 8, 16, M)), rng.integers(0, V, (N, 8, 16, C)), rng.integers(0, 4096, (N, 8, 16)), rng.integers(1500, 1751, (N, 8, 16)))
def setup_inputs_spread(rng):
    v = np.floor(256 * rng.random((N, 8, 16, V)) * np.exp2(-8 * rng.random((N, 8, 1, V)))).astype(np.int64)
    om = np.floor(4096 * np.exp2(-12.5 * rng.random((N, 8, 16)))).astype(np.int64)
    lev = rng.choice(np.array([300, 700, 1200, 2500, 4080]), (N, 8, 1)); th = np.floor(lev * (0.6 + 0.4 * rng.random((N, 8, 16)))).astype(np.int64)
    pw = rng.choice(np.array([1.0, 1.5, 2.0, 3.0]), (N, 8, 1, 1))
    words = np.floor(V * rng.random((N, 8, 16, M)) ** pw).astype(np.int64); rel = np.floor(V * rng.random((N, 8, 16, C)) ** pw).astype(np.int64)
    return pack(np.minimum(v, 255), np.minimum(words, V - 1), np.minimum(rel, V - 1), np.minimum(om, 4095), np.minimum(th, 4080))
def setup_inputs_ends(rng):
    v = 255 * rng.integers(0, 2, (N, 8, 16, V)); full = rng.random((N, 8)) < 0.5; full[:, 6:] = True
    v[full, :, V - 16:] = 255; v[full, :, 0] = 0
    om = 4095 * rng.integers(0, 2, (N, 8, 16))
    for q in range(N):
        a = 7 - (N - 1 - q) % 2; om[q, 6:] = 4095; om[q, 13 - a, 15] = 272
    hit = [((u * u >> 5) + 37 * u) & (C - 1) for u in (0, 16, 4095)]
    words = (V - 1) * rng.integers(0, 2, (N, 8, 16, M)); mix = rng.random((N, 8, 1, M)) < 0.2; mix[..., 0] = False; mix[..., M - 1] = False
    words = np.where(mix, rng.integers(0, V, (N, 8, 16, M)), words); words[:, :, 0, M - 1] = V - 1; words[:, :, 0, 0] = 0
    rel = (V - 1) * rng.integers(0, 2, (N, 8, 16, C)); mix = rng.random((N, 8, 1, C)) < 0.2; mix[..., hit] = False
    rel = np.where(mix, rng.integers(0, V, (N, 8, 16, C)), rel)
    rel[:, 6:, :, 0] = V - 16 + np.arange(16)
    for c in hit[1:]:
        rel[:, 6:, :, c] = 0; rel[:, 6:, 6, c] = V - 1; rel[:, 6:, 15, c] = V - 1
    pre = rng.choice(np.array([0, 4, H - 1, H, 12, 16]), (N, 8)); pre[:, 0] = 0; pre[:, 6] = 12; pre[:, 7] = 16
    th = 4080 * (np.arange(16) < pre[:, :, None]).astype(np.int64)
    for q in range(N):
        if (N - 1 - q) % 2 == 1:
            th[q, 7, 15] = 4079; th[q, 6, H - 1] = 4079
        else:
            th[q, 6, 11] = 4079
    return pack(v, words, rel, om, th)
def setup_inputs_corners(rng):
    val = np.array([0, 8, 9, 247, 248, 249]); cls = rng.choice(6, (N, 8, V), p=[0.4, 0.1, 0.1, 0.1, 0.2, 0.1])
    cls[:, ::2, 0] = 0; cls[:, 1::2, 0] = 4; cls[:, ::2, V - 1] = 4; cls[:, 1::2, V - 1] = 0
    ft = rng.integers(0, 16, (N, 8, 1, V)); v = rng.integers(0, 7, (N, 8, 16, 1)) + np.where(np.arange(16).reshape(16, 1) == ft, val[cls][:, :, None, :], 0)
    cnt = np.array([31, 8 * M, 33, 0, 63, 32, 1, 64]); order = rng.permutation(N); kk = np.arange(16).reshape(16, 1)
    words = np.zeros((N, 8, 16, M), np.int64); rel = np.zeros((N, 8, 16, C), np.int64); om = np.zeros((N, 8, 16), np.int64)
    for q in range(N):
        hit = (rng.permutation(8 * M) < int(cnt[order[q]])).reshape(8, M)
        lw = np.where(hit, rng.choice(np.array([H, 12, 15, 16]), (8, M)), rng.choice(np.array([0, 1, H - 1]), (8, M)))
        for g in range(8):
            z = np.flatnonzero(cls[q, g] == 0); b = np.flatnonzero(cls[q, g] != 0)
            za = z[rng.integers(0, len(z), (16, M))]; bb = b[rng.integers(0, len(b), (16, M))]
            words[q, g] = np.where(kk < lw[g], za, np.where(kk == lw[g], bb, rng.integers(0, V, (16, M))))
            rel[q, g] = z[rng.integers(0, len(z), (16, C))]
            m = (q + g) % 4
            if m == 1: om[q, g, int(rng.integers(0, 16))] = 4095
            if m == 2: om[q, g] = 4095
            if m == 3: om[q, g] = rng.integers(0, 4096, 16)
    return pack(v, words, rel, om, rng.choice(np.array([0, 0, 1]), (N, 8, 16)))
def setup_inputs_ties(rng):
    pr = rng.integers(0, 256, (N, 8, 16, 6)); v = np.take_along_axis(pr, rng.integers(0, 6, (N, 8, 1, V)), 3)
    dd = np.sort(np.add.reduce(np.abs(pr[:, :, :, :, None] - pr[:, :, :, None, :]), axis=2).reshape(N, 8, 36), axis=2)
    ix = np.minimum(rng.choice(np.array([20, 28, 33]), (N, 8, 1)) + rng.integers(0, 8, (N, 8, 16)), 35)
    th = np.maximum(np.take_along_axis(dd, ix, 2) - rng.integers(0, 2, (N, 8, 16)), 0)
    words = rng.integers(0, V, (N, 8, 16, M)); words[:, :, :, ::3] = words[:, :, :1, ::3].copy()
    rel = rng.integers(0, V, (N, 8, 16, C)); rel[:, :, :, ::4] = rel[:, :, :1, ::4].copy()
    om = rng.integers(0, 4096, (N, 8, 16))
    for q in range(N):
        for g in range(1, 8, 2):
            b = int(rng.integers(1, V - 2)); a = rng.integers(0, 100, 16)
            v[q, g, :, b] = a; v[q, g, :, b + 1] = a + 150; v[q, g, :, V - 1] = a + 100; v[q, g, :, 0] = a + 100; v[q, g, int(rng.integers(0, 16)), 0] += 1
            u = int(np.add.reduce(om[q, g] * a)) & 4095; c = ((u * u >> 5) + 37 * u) & (C - 1)
            rel[q, g, :, c] = b + 1; rel[q, g, 0, c] = 0; rel[q, g, 15, c] = V - 1
            words[q, g, 0, 1::8] = b; th[q, g, 0] = 1600
    return pack(v, words, rel, om, th)
def setup_inputs_still(rng):
    far = V // 2 + rng.permutation(V // 2)[:V // 4]; zero = rng.permutation(np.setdiff1d(np.arange(V), far))[:V // 4]
    val = rng.choice(np.array([1, 8, 9, 100, 248]), (N, 8, V)); val[..., zero] = 0; val[..., far] = 0
    ft = rng.integers(0, 16, (N, 8, 1, V)); kk = np.arange(16).reshape(16, 1)
    v = rng.integers(0, 7, (N, 8, 16, 1)) + np.where(kk == ft, val[:, :, None, :], 0)
    v[:, :, 2:5, far] = 255 - rng.integers(0, 7, (N, 8, 3, V // 4))
    words = np.where((kk + rng.integers(0, 4, (N, 8, 1, M))) % 4 == 0, far[rng.integers(0, V // 4, (N, 8, 16, M))], rng.integers(0, V, (N, 8, 16, M)))
    rel = zero[rng.integers(0, V // 4, (N, 8, 16, C))]
    cnt = rng.permutation(np.array([1, 31, 33, 63])); par = int(rng.integers(0, 2))
    for q in range(par, N, 2):
        hit = np.zeros((8, M), bool); hit[:, :M // 2] = (rng.permutation(8 * (M // 2)) < int(cnt[q // 2])).reshape(8, M // 2)
        lw = rng.choice(np.array([H, 12, 16]), (8, 1, M))
        w = np.where(kk < lw, zero[rng.integers(0, V // 4, (8, 16, M))], far[rng.integers(0, V // 4, (8, 16, M))])
        words[q] = np.where(hit[:, None, :], w, words[q])
    return pack(v, words, rel, rng.integers(0, 4096, (N, 8, 16)), rng.choice(np.array([0, 0, 1]), (N, 8, 16)))
def check_inputs(d):
    bad = []
    for k, hi in (("x", 255), ("wd", V - 1), ("rt", V - 1), ("wt", 4095), ("th", 4080)):
        v = np.asarray(d[k]).astype(np.float64)
        if not (np.min(v) >= 0 and np.max(v) <= hi): bad.append("range of " + k)
        elif np.any(v != np.floor(v)): bad.append("whole numbers of " + k)
    return bad
def reference(x, wd, rt, wt, th):
    X = x.astype(np.float32).astype(np.int32).reshape(N, 8, 16, V)
    W = wd.astype(np.int64).reshape(N, 8, 16, M); RT = rt.astype(np.int64).reshape(N, 8, 16, C)
    om = wt.astype(np.int64).reshape(N, 8, 16, 1); lim = th.astype(np.int64).reshape(N, 8, 16, 1)
    A = np.zeros(N, np.int64); k = np.arange(16).reshape(1, 1, 16, 1); i = np.arange(M).reshape(1, 1, M)
    def pick(c):
        return np.take_along_axis(X, c.reshape(N, 8, 1, 16 * M), 3).reshape(N, 8, 16, 16, M)
    for t in range(VIS):
        if t > 0:
            W = np.roll(np.roll(W, ST, axis=0), (t + t // N) - (t - 1 + (t - 1) // N), axis=1)
        xw = pick(W); x0 = xw[:, :, :, 0]
        u = np.add.reduce(om * x0, axis=2) & 4095
        c = ((u * u >> 5) + 37 * u) & (C - 1)
        R = np.take_along_axis(RT, c[:, :, None, :], 3)
        s = np.argmin(np.add.reduce(np.abs(pick(R) - x0[:, :, :, None, :]), axis=2), axis=2)
        Q = np.take_along_axis(R, (s[:, :, None, :] + k) & 15, 2)
        xq = pick(Q); gap = np.add.reduce(np.abs(xw - xq), axis=2)
        ok = (gap <= lim + 8 * (A & 31).reshape(N, 1, 1, 1)).astype(np.int64)
        l = np.add.reduce(np.minimum.accumulate(ok, axis=2), axis=2)[:, :, None, :]
        rep = l >= H; uu = u[:, :, None, :]
        new = np.where(k < 16 - l, Q[:, :, ::-1] ^ 1, np.where(k < 32 - 2 * l, np.take_along_axis(W, (k + 2 * l - 16) & 15, 2), ((Q * uu >> 5) + Q) & (V - 1)))
        W = np.where(rep, new, np.take_along_axis(W, (k + l + 1) & 15, 2))
        at = (B * i + (u & (B - 1)))[:, :, None, :]
        np.put_along_axis(X, at, np.where(rep, (x0 + xq[:, :, :, 15]) >> 1, np.take_along_axis(X, at, 3)), 3)
        A = np.add.reduce(rep.reshape(N, 8 * M).astype(np.int64), axis=1)
    return {"yx": X.reshape(N, 128, V).astype(np.float32).astype(BF), "yw": W.reshape(N, 128, M).astype(np.float32)}

@@ -1,0 +1,556 @@
+from concourse.mybir import dt, AluOpType, AxisListType, ActivationFunctionType as AF
+
+NC = 2
+n = 256 // NC
+nb = n // 16
+CWID = 4096 // NC
+VIS, ST = 4, 3
+ROT = 712
+BF, FP, F16, I32, U16 = "bfloat16", "float32", "float16", "int32", "uint16"
+
+SCRATCH = {
+    "X": ("sbuf", [128, 4096 + 256], BF),
+    "RT2": ("sbuf", [128, 16384], I32),
+    "rs2": ("dram", [8, 32, 1024], I32),
+    "WI": ("sbuf", [128, 256], I32),
+    "wt0": ("sbuf", [128, 1], I32), "th0": ("sbuf", [128, 1], I32),
+    "PM": ("sbuf", [128, 2], I32), "PQ": ("sbuf", [128, 2], I32), "P5": ("sbuf", [128, 2], I32),
+    "FC": ("sbuf", [128, 16], FP), "WC": ("sbuf", [128, 2], I32),
+    "X144": ("sbuf", [128, 144], BF), "U256": ("sbuf", [128, 256], BF), "G128": ("sbuf", [128, 128], BF),
+    "K16": ("sbuf", [128, n], BF), "E32": ("sbuf", [128, 8, 32], BF), "J0": ("sbuf", [128, n], FP),
+    "IW": ("sbuf", [128, NC * nb], I32), "ALT": ("sbuf", [128, NC * nb], FP), "IDU": ("sbuf", [128, NC * nb], FP),
+    "C0": ("sbuf", [128, n], FP), "D1": ("sbuf", [128, n], FP), "TM": ("sbuf", [128, n], FP), "KB": ("sbuf", [128, n], BF),
+    "EQ0": ("sbuf", [128, 8, 32], F16), "EQ1": ("sbuf", [128, 8, 32], F16),
+    "R0": ("sbuf", [128, 16, 128], F16), "R1": ("sbuf", [128, 8, 128], F16),
+    "ZD": ("sbuf", [128, 144], BF), "ZG": ("sbuf", [128, 144], BF), "ZH": ("sbuf", [128, 144], BF), "ZL": ("sbuf", [128, 144], BF),
+    "BH": ("sbuf", [128, 128], BF), "BL": ("sbuf", [128, 128], BF),
+    "ID": ("sbuf", [128, 128], BF), "NID": ("sbuf", [128, 128], BF), "HID": ("sbuf", [128, 128], BF), "UNR": ("sbuf", [128, 128], BF),
+    "ONE": ("sbuf", [128, 128], BF), "BK1": ("sbuf", [128, 128], F16), "THd": ("sbuf", [128, n], F16), "TH": ("sbuf", [128, n], FP),
+    "CA": ("sbuf", [128, 1024], BF), "CB": ("sbuf", [128, 1024], BF), "CD": ("sbuf", [128, 1024], BF),
+    "SA": ("sbuf", [128, 1024], F16), "SW": ("sbuf", [128, 1024], F16), "SE": ("sbuf", [128, 1024], F16),
+    "RSUM": ("sbuf", [128, 1], FP), "RI": ("sbuf", [128, 1], I32), "RA": ("sbuf", [128, 1], FP),
+    "THt": ("sbuf", [128, n], FP),
+    "ZX": ("sbuf", [128, 144], F16), "ZP": ("sbuf", [128, 144], F16),
+    "UU": ("sbuf", [128, NC * nb], I32), "u15": ("sbuf", [128, NC * nb], I32), "DU": ("sbuf", [128, NC * nb], FP),
+    "LS": ("sbuf", [128, NC * n], FP), "rep": ("sbuf", [128, NC * nb], BF), "ot": ("sbuf", [128, NC * nb], FP),
+    "of": ("sbuf", [128, NC * nb], FP), "oo": ("sbuf", [128, NC * nb], U16), "AV": ("sbuf", [128, NC * n], I32),
+    "P0a": ("psum", [128, n // 2, 8], FP), "P0b": ("psum", [128, n // 2, 8], FP),
+    "PNa": ("psum", [128, 4, n], FP), "PNb": ("psum", [128, 4, n], FP),
+}
+for _h in range(NC):
+    for _nm, _sh, _d in (("XW", [128, 16 * n], BF), ("XR", [128, 16 * n], BF), ("AB", [128, n, 16], BF), ("DD", [128, 16 * n], BF),
+                         ("NT", [128, 17 * n], FP), ("RD", [128, 16 * n], FP), ("W16", [128, n], F16),
+                         ("W0u", [128, nb], U16), ("x0", [128, n], BF), ("ui", [128, nb], I32), ("vv", [128, nb], I32), ("sq", [128, nb], I32), ("cc", [128, nb], I32),
+                         ("c16", [128, nb], U16), ("Ro", [128, n], U16), ("R16", [128, n], F16), ("SC", [128, n], I32), ("s10", [128, nb], I32),
+                         ("qi", [128, nb], I32), ("qo", [128, nb], U16), ("Qo", [128, n], U16), ("Qi", [128, n], I32),
+                         ("SN", [128, n], I32), ("un", [128, n], I32), ("pr", [128, n], I32), ("ps", [128, n], I32), ("fs", [128, n], I32),
+                         ("f12", [128, n], I32), ("F16", [128, n], F16), ("q1", [128, n], I32), ("ee", [128, n], FP), ("CQ", [128, n], F16),
+                         ("ff", [128, n], FP), ("no", [128, nb], U16), ("NF", [128, n], FP), ("XO", [128, 4096 + n], BF)):
+        SCRATCH[_nm + str(_h)] = ("sbuf", _sh, _d)
+    SCRATCH["PD%d" % _h] = ("psum", [128, 512], FP)
+    SCRATCH["PU%d" % _h] = ("psum", [128, 512], FP)
+for _t in range(VIS):
+    SCRATCH["Wo%d" % _t] = ("sbuf", [128, 256], U16)
+    if _t:
+        SCRATCH["ST%d" % _t] = ("sbuf", [128, 256], U16)
+
+AL = {"sq": "ui", "qi": "ui", "s10": "vv", "SN": "pr", "fs": "pr", "f12": "ps", "ff": "ee", "no": "c16", "W0u": "qo", "NF": "ee", "R16": "CQ"}
+for _k in AL:
+    for _h in range(NC):
+        SCRATCH.pop(_k + str(_h))
+
+NDMA = 44
+SEMAPHORES = ["qV", "qA", "qT", "qG", "ls"] + ["d%d" % i for i in range(NDMA)] + ["ar%d_%d" % (t, h) for t in range(1, VIS) for h in range(NC)]
+
+CY = 0.00083
+PEC = 0.00042
+GA = 1.5
+HOP = 0.10
+
+
+def cv(cyc):
+    return 0.05 + max(64, cyc) * CY
+
+
+def ca(cyc):
+    return 0.065 + max(64, cyc) * CY
+
+
+def build(g, core, rank, T, topo):
+    ops = []
+    A = AluOpType
+    v, a, t = g.vector, g.scalar, g.tensor
+
+    def al(nm):
+        return AL[nm[:-1]] + nm[-1] if nm[:-1] in AL else nm
+
+    def add(alts, rd, wr, lat=0.0, tag=""):
+        ops.append({"alts": alts, "rd": [al(x) for x in rd], "wr": [al(x) for x in wr], "lat": lat, "tag": tag})
+
+    def V(cyc, rd, wr, fn):
+        add([("V", cv(cyc), fn)], rd, wr)
+
+    def AV(cyc, rd, wr, fv, fa):
+        add([("V", cv(cyc), fv), ("A", ca(cyc), fa)], rd, wr)
+
+    def ACT(cyc, rd, wr, fn):
+        add([("A", ca(cyc), fn)], rd, wr)
+
+    def PE(cols, rd, wr, calls):
+        def fn():
+            ins = None
+            for c in calls:
+                ins = t.matmul(*c)
+            return ins
+        add([("T", cols * PEC + 0.05, fn)], rd, wr)
+
+    def DMA(us, rd, wr, fn, q="S", tag=""):
+        add([(q, 0.08, fn)], rd, wr, lat=us, tag=tag)
+
+    def G(us, wr, fn, rd=()):
+        add([("G", us, fn)], list(rd), wr)
+
+    fl = {"allow_small_or_imprecise_dtypes": True}
+    DMA(4.5, [], ["X"], lambda: g.sync.dma_start(T.X[:, 0:4096], T.x[:, :]))
+    DMA(2.0, [], ["WI"], lambda: g.scalar.dma_start(T.WI[:], T.wd[:, :]), "D")
+    DMA(2.0, [], ["wt0"], lambda: g.scalar.dma_start(T.wt0[:], T.wt[:, :]), "D")
+    DMA(3.0, [], ["RTa"], lambda: g.sync.dma_start(T.RT2[:, ROT:1024], T.rt[:, 0:1024 - ROT]))
+    DMA(3.0, [], ["RTb"], lambda: g.sync.dma_start(T.RT2[:, 0:ROT], T.rt[:, 1024 - ROT:1024]))
+    DMA(2.0, [], ["th0"], lambda: g.sync.dma_start(T.th0[:], T.th[:, :]))
+    for i, (lo, hi, s0, s1) in enumerate(((ROT, 1024, 0, 1024 - ROT), (0, ROT, 1024 - ROT, 1024))):
+        for rr in (0, 16):
+            DMA(4.0, ["WI"], ["rs2_%d_%d" % (i, rr)],
+                lambda lo=lo, hi=hi, s0=s0, s1=s1, rr=rr: g.sync.dma_start(T.rs2[:, rr:rr + 16, lo:hi], T.rt[:, s0:s1]))
+    for s in range(1, 16):
+        DMA(4.0 + 1.3 * s, ["rs2_%d_%d" % (i, rr) for i in (0, 1) for rr in (0, 16)], ["RS%d" % s],
+            lambda s=s: g.sync.dma_start(T.RT2[:, 1024 * s:1024 * (s + 1)], T.rs2[:, s:s + 16, :]))
+    RTALL = ["RTa", "RTb"] + ["RS%d" % s for s in range(1, 16)]
+
+    G(0.2, ["PM"], lambda: g.iota(T.PM[:], [[16, 2]], 0, 1))
+    G(0.4, ["X144"], lambda: g.iota(T.X144[:], [[1, 144]], 0, 0, **fl))
+    G(0.4, ["G128"], lambda: g.iota(T.G128[:], [[16, 8], [0, 16]], 0, 0, **fl))
+    G(0.5, ["U256"], lambda: g.iota(T.U256[:], [[0, 2], [1, 128]], 0, 0, **fl))
+    G(0.4, ["K16"], lambda: g.iota(T.K16[:], [[0, nb], [1, 16]], 0, 0, **fl))
+    G(0.2, ["IW"], lambda: g.iota(T.IW[:], [[16, NC * nb]], 0, 0))
+    G(0.6, ["E32"], lambda: g.iota(T.E32[:], [[16, 8], [0, 2], [1, 16]], 0, 0, **fl))
+    G(0.4, ["J0"], lambda: g.iota(T.J0[:], [[16, nb], [0, 16]], 0, 0, **fl))
+    for nm, base, pat in (("CA", 15, [[0, 8], [16, 8], [-1, 16]]), ("CB", 14, [[-2, 8], [16, 8], [1, 16]]), ("CD", 0, [[0, 8], [16, 8], [1, 16]])):
+        G(1.9, [nm], lambda nm=nm, base=base, pat=pat: g.iota(T[nm][:], pat, base, 0, **fl))
+    for nm, base, pat in (("CA", 0, [[1, 8], [0, 8], [-1, 16]]), ("CB", -1, [[-1, 8], [0, 8], [1, 16]]),
+                          ("CB", 1, [[2, 8], [0, 8], [-1, 16]]), ("CD", 0, [[-2, 8], [0, 8], [1, 16]])):
+        G(1.9, [nm], lambda nm=nm, base=base, pat=pat: g.affine_select(T[nm][:], T[nm][:], pat, A.is_ge, -1.0, base, 0), [nm])
+    V(2, [], ["PM"], lambda: v.tensor_scalar(T.PM[:], T.PM[:], 127, None, A.bitwise_and))
+    V(2, ["PM"], ["PQ"], lambda: v.tensor_scalar(T.PQ[:], T.PM[:], 112, None, A.bitwise_and))
+    V(2, ["PM"], ["P5"], lambda: v.tensor_scalar(T.P5[:], T.PM[:], 15, None, A.bitwise_and))
+    V(2, ["PM"], ["FC0"], lambda: v.tensor_copy(T.FC[:, 0:2], T.PM[:]))
+    V(2, ["PQ"], ["FC2"], lambda: v.tensor_scalar(T.FC[:, 2:4], T.PQ[:], 15.0, None, A.add))
+    V(2, ["PQ"], ["FC4"], lambda: v.tensor_copy(T.FC[:, 4:6], T.PQ[:]))
+    V(2, ["P5"], ["FC6"], lambda: v.tensor_copy(T.FC[:, 6:8], T.P5[:]))
+    V(2, ["wt0"], ["WCa"], lambda: v.tensor_scalar(T.WC[:, 0:1], T.wt0[:], 0xFC0, None, A.bitwise_and))
+    V(2, ["wt0"], ["WCb"], lambda: v.tensor_scalar(T.WC[:, 1:2], T.wt0[:], 63, None, A.bitwise_and))
+    V(2, ["WCa", "WCb"], ["FC8"], lambda: v.tensor_copy(T.FC[:, 8:10], T.WC[:]))
+    V(2, ["th0"], ["FC10"], lambda: v.tensor_scalar(T.FC[:, 10:11], T.th0[:], -2048.0, None, A.add))
+
+    def col(i):
+        return T.FC[:, i:i + 1]
+
+    def EQ(out, src, c, mul, cyc, rd, f=None):
+        def fn():
+            if mul is None:
+                return v.tensor_scalar(T[out][:], src(), col(c), None, A.is_equal)
+            return v.tensor_scalar(T[out][:], src(), col(c), mul if f is None else col(f), A.is_equal, A.mult)
+        V(cyc, rd, [out], fn)
+    V(256, ["WI"], ["Wo0_%d" % h for h in range(NC)], lambda: v.tensor_copy(T.Wo0[:], T.WI[:]))
+    V(2, ["PM"], ["FC11"], lambda: v.tensor_scalar(T.FC[:, 11:12], T.PM[:, 0:1], 15.0, None, A.add))
+    V(2, ["FC6"], ["FC12"], lambda: v.tensor_scalar(T.FC[:, 12:13], T.FC[:, 6:7], 0.0, None, A.is_equal))
+    EQ("ZX", lambda: T.X144[:], 11, 1.0, 72, ["X144", "FC11", "FC12"], 12)
+    EQ("ZH", lambda: T.X144[:], 2, 1.0, 72, ["X144", "FC2", "FC8"], 8)
+    EQ("ZL", lambda: T.X144[:], 2, 1.0, 72, ["X144", "FC2", "FC8"], 9)
+    EQ("ZD", lambda: T.X144[:], 2, 16384.0, 72, ["X144", "FC2"])
+    EQ("ID", lambda: T.U256[:, 0:128], 0, None, 64, ["U256", "FC0"])
+    EQ("NID", lambda: T.U256[:, 0:128], 0, -1.0, 64, ["U256", "FC0"])
+    V(64, ["K16"], ["KB"], lambda: v.tensor_scalar(T.KB[:], T.K16[:], 1024.0, None, A.mult))
+    V(n, ["K16"], ["C0"], lambda: v.tensor_scalar(T.C0[:], T.K16[:], 0.0, float(2 ** 30), A.is_equal, A.mult))
+    V(nb, ["FC6"], ["IW"], lambda: v.tensor_scalar(T.IW[:], T.IW[:], col(6), None, A.add))
+    EQ("BH", lambda: T.G128[:], 4, 1.0, 64, ["G128", "FC4", "FC8"], 8)
+    EQ("BL", lambda: T.G128[:], 4, 1.0, 64, ["G128", "FC4", "FC8"], 9)
+    EQ("EQ0", lambda: T.E32[:], 0, None, 128, ["E32", "FC0"])
+    for r in range(16):
+        V(64, ["EQ0"], ["R0_%d" % r], lambda r=r: v.tensor_copy(T.R0[:, r, :], T.EQ0[:, :, r:r + 16]))
+    EQ("EQ1", lambda: T.E32[:], 1, None, 128, ["E32", "FC0"])
+    for r in range(1, 9):
+        V(64, ["EQ1"], ["R1_%d" % r], lambda r=r: v.tensor_copy(T.R1[:, r - 1, :], T.EQ1[:, :, r:r + 16]))
+    EQ("ZG", lambda: T.X144[:], 3, None, 72, ["X144", "FC2"])
+    EQ("BK1", lambda: T.G128[:], 5, None, 64, ["G128", "FC4"])
+    EQ("THd", lambda: T.K16[:], 6, 1.0, 64, ["K16", "FC6", "FC10"], 10)
+    PE(n, ["BK1", "THd"], ["PU0"], [(T.PU0[:, 0:n], T.BK1[:], T.THd[:], True, True)])
+    V(n, [], ["TH", "PU0"], lambda: v.tensor_scalar(T.TH[:], T.PU0[:, 0:n], 2048.0, None, A.add))
+    EQ("HID", lambda: T.U256[:, 0:128], 0, 0.5, 64, ["U256", "FC0"])
+    EQ("UNR", lambda: T.U256[:, 16:144], 0, None, 64, ["U256", "FC0"])
+    V(64, [], ["ONE"], lambda: v.memset(T.ONE[:], 1.0))
+    V(n, ["K16"], ["TM"], lambda: v.tensor_scalar(T.TM[:], T.K16[:], 15.0, None, A.is_equal))
+    V(n, ["FC6"], ["J0"], lambda: v.tensor_scalar(T.J0[:], T.J0[:], col(6), 1.0 / (16 * n), A.add, A.mult))
+    V(n, [], ["J0"], lambda: v.tensor_scalar(T.J0[:], T.J0[:], -8.0, None, A.add))
+    V(2 * n, ["J0", "TM"], ["D1"], lambda: v.tensor_tensor(T.D1[:], T.J0[:], T.TM[:], A.mult))
+    V(n, [], ["D1"], lambda: v.tensor_scalar(T.D1[:], T.D1[:], 0.0625, None, A.add))
+    V(nb, ["IW"], ["ALT"], lambda: v.tensor_scalar(T.ALT[:], T.IW[:], 4096.0, None, A.add))
+    V(nb, ["IW"], ["IDU"], lambda: v.tensor_scalar(T.IDU[:], T.IW[:], 15.0, -4096.0, A.mult, A.add))
+    EQ("SA", lambda: T.CA[:], 1, None, 512, ["CA", "FC0"])
+    EQ("SW", lambda: T.CB[:], 1, None, 512, ["CB", "FC0"])
+    EQ("SE", lambda: T.CD[:], 1, None, 512, ["CD", "FC0"])
+
+    X = lambda: T.X[:, 0:4096]
+    H2 = n // 2
+    dst = T.cores[(rank + ST) % len(T.cores)]
+    rid, pid, _se = topo.addr(dst)
+    eng = topo.engines(core, dst)[:8]
+    msk = sum(1 << e for e in eng)
+    pn = [0]
+    P0 = ["P0a", "P0b"]
+    PN = ["PNa", "PNb"]
+
+    for vis in range(VIS):
+        last = vis == VIS - 1
+        for h in range(NC):
+            hs = str(h)
+            W = lambda h=h, vis=vis: T["Wo%d" % vis][:, h * n:(h + 1) * n]
+            for q in range(2):
+                AV(GA * 8 * n, ["Wo%d_%d" % (vis, h), "X"], ["XW%s_%d" % (hs, q)],
+                   lambda h=h, q=q, vis=vis, hs=hs: v.tensor_copy(T["XW" + hs][:, q * 8 * n:(q + 1) * 8 * n], X().indirect(T["Wo%d" % vis][:, h * n + q * H2:h * n + (q + 1) * H2])),
+                   lambda h=h, q=q, vis=vis, hs=hs: a.activation(T["XW" + hs][:, q * 8 * n:(q + 1) * 8 * n], X().indirect(T["Wo%d" % vis][:, h * n + q * H2:h * n + (q + 1) * H2]), AF.Identity))
+        for h in range(NC):
+            hs = str(h)
+            b = lambda nm, hs=hs: T[AL.get(nm, nm) + hs]
+            UU = lambda h=h: T.UU[:, h * nb:(h + 1) * nb]
+            uun = "UU" + hs
+            V(n * 0.5, ["Wo%d_%d" % (vis, h)], ["W16" + hs],
+              lambda b=b, h=h, vis=vis: v.tensor_scalar(b("W16")[:], T["Wo%d" % vis][:, h * n:(h + 1) * n], -2048.0, None, A.add))
+            PE(64 * 16, ["W16" + hs, "ZX"], ["PU" + hs],
+               [(b("PU")[:, 496:496 + nb], T.ZX[:, 15 - m:143 - m], b("W16")[:, m::16], m == 0, m == 15) for m in range(16)])
+            V(nb, [], ["PU" + hs, "W0u" + hs], lambda b=b: v.tensor_scalar(b("W0u")[:], b("PU")[:, 496:496 + nb], 2048.0, None, A.add))
+            AV(GA * n, ["W0u" + hs, "X"], ["x0" + hs], lambda b=b: v.tensor_copy(b("x0")[:], X().indirect(b("W0u")[:])),
+               lambda b=b: a.activation(b("x0")[:], X().indirect(b("W0u")[:]), AF.Identity))
+            calls = []
+            for m in range(16):
+                for z in ("ZH", "ZL"):
+                    calls.append((b("PU")[:, 0:nb], T[z][:, 15 - m:143 - m], b("x0")[:, m::16], m == 0 and z == "ZH", m == 15 and z == "ZL"))
+            PE(64 * 32, ["x0" + hs, "ZH", "ZL"], ["PU" + hs], calls)
+            V(nb, [], ["PU" + hs, "ui" + hs], lambda b=b: v.tensor_copy(b("ui")[:], b("PU")[:, 0:nb]))
+            V(nb, ["ui" + hs], [uun], lambda b=b, UU=UU: v.tensor_scalar(UU(), b("ui")[:], 4095, None, A.bitwise_and))
+            V(nb, [uun], ["vv" + hs], lambda b=b, UU=UU: v.tensor_scalar(b("vv")[:], UU(), 592.0, None, A.add))
+            V(nb, ["vv" + hs], ["sq" + hs], lambda b=b: v.tensor_tensor(b("sq")[:], b("vv")[:], b("vv")[:], A.mult))
+            V(nb, ["sq" + hs], ["cc" + hs], lambda b=b: v.tensor_scalar(b("cc")[:], b("sq")[:], 5, 1023, A.arith_shift_right, A.bitwise_and))
+            V(nb, ["cc" + hs], ["c16" + hs], lambda b=b: v.tensor_copy(b("c16")[:], b("cc")[:]))
+            V(GA * n, ["c16" + hs, "RTa", "RTb"], ["Ro" + hs], lambda b=b: v.tensor_copy(b("Ro")[:], T.RT2[:, 0:1024].indirect(b("c16")[:])))
+            PE(2 * n, ["x0" + hs, "BH", "BL"], ["PU" + hs], [(b("PU")[:, n:2 * n], T.BH[:], b("x0")[:], True, False),
+                                                           (b("PU")[:, n:2 * n], T.BL[:], b("x0")[:], False, True)])
+            V(n, [], ["PU" + hs, "SN" + hs], lambda b=b: v.tensor_copy(b("SN")[:], b("PU")[:, n:2 * n]))
+            V(n, ["SN" + hs], ["un" + hs], lambda b=b: v.tensor_scalar(b("un")[:], b("SN")[:], 4095, None, A.bitwise_and))
+        V(NC * nb, ["UU%d" % h for h in range(NC)], ["u15"], lambda: v.tensor_scalar(T.u15[:], T.UU[:], 15, None, A.bitwise_and))
+        if not last:
+            V(2 * NC * nb, ["u15", "IDU"], ["DU"], lambda: v.tensor_tensor(T.DU[:], T.u15[:], T.IDU[:], A.add))
+        else:
+            for h in range(NC):
+                V(2 * nb, ["u15", "IDU"], ["DU%d" % h, "DU"], lambda h=h: v.tensor_tensor(T.DU[:, h * nb:(h + 1) * nb], T.u15[:, h * nb:(h + 1) * nb], T.IDU[:, 0:nb], A.add))
+        for h in range(NC):
+            hs = str(h)
+            b = lambda nm, hs=hs: T[AL.get(nm, nm) + hs]
+            if vis == 0:
+                V(n * 0.5, ["Ro" + hs], ["R16" + hs], lambda b=b: v.tensor_scalar(b("R16")[:], b("Ro")[:], -2048.0, None, A.add))
+                for r4 in range(4):
+                    p = PN[pn[0] % 2]
+                    pn[0] += 1
+                    PE(4 * n, ["R16" + hs] + ["R0_%d" % r for r in range(4 * r4, 4 * r4 + 4)], [p],
+                       [(T[p][:, i, :], T.R0[:, 4 * r4 + i, :], b("R16")[:], True, True) for i in range(4)])
+                    AV(4 * n, [], [p, "RD%s_%d" % (hs, r4)],
+                       lambda b=b, p=p, r4=r4: v.tensor_scalar(b("RD")[:, 4 * n * r4:4 * n * (r4 + 1)], T[p][:], 2048.0, None, A.add),
+                       lambda b=b, p=p, r4=r4: a.activation(b("RD")[:, 4 * n * r4:4 * n * (r4 + 1)], T[p][:], AF.Identity, bias=2048.0))
+            for q in range(2):
+                AV(GA * 8 * n, ["Ro" + hs, "X"], ["XR%s_%d" % (hs, q)],
+                   lambda b=b, q=q: v.tensor_copy(b("XR")[:, q * 8 * n:(q + 1) * 8 * n], X().indirect(b("Ro")[:, q * H2:(q + 1) * H2])),
+                   lambda b=b, q=q: a.activation(b("XR")[:, q * 8 * n:(q + 1) * 8 * n], X().indirect(b("Ro")[:, q * H2:(q + 1) * H2]), AF.Identity))
+            for w in range(2):
+                w0, w1 = w * H2, (w + 1) * H2
+                for o in range(2):
+                    p = P0[o]
+                    calls = []
+                    for kk in range(8):
+                        calls.append((T[p][:, :, kk], T.ID[:], b("XR")[:, 16 * w0 + 8 * o + kk:16 * w1:16], True, False))
+                        calls.append((T[p][:, :, kk], T.NID[:], b("x0")[:, w0:w1], False, True))
+                    PE(8 * n, ["XR%s_%d" % (hs, w), "x0" + hs, "ID", "NID"], [p], calls)
+                    ACT(4 * n, [], [p, "AB%s_%d%d" % (hs, w, o)],
+                        lambda b=b, p=p, o=o, w0=w0, w1=w1: a.activation(b("AB")[:, w0:w1, 8 * o:8 * o + 8], T[p][:], AF.Abs))
+                calls = [(b("PD")[:, w0:w1], T.ID[:], T.KB[:, w0:w1], True, False)]
+                for m in range(16):
+                    calls.append((b("PD")[:, w0:w1], T.ZD[:, 15 - m:143 - m], b("AB")[:, w0 + m:w1:16, :], False, m == 15))
+                PE(17 * H2, ["AB%s_%d%d" % (hs, w, o) for o in range(2)] + ["ZD", "KB", "ID"], ["PD" + hs], calls)
+            V(n, ["C0"], ["PD" + hs, "SC" + hs], lambda b=b: v.tensor_tensor_scan(b("SC")[:], T.C0[:], b("PD")[:, 0:n], 0.0, A.max, A.min))
+            if vis == 0:
+                sh = 10 - (n.bit_length() - 1)
+                V(nb, ["SC" + hs], ["s10" + hs], lambda b=b: v.tensor_scalar(b("s10")[:], b("SC")[:, 15::16], 0x3C00, sh, A.bitwise_and, A.arith_shift_right))
+                V(2 * nb, ["s10" + hs, "IW"], ["qi" + hs], lambda b=b: v.tensor_tensor(b("qi")[:], b("s10")[:], T.IW[:, 0:nb], A.add))
+            else:
+                V(nb, ["SC" + hs], ["s10" + hs], lambda b=b: v.tensor_scalar(b("s10")[:], b("SC")[:, 15::16], 0x3C00, None, A.bitwise_and))
+                V(2 * nb, ["s10" + hs, "cc" + hs], ["qi" + hs], lambda b=b: v.tensor_tensor(b("qi")[:], b("s10")[:], b("cc")[:], A.add))
+            V(nb, ["qi" + hs], ["qo" + hs], lambda b=b: v.tensor_copy(b("qo")[:], b("qi")[:]))
+            if vis == 0:
+                V(GA * n, ["qo" + hs] + ["RD%s_%d" % (hs, r4) for r4 in range(4)], ["Qo" + hs], lambda b=b: v.tensor_copy(b("Qo")[:], b("RD")[:].indirect(b("qo")[:])))
+            else:
+                V(GA * n, ["qo" + hs] + RTALL, ["Qo" + hs], lambda b=b: v.tensor_copy(b("Qo")[:], T.RT2[:].indirect(b("qo")[:])))
+        for h in range(NC):
+            hs = str(h)
+            b = lambda nm, hs=hs: T[nm + hs]
+            for j4 in (9, 13):
+                p = PN[pn[0] % 2]
+                pn[0] += 1
+                PE(4 * n, ["W16" + hs] + ["R1_%d" % (17 - j) for j in range(j4, j4 + 4)], [p],
+                   [(T[p][:, i, :], T.R1[:, 16 - (j4 + i), :], b("W16")[:], True, True) for i in range(4)])
+                AV(4 * n, [], [p, "NT%s_%d" % (hs, j4)],
+                   lambda b=b, p=p, j4=j4: v.tensor_scalar(b("NT")[:, n * j4:n * (j4 + 4)], T[p][:], 2048.0, None, A.add),
+                   lambda b=b, p=p, j4=j4: a.activation(b("NT")[:, n * j4:n * (j4 + 4)], T[p][:], AF.Identity, bias=2048.0))
+        for h in range(NC):
+            hs = str(h)
+            b = lambda nm, hs=hs: T[AL.get(nm, nm) + hs]
+            for q in range(2):
+                w0, w1 = q * H2, (q + 1) * H2
+                if q < SPL:
+                    V(GA * 8 * n, ["Qo" + hs, "X", "XW%s_%d" % (hs, q)], ["DD%s_%d" % (hs, q)],
+                      lambda b=b, q=q: v.tensor_tensor(b("DD")[:, q * 8 * n:(q + 1) * 8 * n], X().indirect(b("Qo")[:, q * H2:(q + 1) * H2]), b("XW")[:, q * 8 * n:(q + 1) * 8 * n], A.subtract))
+                    ACT(8 * n, ["DD%s_%d" % (hs, q)], ["AB%s_%d0" % (hs, q), "AB%s_%d1" % (hs, q)],
+                        lambda b=b, q=q: a.activation(b("AB")[:, q * H2:(q + 1) * H2, :], b("DD")[:, q * 8 * n:(q + 1) * 8 * n], AF.Abs))
+                else:
+                    ACT(GA * 8 * n, ["Qo" + hs, "X"], ["DD%s_%d" % (hs, q)],
+                        lambda b=b, q=q: a.activation(b("DD")[:, q * 8 * n:(q + 1) * 8 * n], X().indirect(b("Qo")[:, q * H2:(q + 1) * H2]), AF.Identity))
+                    for o in range(2):
+                        p = P0[o]
+                        calls = []
+                        for kk in range(8):
+                            calls.append((T[p][:, :, kk], T.ID[:], b("DD")[:, 16 * w0 + 8 * o + kk:16 * w1:16], True, False))
+                            calls.append((T[p][:, :, kk], T.NID[:], b("XW")[:, 16 * w0 + 8 * o + kk:16 * w1:16], False, True))
+                        PE(8 * n, ["DD%s_%d" % (hs, q), "XW%s_%d" % (hs, q), "ID", "NID"], [p], calls)
+                        ACT(4 * n, [], [p, "AB%s_%d%d" % (hs, q, o)],
+                            lambda b=b, p=p, o=o, w0=w0, w1=w1: a.activation(b("AB")[:, w0:w1, 8 * o:8 * o + 8], T[p][:], AF.Abs))
+                calls = []
+                for m in range(16):
+                    calls.append((b("PD")[:, q * H2:(q + 1) * H2], T.ZG[:, 15 - m:143 - m], b("AB")[:, q * H2 + m:(q + 1) * H2:16, :], m == 0, m == 15))
+                PE(16 * H2, ["AB%s_%d%d" % (hs, q, i) for i in range(2)] + ["ZG"], ["PD" + hs], calls)
+            DDr = ["DD%s_0" % hs, "DD%s_1" % hs]
+            XWr = ["XW%s_0" % hs, "XW%s_1" % hs]
+            V(n, ["Qo" + hs], ["Qi" + hs], lambda b=b: v.tensor_copy(b("Qi")[:], b("Qo")[:]))
+            V(2 * n, ["Qi" + hs, "un" + hs], ["pr" + hs], lambda b=b: v.tensor_tensor(b("pr")[:], b("Qi")[:], b("un")[:], A.mult))
+            V(n, ["pr" + hs], ["ps" + hs], lambda b=b: v.tensor_scalar(b("ps")[:], b("pr")[:], 5, None, A.arith_shift_right))
+            V(2 * n, ["ps" + hs, "Qi" + hs], ["fs" + hs], lambda b=b: v.tensor_tensor(b("fs")[:], b("ps")[:], b("Qi")[:], A.add))
+            V(n, ["fs" + hs], ["f12" + hs], lambda b=b: v.tensor_scalar(b("f12")[:], b("fs")[:], 4095, None, A.bitwise_and))
+            V(n, ["f12" + hs], ["F16" + hs], lambda b=b: v.tensor_scalar(b("F16")[:], b("f12")[:], -2048.0, None, A.add))
+            V(n, ["Qi" + hs], ["q1" + hs], lambda b=b: v.tensor_scalar(b("q1")[:], b("Qi")[:], 1, None, A.bitwise_and))
+            V(n, ["q1" + hs], ["ee" + hs], lambda b=b: v.tensor_scalar(b("ee")[:], b("q1")[:], -2.0, -2047.0, A.mult, A.add))
+            V(2 * n, ["ee" + hs, "Qi" + hs], ["CQ" + hs], lambda b=b: v.tensor_tensor(b("CQ")[:], b("ee")[:], b("Qi")[:], A.add))
+            for js in ((0, 1, 2, 3), (4, 5, 6, 7), (8,)):
+                p = PN[pn[0] % 2]
+                pn[0] += 1
+                calls = []
+                for i, j in enumerate(js):
+                    lst = []
+                    if j > 0:
+                        lst.append((T.SW[:, 128 * (j - 1):128 * j], b("W16")[:]))
+                        lst.append((T.SA[:, 128 * (j - 1):128 * j], b("CQ")[:]))
+                    if j < 8:
+                        lst.append((T.SE[:, 128 * j:128 * (j + 1)], b("F16")[:]))
+                    for z, (l_, r_) in enumerate(lst):
+                        calls.append((T[p][:, i, :], l_, r_, z == 0, z == len(lst) - 1))
+                PE(len(calls) * n, ["W16" + hs, "CQ" + hs, "F16" + hs, "SA", "SW", "SE"], [p], calls)
+                k = len(js)
+                AV(k * n, [], [p, "NT%s_%d" % (hs, js[0])],
+                   lambda b=b, p=p, k=k, j=js[0]: v.tensor_scalar(b("NT")[:, n * j:n * (j + k)], T[p][:, 0:k, :], 2048.0, None, A.add),
+                   lambda b=b, p=p, k=k, j=js[0]: a.activation(b("NT")[:, n * j:n * (j + k)], T[p][:, 0:k, :], AF.Identity, bias=2048.0))
+            calls = []
+            for q in range(2):
+                o_ = b("PU")[:, 2 * n + q * H2:2 * n + (q + 1) * H2]
+                calls.append((o_, T.HID[:], b("DD")[:, 8 * n * q + 15:8 * n * (q + 1):16], True, False))
+                if q < SPL:
+                    calls.append((o_, T.HID[:], b("XW")[:, 8 * n * q + 15:8 * n * (q + 1):16], False, False))
+                calls.append((o_, T.HID[:], b("x0")[:, q * H2:(q + 1) * H2], False, True))
+            PE(3 * n, DDr + XWr + ["HID", "x0" + hs], ["PU" + hs], calls)
+            V(n, [], ["PU" + hs, "AV" + hs], lambda b=b, h=h: v.tensor_scalar(T.AV[:, h * n:(h + 1) * n], b("PU")[:, 2 * n:3 * n], -0.25, None, A.add))
+        thn = "TH" if vis == 0 else "THt"
+        for h in range(NC):
+            hs = str(h)
+            b = lambda nm, hs=hs: T[AL.get(nm, nm) + hs]
+            V(n, [thn], ["PD" + hs, "ff" + hs], lambda b=b, thn=thn: v.tensor_tensor(b("ff")[:], b("PD")[:, 0:n], T[thn][:], A.is_gt))
+            V(n, ["ff" + hs, "D1"], ["LS" + hs], lambda b=b, h=h: v.tensor_tensor_scan(T.LS[:, h * n:(h + 1) * n], b("ff")[:], T.D1[:], -8.0, A.max, A.add))
+            V(nb, ["LS" + hs], ["no" + hs], lambda b=b, h=h: v.tensor_scalar(b("no")[:], T.LS[:, h * n + 15:(h + 1) * n:16], 16.0 * n, 7.0 * 16 * n, A.mult, A.add))
+            NTr = ["NT%s_%d" % (hs, j) for j in (0, 4, 8, 9, 13)]
+            if last:
+                V(GA * n, ["no" + hs] + NTr, ["NF" + hs], lambda b=b: v.tensor_copy(b("NF")[:], b("NT")[:].indirect(b("no")[:])))
+                DMA(2.0, ["NF" + hs], ["yw%s_0" % hs], lambda b=b, h=h: g.sync.dma_start(T.yw[0:112, h * n:(h + 1) * n], b("NF")[16:128, :]))
+                DMA(2.0, ["NF" + hs], ["yw%s_1" % hs], lambda b=b, h=h: g.sync.dma_start(T.yw[112:128, h * n:(h + 1) * n], b("NF")[0:16, :]))
+            else:
+                st = "ST%d_%d" % (vis + 1, h)
+                V(GA * n, ["no" + hs] + NTr, [st], lambda b=b, h=h, vis=vis: v.tensor_copy(T["ST%d" % (vis + 1)][:, h * n:(h + 1) * n], b("NT")[:].indirect(b("no")[:])))
+                add([("R", 1.0, lambda h=h, vis=vis: g.remote_dma(T["Wo%d" % (vis + 1)][:, h * n:(h + 1) * n], T["ST%d" % (vis + 1)][:, h * n:(h + 1) * n], T.sem["ar%d_%d" % (vis + 1, h)],
+                                                                        T.sem.ls, pid, rid, msk))], [st], ["Wo%d_%d" % (vis + 1, h)], lat=3.0, tag="ar%d_%d" % (vis + 1, h))
+        for hh in ([(h,) for h in range(NC)] if last else [tuple(range(NC))]):
+            lo, hi = hh[0], hh[-1] + 1
+            rn = ["rep%d" % h for h in hh]
+            hx = str(hh[-1])
+            P = "PU" + hx
+            c0, c1 = lo * nb, hi * nb
+            at = 0 if last else c0
+            V(c1 - c0, ["LS%d" % h for h in hh], rn, lambda c0=c0, c1=c1: v.tensor_scalar(T.rep[:, c0:c1], T.LS[:, 16 * c0 + 15:16 * c1:16], -6.4375, None, A.is_lt))
+            PE(64, rn + ["UNR"], [P], [(T[P][:, 400:400 + c1 - c0], T.UNR[:], T.rep[:, c0:c1], True, True)])
+            V(c1 - c0, ["DU"] + (["DU%d" % h for h in hh] if last else []), [P, "ot" + hx], lambda c0=c0, c1=c1, P=P: v.tensor_tensor(T.ot[:, c0:c1], T[P][:, 400:400 + c1 - c0], T.DU[:, c0:c1], A.mult))
+            V(2 * (c1 - c0), ["ot" + hx, "ALT"], ["of" + hx], lambda c0=c0, c1=c1, at=at: v.tensor_tensor(T.of[:, c0:c1], T.ot[:, c0:c1], T.ALT[:, at:at + c1 - c0], A.add))
+            V(c1 - c0, ["of" + hx], ["oo" + hx], lambda c0=c0, c1=c1: v.tensor_copy(T.oo[:, c0:c1], T.of[:, c0:c1]))
+            if not last:
+                V(3 * n * NC, ["AV%d" % h for h in hh] + ["oo" + hx], ["X"], lambda: v.tensor_copy(T.X[:].indirect(T.oo[:]), T.AV[:]))
+        if last:
+            for h in range(NC):
+                hs = str(h)
+                b = lambda nm, hs=hs: T[nm + hs]
+                DMA(3.5, ["X"], ["XO" + hs], lambda b=b, h=h: g.sync.dma_start(b("XO")[:, 0:CWID], T.X[:, h * CWID:(h + 1) * CWID]))
+                V(3 * n, ["AV" + hs, "oo" + hs], ["XO" + hs], lambda b=b, h=h: v.tensor_copy(b("XO")[:].indirect(T.oo[:, h * nb:(h + 1) * nb]), T.AV[:, h * n:(h + 1) * n]))
+                DMA(3.0, ["XO" + hs], ["yx" + hs], lambda b=b, h=h: g.sync.dma_start(T.yx[:, h * CWID:(h + 1) * CWID], b("XO")[:, 0:CWID]))
+        else:
+            PE(64, ["rep%d" % h for h in range(NC)] + ["ONE"], ["PU0"], [(T.PU0[:, 432:432 + NC * nb], T.ONE[:], T.rep[:], True, True)])
+            V(nb, [], ["PU0", "RSUM"], lambda: v.tensor_reduce(T.RSUM[:], T.PU0[:, 432:432 + NC * nb], AxisListType.X, A.add))
+            V(1, ["RSUM"], ["RI"], lambda: v.tensor_copy(T.RI[:], T.RSUM[:]))
+            V(1, [], ["RI"], lambda: v.tensor_scalar(T.RI[:], T.RI[:], 31, None, A.bitwise_and))
+            V(1, ["RI"], ["RA"], lambda: v.tensor_scalar(T.RA[:], T.RI[:], 8.0, None, A.mult))
+            V(n, ["TH", "RA"], ["THt"], lambda: v.tensor_scalar(T.THt[:], T.TH[:], T.RA[:, 0:1], None, A.add))
+    return ops, len(eng)
+
+
+SPL = 1
+LOOK = 0.1
+VBIAS = 1.0
+EN = {"XR1_1": "V", "XR0_0": "V", "NT0_9": "V", "NT1_9": "A", "RD0_2": "A", "XW0_1": "A", "RD0_0": "A", "RD1_0": "V", "NT1_4": "V"}
+TW = {"AV0": 0.1, "F161": -1.7, "ONE": -2.6, "LS0": 0.1, "DU": -4.5, "ui1": 3.9, "AB1_01": 0.1, "BH": -1.8, "CA": 5.5, "XR1_1": -2.1, "AB0_10": 0.5, "TM": 3.1,
+      "SE": 0.7, "EQ0": 6.4, "XR0_0": -1.6, "un0": -0.2, "Qo0": 2.0, "BK1": -0.7, "EQ1": 1.3, "ZH": -5.3, "th0": -3.9, "XW1_0": 5.5, "NT0_9": -0.6, "KB": 3.7,
+      "q10": 2.1, "ST1_1": -0.2, "SC0": -3.8, "DD0_0": -1.3, "ui0": -0.1, "RA": 2.1, "SA": 1.3, "Ro1": 1.2, "oo0": 1.8, "PNb": -1.1, "P0a": 3.5, "XW1_1": -2.9,
+      "RD0_1": -0.9, "RD0_2": -5.3, "Ro0": -0.6, "ST3_0": -1.4, "Qi1": 1.1, "DD1_0": -0.5, "q11": 0.3, "RD1_1": 0.9, "u15": 4.1, "qo0": 1.6, "c161": -0.5,
+      "yx1": -3.5, "ST3_1": -1.4, "ST2_1": -1.5, "CD": -4.0, "NID": 1.3, "C0": -3.8, "NT1_8": -2.8, "AB1_00": 3.3, "DD1_1": -0.2, "rep0": -1.0, "Wo2_0": -1.9}
+
+
+PHYS = {"V": "V", "A": "A", "D": "A", "T": "T", "G": "G", "R": "G", "S": "S"}
+
+
+def schedule(ops):
+    N = len(ops)
+    lastw, readers = {}, {}
+    for i, o in enumerate(ops):
+        d = set()
+        for r in o["rd"]:
+            if r in lastw:
+                d.add(lastw[r])
+        for w in o["wr"]:
+            if w in lastw:
+                d.add(lastw[w])
+            d.update(readers.get(w, ()))
+        d.discard(i)
+        o["dep"] = sorted(d)
+        for r in o["rd"]:
+            readers.setdefault(r, []).append(i)
+        for w in o["wr"]:
+            lastw[w] = i
+            readers[w] = []
+    succ = [[] for _ in range(N)]
+    for i, o in enumerate(ops):
+        for d in o["dep"]:
+            succ[d].append(i)
+    pri = [0.0] * N
+    for i in range(N - 1, -1, -1):
+        o = ops[i]
+        pri[i] = min(x[1] for x in o["alts"]) + o["lat"] + max([pri[s] + HOP for s in succ[i]], default=0.0)
+    for i, o in enumerate(ops):
+        pri[i] += TW.get(o["wr"][-1], 0.0)
+    left = [len(o["dep"]) for o in ops]
+    fin = [0.0] * N
+    free = {"V": 0.0, "A": 0.0, "T": 0.0, "G": 0.0, "S": 0.0}
+    cand = [i for i in range(N) if left[i] == 0]
+    rdy = {i: 0.0 for i in cand}
+    order = []
+    while cand:
+        best = None
+        ests = []
+        for i in cand:
+            for x in ops[i]["alts"]:
+                if EN.get(ops[i]["wr"][-1], x[0]) != x[0]:
+                    continue
+                st = max(free[PHYS[x[0]]], rdy[i])
+                ests.append((st, st + x[1], i, x))
+        bi = {}
+        for e in ests:
+            w = e[1] + (VBIAS if e[3][0] == "V" else 0.0)
+            if e[2] not in bi or w < bi[e[2]][0]:
+                bi[e[2]] = (w, e)
+        bi = [x[1] for x in bi.values()]
+        tmin = min(e[0] for e in bi)
+        best = max((e for e in bi if e[0] <= tmin + LOOK), key=lambda e: (pri[e[2]], -e[2]))
+        st, en, i, x = best
+        cand.remove(i)
+        ops[i]["q"], ops[i]["fn"], ops[i]["start"] = x[0], x[2], st
+        free[PHYS[x[0]]] = en
+        fin[i] = en + ops[i]["lat"]
+        order.append(i)
+        for s in succ[i]:
+            left[s] -= 1
+            if left[s] == 0:
+                cand.append(s)
+                rdy[s] = max(fin[d] for d in ops[s]["dep"]) + HOP
+    return order, max(fin)
+
+
+def rank_program(g, core, T, topo):
+    rank = T.rank_of(core)
+    if rank is None:
+        return
+    ops, neng = build(g, core, rank, T, topo)
+    order, _ = schedule(ops)
+    S = T.sem
+    handle = {"V": g.vector, "A": g.scalar, "T": g.tensor, "G": g, "S": g.sync}
+    cnt = {"V": 0, "A": 0, "T": 0, "G": 0}
+    known = {q: {} for q in handle}
+    nd, nsend = 0, 0
+    used = {}
+    for i in order:
+        o = ops[i]
+        q = PHYS[o["q"]]
+        kn = known[q]
+        need = {}
+        for d in o["dep"]:
+            sm, val = ops[d]["done"]
+            if kn.get(sm, 0) < val:
+                need[sm] = max(need.get(sm, 0), val)
+        items = sorted(need.items(), key=lambda kv: -max(ops[d]["start"] for d in o["dep"] if ops[d]["done"][0] == kv[0]))
+        for sm, val in items:
+            if kn.get(sm, 0) >= val:
+                continue
+            handle[q].wait_ge(S[sm], val)
+            kn[sm] = val
+            for d in o["dep"]:
+                if ops[d]["done"] == (sm, val):
+                    for k2, v2 in ops[d]["kn"].items():
+                        if kn.get(k2, 0) < v2:
+                            kn[k2] = v2
+        ins = o["fn"]()
+        if o["q"] in ("S", "D"):
+            sm = "d%d" % nd
+            nd += 1
+            ins.then_inc(S[sm], 16)
+            o["done"] = (sm, 16)
+            used[sm] = 16
+        elif o["q"] == "R":
+            nsend += 1
+            o["done"] = (o["tag"], neng)
+            used[o["tag"]] = neng
+        else:
+            cnt[q] += 1
+            sm = "q" + q
+            ins.then_inc(S[sm], 1)
+            o["done"] = (sm, cnt[q])
+            used[sm] = cnt[q]
+        o["kn"] = {} if o["q"] == "R" else dict(kn)
+    used["ls"] = nsend * neng
+    for sm, val in used.items():
+        if known["G"].get(sm, 0) < val:
+            g.wait_ge(S[sm], val)

@@ -3,69 +3,58 @@ from concourse.mybir import dt, AluOpType, AxisListType, ActivationFunctionType 
 NC = 2
 n = 256 // NC
 nb = n // 16
-CWID = 4096 // NC
+H2 = 64
+NP = n // H2
 VIS, ST = 4, 3
 ROT = 712
 BF, FP, F16, I32, U16 = "bfloat16", "float32", "float16", "int32", "uint16"
+PAR = {'ps': [1, 0], 'xs': [2, 2, 1, 1], 'ws': [1, 1, 2, 2], 'way': 'MMMA', 'sh': 'u', 'rl': 3.0, 'w0': 'm', 'rd': [0], 'dt': [0, 1]}
 
 SCRATCH = {
-    "X": ("sbuf", [128, 4096 + 256], BF),
-    "RT2": ("sbuf", [128, 16384], I32),
-    "rs2": ("dram", [8, 32, 1024], I32),
-    "WI": ("sbuf", [128, 256], I32),
-    "wt0": ("sbuf", [128, 1], I32), "th0": ("sbuf", [128, 1], I32),
-    "PM": ("sbuf", [128, 2], I32), "PQ": ("sbuf", [128, 2], I32), "P5": ("sbuf", [128, 2], I32),
-    "FC": ("sbuf", [128, 16], FP), "WC": ("sbuf", [128, 2], I32),
-    "X144": ("sbuf", [128, 144], BF), "U256": ("sbuf", [128, 256], BF), "G128": ("sbuf", [128, 128], BF),
-    "K16": ("sbuf", [128, n], BF), "E32": ("sbuf", [128, 8, 32], BF), "J0": ("sbuf", [128, n], FP),
-    "IW": ("sbuf", [128, NC * nb], I32), "ALT": ("sbuf", [128, NC * nb], FP), "IDU": ("sbuf", [128, NC * nb], FP),
-    "C0": ("sbuf", [128, n], FP), "D1": ("sbuf", [128, n], FP), "TM": ("sbuf", [128, n], FP), "KB": ("sbuf", [128, n], BF),
-    "EQ0": ("sbuf", [128, 8, 32], F16), "EQ1": ("sbuf", [128, 8, 32], F16),
-    "R0": ("sbuf", [128, 16, 128], F16), "R1": ("sbuf", [128, 8, 128], F16),
-    "ZD": ("sbuf", [128, 144], BF), "ZG": ("sbuf", [128, 144], BF), "ZH": ("sbuf", [128, 144], BF), "ZL": ("sbuf", [128, 144], BF),
-    "BH": ("sbuf", [128, 128], BF), "BL": ("sbuf", [128, 128], BF),
-    "ID": ("sbuf", [128, 128], BF), "NID": ("sbuf", [128, 128], BF), "HID": ("sbuf", [128, 128], BF), "UNR": ("sbuf", [128, 128], BF),
-    "ONE": ("sbuf", [128, 128], BF), "BK1": ("sbuf", [128, 128], F16), "THd": ("sbuf", [128, n], F16), "TH": ("sbuf", [128, n], FP),
-    "CA": ("sbuf", [128, 1024], BF), "CB": ("sbuf", [128, 1024], BF), "CD": ("sbuf", [128, 1024], BF),
-    "SA": ("sbuf", [128, 1024], F16), "SW": ("sbuf", [128, 1024], F16), "SE": ("sbuf", [128, 1024], F16),
-    "RSUM": ("sbuf", [128, 1], FP), "RI": ("sbuf", [128, 1], I32), "RA": ("sbuf", [128, 1], FP),
-    "THt": ("sbuf", [128, n], FP),
-    "ZX": ("sbuf", [128, 144], F16), "ZP": ("sbuf", [128, 144], F16),
-    "UU": ("sbuf", [128, NC * nb], I32), "u15": ("sbuf", [128, NC * nb], I32), "DU": ("sbuf", [128, NC * nb], FP),
-    "LS": ("sbuf", [128, NC * n], FP), "rep": ("sbuf", [128, NC * nb], BF), "ot": ("sbuf", [128, NC * nb], FP),
-    "of": ("sbuf", [128, NC * nb], FP), "oo": ("sbuf", [128, NC * nb], U16), "AV": ("sbuf", [128, NC * n], I32),
-    "P0a": ("psum", [128, n // 2, 8], FP), "P0b": ("psum", [128, n // 2, 8], FP),
-    "PNa": ("psum", [128, 4, n], FP), "PNb": ("psum", [128, 4, n], FP),
+    "X": ("sbuf", [128, 4096 + 256], BF), "XO": ("sbuf", [128, 4096 + 256], BF),
+    "RT2": ("sbuf", [128, 16384], I32), "rs2": ("dram", [8, 32, 1024], I32), "IOT": ("sbuf", [128, 4096], FP),
+    "WI": ("sbuf", [128, 256], I32), "wt0": ("sbuf", [128, 1], I32), "th0": ("sbuf", [128, 1], I32),
+    "PI": ("sbuf", [128, 8], I32), "FC": ("sbuf", [128, 16], FP), "GE": ("sbuf", [128, 32], FP),
+    "X144": ("sbuf", [128, 144], BF), "CW": ("sbuf", [128, 144], BF), "CU": ("sbuf", [128, 128], BF), "GW": ("sbuf", [128, 128], BF), "T3": ("sbuf", [128, 128], BF),
+    "K16": ("sbuf", [128, n], BF), "KB": ("sbuf", [128, n], BF), "C0": ("sbuf", [128, n], FP), "C1": ("sbuf", [128, n], FP), "NB": ("sbuf", [128, n], BF),
+    "E32": ("sbuf", [128, 8, 32], BF), "EQ0": ("sbuf", [128, 8, 32], BF), "EQ1": ("sbuf", [128, 8, 32], BF),
+    "R0": ("sbuf", [128, 16, 128], BF), "R1": ("sbuf", [128, 8, 128], BF), "SA": ("sbuf", [128, 8, 128], BF), "SW": ("sbuf", [128, 8, 128], BF), "SE": ("sbuf", [128, 8, 128], BF),
+    "IW": ("sbuf", [128, 16], FP), "II": ("sbuf", [128, 16], BF), "ONE": ("sbuf", [128, 128], BF), "J0": ("sbuf", [128, n], FP), "D1": ("sbuf", [128, n], FP),
+    "ZX": ("sbuf", [128, 144], BF), "ZD": ("sbuf", [128, 144], BF), "ZG": ("sbuf", [128, 144], BF),
+    "ID": ("sbuf", [128, 128], BF), "NID": ("sbuf", [128, 128], BF), "HID": ("sbuf", [128, 128], BF), "SH": ("sbuf", [128, 128], BF), "SR": ("sbuf", [128, 128], BF),
+    "UN": ("sbuf", [128, 128], BF), "BLK": ("sbuf", [128, 128], BF), "BH": ("sbuf", [128, 128], BF), "BL": ("sbuf", [128, 128], BF), "BK1": ("sbuf", [128, 128], BF),
+    "S0": ("sbuf", [128, 128], BF), "THd": ("sbuf", [128, n], F16), "THn": ("sbuf", [128, n], F16),
+    "XW": ("sbuf", [128, 4096], BF), "XR": ("sbuf", [128, 4096], BF), "AB": ("sbuf", [128, 256, 16], BF), "DD": ("sbuf", [128, 4096], BF),
+    "NT": ("sbuf", [128, 17 * 256], FP), "RD": ("sbuf", [128, 4096], FP),
+    "W16": ("sbuf", [128, 256], F16), "S1": ("sbuf", [128, 256], FP), "W0u": ("sbuf", [128, 16], U16), "X0": ("sbuf", [128, 256], BF),
+    "SU": ("sbuf", [128, 256], I32), "SK": ("sbuf", [128, 256], I32),
+    "U": ("sbuf", [128, 16], I32), "vv": ("sbuf", [128, 16], I32), "sq": ("sbuf", [128, 16], I32), "CC": ("sbuf", [128, 16], I32), "c16": ("sbuf", [128, 16], U16),
+    "Ro": ("sbuf", [128, 256], U16), "R16": ("sbuf", [128, 256], F16), "s10": ("sbuf", [128, 16], I32), "qi": ("sbuf", [128, 16], FP), "qo": ("sbuf", [128, 16], U16),
+    "Qo": ("sbuf", [128, 256], U16), "Qi": ("sbuf", [128, 256], I32), "pr": ("sbuf", [128, 256], I32), "ps": ("sbuf", [128, 256], I32),
+    "F16": ("sbuf", [128, 256], F16), "q1": ("sbuf", [128, 256], I32), "ee": ("sbuf", [128, 256], FP), "CQ": ("sbuf", [128, 256], F16),
+    "Zs": ("sbuf", [128, 256], BF), "LS": ("sbuf", [128, 256], FP), "no": ("sbuf", [128, 16], U16), "NF": ("sbuf", [128, 256], FP),
+    "u16": ("sbuf", [128, 16], U16), "u15": ("sbuf", [128, 16], I32), "oT": ("sbuf", [128, 16], FP),
+    "rep": ("sbuf", [128, 16], BF), "of": ("sbuf", [128, 16], FP), "oo": ("sbuf", [128, 16], U16), "AV": ("sbuf", [128, 256], I32),
+    "AC": ("sbuf", [128, 16], FP), "AS": ("sbuf", [128, 1], FP), "AI": ("sbuf", [128, 2], I32), "BA": ("sbuf", [128, 1], FP),
+    "W32": ("sbuf", [128, 256], FP), "sW0": ("dram", [16, 32, n], FP), "sW1": ("dram", [16, 32, n], FP),
+    "PC0": ("psum", [128, 512], FP), "PC1": ("psum", [128, 512], FP),
 }
-for _h in range(NC):
-    for _nm, _sh, _d in (("XW", [128, 16 * n], BF), ("XR", [128, 16 * n], BF), ("AB", [128, n, 16], BF), ("DD", [128, 16 * n], BF),
-                         ("NT", [128, 17 * n], FP), ("RD", [128, 16 * n], FP), ("W16", [128, n], F16),
-                         ("W0u", [128, nb], U16), ("x0", [128, n], BF), ("ui", [128, nb], I32), ("vv", [128, nb], I32), ("sq", [128, nb], I32), ("cc", [128, nb], I32),
-                         ("c16", [128, nb], U16), ("Ro", [128, n], U16), ("R16", [128, n], F16), ("SC", [128, n], I32), ("s10", [128, nb], I32),
-                         ("qi", [128, nb], I32), ("qo", [128, nb], U16), ("Qo", [128, n], U16), ("Qi", [128, n], I32),
-                         ("SN", [128, n], I32), ("un", [128, n], I32), ("pr", [128, n], I32), ("ps", [128, n], I32), ("fs", [128, n], I32),
-                         ("f12", [128, n], I32), ("F16", [128, n], F16), ("q1", [128, n], I32), ("ee", [128, n], FP), ("CQ", [128, n], F16),
-                         ("ff", [128, n], FP), ("no", [128, nb], U16), ("NF", [128, n], FP), ("XO", [128, 4096 + n], BF)):
-        SCRATCH[_nm + str(_h)] = ("sbuf", _sh, _d)
-    SCRATCH["PD%d" % _h] = ("psum", [128, 512], FP)
-    SCRATCH["PU%d" % _h] = ("psum", [128, 512], FP)
+POOL = ["B%d" % _b for _b in range(6)]
+for _b in POOL:
+    SCRATCH[_b] = ("psum", [128, 512], FP)
 for _t in range(VIS):
-    SCRATCH["Wo%d" % _t] = ("sbuf", [128, 256], U16)
+    SCRATCH["WF%d" % _t] = ("sbuf", [128, 256], U16)
     if _t:
         SCRATCH["ST%d" % _t] = ("sbuf", [128, 256], U16)
 
-AL = {"sq": "ui", "qi": "ui", "s10": "vv", "SN": "pr", "fs": "pr", "f12": "ps", "ff": "ee", "no": "c16", "W0u": "qo", "NF": "ee", "R16": "CQ"}
-for _k in AL:
-    for _h in range(NC):
-        SCRATCH.pop(_k + str(_h))
-
-NDMA = 44
+NDMA = 32
 SEMAPHORES = ["qV", "qA", "qT", "qG", "ls"] + ["d%d" % i for i in range(NDMA)] + ["ar%d_%d" % (t, h) for t in range(1, VIS) for h in range(NC)]
 
-CY = 0.00083
-PEC = 0.00042
+CY = 0.00083 * 1.12
+PEC = 0.00042 * 1.12
 GA = 1.5
-HOP = 0.10
+SCA = 3.0
+HOP = 0.12
 
 
 def cv(cyc):
@@ -76,436 +65,470 @@ def ca(cyc):
     return 0.065 + max(64, cyc) * CY
 
 
-def build(g, core, rank, T, topo):
+def build(g, core, rank, T, topo, bank):
     ops = []
     A = AluOpType
     v, a, t = g.vector, g.scalar, g.tensor
+    cur = [0, "", 0]
 
-    def al(nm):
-        return AL[nm[:-1]] + nm[-1] if nm[:-1] in AL else nm
-
-    def add(alts, rd, wr, lat=0.0, tag=""):
-        ops.append({"alts": alts, "rd": [al(x) for x in rd], "wr": [al(x) for x in wr], "lat": lat, "tag": tag})
+    def add(alts, rd, wr, lat=0.0, tag="", take=None, give=None, pre=(), acc=False):
+        ops.append({"v": cur[2], "ch": cur[0], "ph": cur[1], "acc": acc, "alts": alts, "rd": list(rd), "wr": list(wr), "lat": lat, "tag": tag,
+                    "take": take, "give": give, "pre": list(pre)})
 
     def V(cyc, rd, wr, fn):
         add([("V", cv(cyc), fn)], rd, wr)
 
-    def AV(cyc, rd, wr, fv, fa):
-        add([("V", cv(cyc), fv), ("A", ca(cyc), fa)], rd, wr)
-
     def ACT(cyc, rd, wr, fn):
         add([("A", ca(cyc), fn)], rd, wr)
 
-    def PE(cols, rd, wr, calls):
+    def AV(cyc, rd, wr, fv, fa, half=False):
+        add([("V", cv(cyc / 2 if half else cyc), fv), ("A", ca(cyc), fa)], rd, wr)
+
+    def PE(cols, rd, wr, calls, **k):
         def fn():
             ins = None
-            for c in calls:
+            for c in (calls() if "take" in k else calls):
                 ins = t.matmul(*c)
             return ins
-        add([("T", cols * PEC + 0.05, fn)], rd, wr)
+        add([("T", cols * PEC + 0.05, fn)], rd, wr, **k)
 
-    def DMA(us, rd, wr, fn, q="S", tag=""):
-        add([(q, 0.08, fn)], rd, wr, lat=us, tag=tag)
+    def DMA(us, rd, wr, pairs, q="S"):
+        eng_ = g.sync if q == "S" else g.scalar
+        add([(q, 0.08 * len(pairs), lambda: [eng_.dma_start(o, i) for o, i in pairs])], rd, wr, lat=us)
 
-    def G(us, wr, fn, rd=()):
-        add([("G", us, fn)], list(rd), wr)
+    def G(cnt, wr, fn, rd=()):
+        add([("G", 0.15 + 2 * cnt * CY, fn)], list(rd), wr)
+
+    def gather(cnt, rd, wr, out, win):
+        AV(GA * cnt, rd, wr, lambda: v.tensor_copy(out, win), lambda: a.activation(out, win, AF.Identity))
+
+    def affine(cyc, rd, wr, out, src, mul, plus, half=False):
+        AV(cyc, rd, wr, lambda: v.tensor_scalar(out, src, mul, plus, A.mult, A.add), lambda: a.activation(out, src, AF.Identity, bias=plus, scale=mul), half)
+
+    nk = [0]
+
+    def pooled(cols, rd, calls, cyc, crd, wr, use):
+        nk[0] += 1
+        key = "k%d" % nk[0]
+        PE(cols, rd + crd, [key], lambda: calls(T[bank[key]]), take=key, pre=wr)
+        add([(q, cv(cyc) if q == "V" else ca(cyc), (lambda f=f: f(T[bank[key]]))) for q, f in use], [key] + crd, wr, give=key)
+
+    def plus(out, w, c):
+        return [("V", lambda P: v.tensor_scalar(out, P[:, 0:w], c, None, A.add)), ("A", lambda P: a.activation(out, P[:, 0:w], AF.Identity, bias=c))]
+
+    def most(out, w):
+        return [("V", lambda P: v.tensor_tensor_scan(out, T.C0[:, 0:w], P[:, 0:w], 0.0, A.min, A.max))]
+
+    def least(out, w):
+        return [("V", lambda P: v.tensor_tensor_scan(out, T.C1[:, 0:w], P[:, 0:w], 0.0, A.max, A.min))]
 
     fl = {"allow_small_or_imprecise_dtypes": True}
-    DMA(4.5, [], ["X"], lambda: g.sync.dma_start(T.X[:, 0:4096], T.x[:, :]))
-    DMA(2.0, [], ["WI"], lambda: g.scalar.dma_start(T.WI[:], T.wd[:, :]), "D")
-    DMA(2.0, [], ["wt0"], lambda: g.scalar.dma_start(T.wt0[:], T.wt[:, :]), "D")
-    DMA(3.0, [], ["RTa"], lambda: g.sync.dma_start(T.RT2[:, ROT:1024], T.rt[:, 0:1024 - ROT]))
-    DMA(3.0, [], ["RTb"], lambda: g.sync.dma_start(T.RT2[:, 0:ROT], T.rt[:, 1024 - ROT:1024]))
-    DMA(2.0, [], ["th0"], lambda: g.sync.dma_start(T.th0[:], T.th[:, :]))
-    for i, (lo, hi, s0, s1) in enumerate(((ROT, 1024, 0, 1024 - ROT), (0, ROT, 1024 - ROT, 1024))):
-        for rr in (0, 16):
-            DMA(4.0, ["WI"], ["rs2_%d_%d" % (i, rr)],
-                lambda lo=lo, hi=hi, s0=s0, s1=s1, rr=rr: g.sync.dma_start(T.rs2[:, rr:rr + 16, lo:hi], T.rt[:, s0:s1]))
-    for s in range(1, 16):
-        DMA(4.0 + 1.3 * s, ["rs2_%d_%d" % (i, rr) for i in (0, 1) for rr in (0, 16)], ["RS%d" % s],
-            lambda s=s: g.sync.dma_start(T.RT2[:, 1024 * s:1024 * (s + 1)], T.rs2[:, s:s + 16, :]))
-    RTALL = ["RTa", "RTb"] + ["RS%d" % s for s in range(1, 16)]
+    DMA(2.0, [], ["WI"], [(T.WI[:], T.wd[:, :])], "D")
+    DMA(5.5, [], ["X"], [(T.X[:, 0:4096], T.x[:, :])])
+    DMA(2.0, [], ["wt0"], [(T.wt0[:], T.wt[:, :])], "D")
+    DMA(7.5, [], ["RT"], [(T.RT2[:, ROT:1024], T.rt[:, 0:1024 - ROT]), (T.RT2[:, 0:ROT], T.rt[:, 1024 - ROT:1024])])
+    DMA(2.0, [], ["th0"], [(T.th0[:], T.th[:, :])], "D")
+    DMA(4.0, ["RT"], ["rs2"], [(T.rs2[:, rr:rr + 16, :], T.RT2[:, 0:1024]) for rr in (0, 16)])
+    DMA(24.0, ["rs2"], ["RS"], [(T.RT2[k::16, 1024:16384], T.rs2[:, k + 1:k + 16, :]) for k in range(16)])
 
-    G(0.2, ["PM"], lambda: g.iota(T.PM[:], [[16, 2]], 0, 1))
-    G(0.4, ["X144"], lambda: g.iota(T.X144[:], [[1, 144]], 0, 0, **fl))
-    G(0.4, ["G128"], lambda: g.iota(T.G128[:], [[16, 8], [0, 16]], 0, 0, **fl))
-    G(0.5, ["U256"], lambda: g.iota(T.U256[:], [[0, 2], [1, 128]], 0, 0, **fl))
-    G(0.4, ["K16"], lambda: g.iota(T.K16[:], [[0, nb], [1, 16]], 0, 0, **fl))
-    G(0.2, ["IW"], lambda: g.iota(T.IW[:], [[16, NC * nb]], 0, 0))
-    G(0.6, ["E32"], lambda: g.iota(T.E32[:], [[16, 8], [0, 2], [1, 16]], 0, 0, **fl))
-    G(0.4, ["J0"], lambda: g.iota(T.J0[:], [[16, nb], [0, 16]], 0, 0, **fl))
-    for nm, base, pat in (("CA", 15, [[0, 8], [16, 8], [-1, 16]]), ("CB", 14, [[-2, 8], [16, 8], [1, 16]]), ("CD", 0, [[0, 8], [16, 8], [1, 16]])):
-        G(1.9, [nm], lambda nm=nm, base=base, pat=pat: g.iota(T[nm][:], pat, base, 0, **fl))
-    for nm, base, pat in (("CA", 0, [[1, 8], [0, 8], [-1, 16]]), ("CB", -1, [[-1, 8], [0, 8], [1, 16]]),
-                          ("CB", 1, [[2, 8], [0, 8], [-1, 16]]), ("CD", 0, [[-2, 8], [0, 8], [1, 16]])):
-        G(1.9, [nm], lambda nm=nm, base=base, pat=pat: g.affine_select(T[nm][:], T[nm][:], pat, A.is_ge, -1.0, base, 0), [nm])
-    V(2, [], ["PM"], lambda: v.tensor_scalar(T.PM[:], T.PM[:], 127, None, A.bitwise_and))
-    V(2, ["PM"], ["PQ"], lambda: v.tensor_scalar(T.PQ[:], T.PM[:], 112, None, A.bitwise_and))
-    V(2, ["PM"], ["P5"], lambda: v.tensor_scalar(T.P5[:], T.PM[:], 15, None, A.bitwise_and))
-    V(2, ["PM"], ["FC0"], lambda: v.tensor_copy(T.FC[:, 0:2], T.PM[:]))
-    V(2, ["PQ"], ["FC2"], lambda: v.tensor_scalar(T.FC[:, 2:4], T.PQ[:], 15.0, None, A.add))
-    V(2, ["PQ"], ["FC4"], lambda: v.tensor_copy(T.FC[:, 4:6], T.PQ[:]))
-    V(2, ["P5"], ["FC6"], lambda: v.tensor_copy(T.FC[:, 6:8], T.P5[:]))
-    V(2, ["wt0"], ["WCa"], lambda: v.tensor_scalar(T.WC[:, 0:1], T.wt0[:], 0xFC0, None, A.bitwise_and))
-    V(2, ["wt0"], ["WCb"], lambda: v.tensor_scalar(T.WC[:, 1:2], T.wt0[:], 63, None, A.bitwise_and))
-    V(2, ["WCa", "WCb"], ["FC8"], lambda: v.tensor_copy(T.FC[:, 8:10], T.WC[:]))
-    V(2, ["th0"], ["FC10"], lambda: v.tensor_scalar(T.FC[:, 10:11], T.th0[:], -2048.0, None, A.add))
+    def IO(nm, pat, base, cnt, sl=None, cm=0):
+        G(cnt, [nm if sl is None else nm + str(sl[0])], lambda: g.iota(T[nm][:] if sl is None else T[nm][:, sl[0]:sl[1]], pat, base, cm, **fl))
+    G(2, ["P"], lambda: g.iota(T.PI[:, 0:2], [[16, 2]], 0, 1))
+    IO("FC", [[0, 1]], 0, 1, (0, 1), 1)
+    IO("X144", [[1, 144]], 0, 144)
+    IO("GW", [[16, 8], [0, 16]], 0, 128)
+    IO("K16", [[0, nb], [1, 16]], 0, n)
+    IO("CW", [[1, 16]], 112, 16, (0, 16))
+    IO("CW", [[1, 128]], 0, 128, (16, 144))
+    CWn = ["CW0", "CW16"]
+    IO("C0", [[0, n]], 2 ** 24 - 1, n)
+    G(n, ["C0"], lambda: g.affine_select(T.C0[:], T.C0[:], [[0, nb], [1, 16]], A.not_equal, -float(2 ** 30), 0, 0))
+    IO("E32", [[16, 8], [0, 2], [1, 16]], 0, 256)
+    IO("C1", [[0, n]], 0, n)
+    G(n, ["C1"], lambda: g.affine_select(T.C1[:], T.C1[:], [[0, nb], [1, 16]], A.not_equal, float(2 ** 30), 0, 0))
+    IO("IW", [[256, 16]], -4096, 16)
+    IO("II", [[16, 16]], 0, 16)
+    IO("T3", [[-1, 16]], 127, 16, (0, 16))
+    IO("T3", [[16, 7], [-1, 16]], 15, 112, (16, 128))
+    IO("CU", [[1, 112]], 16, 112, (0, 112))
+    IO("CU", [[1, 16]], 0, 16, (112, 128))
+    IO("J0", [[-16, nb], [0, 16]], -64 * n, n)
+    for i in range(4):
+        IO("IOT", [[1, 1024]], 1024 * i, 1024, (1024 * i, 1024 * i + 1024))
+    IOTn = ["IOT%d" % (1024 * i) for i in range(4)]
 
-    def col(i):
-        return T.FC[:, i:i + 1]
+    cn = {nm: i for i, nm in enumerate(("0", "a", "g", "gs", "ps", "g15", "gs15", "a0", "wH", "wL", "a16", "th"))}
 
-    def EQ(out, src, c, mul, cyc, rd, f=None):
-        def fn():
-            if mul is None:
-                return v.tensor_scalar(T[out][:], src(), col(c), None, A.is_equal)
-            return v.tensor_scalar(T[out][:], src(), col(c), mul if f is None else col(f), A.is_equal, A.mult)
-        V(cyc, rd, [out], fn)
-    V(256, ["WI"], ["Wo0_%d" % h for h in range(NC)], lambda: v.tensor_copy(T.Wo0[:], T.WI[:]))
-    V(2, ["PM"], ["FC11"], lambda: v.tensor_scalar(T.FC[:, 11:12], T.PM[:, 0:1], 15.0, None, A.add))
-    V(2, ["FC6"], ["FC12"], lambda: v.tensor_scalar(T.FC[:, 12:13], T.FC[:, 6:7], 0.0, None, A.is_equal))
-    EQ("ZX", lambda: T.X144[:], 11, 1.0, 72, ["X144", "FC11", "FC12"], 12)
-    EQ("ZH", lambda: T.X144[:], 2, 1.0, 72, ["X144", "FC2", "FC8"], 8)
-    EQ("ZL", lambda: T.X144[:], 2, 1.0, 72, ["X144", "FC2", "FC8"], 9)
-    EQ("ZD", lambda: T.X144[:], 2, 16384.0, 72, ["X144", "FC2"])
-    EQ("ID", lambda: T.U256[:, 0:128], 0, None, 64, ["U256", "FC0"])
-    EQ("NID", lambda: T.U256[:, 0:128], 0, -1.0, 64, ["U256", "FC0"])
-    V(64, ["K16"], ["KB"], lambda: v.tensor_scalar(T.KB[:], T.K16[:], 1024.0, None, A.mult))
-    V(n, ["K16"], ["C0"], lambda: v.tensor_scalar(T.C0[:], T.K16[:], 0.0, float(2 ** 30), A.is_equal, A.mult))
-    V(nb, ["FC6"], ["IW"], lambda: v.tensor_scalar(T.IW[:], T.IW[:], col(6), None, A.add))
-    EQ("BH", lambda: T.G128[:], 4, 1.0, 64, ["G128", "FC4", "FC8"], 8)
-    EQ("BL", lambda: T.G128[:], 4, 1.0, 64, ["G128", "FC4", "FC8"], 9)
-    EQ("EQ0", lambda: T.E32[:], 0, None, 128, ["E32", "FC0"])
+    def col(nm):
+        return T.FC[:, cn[nm]:cn[nm] + 1]
+
+    def COL(nm, src, rd, s1, s2, o0, o1=None):
+        V(1, rd, ["FC" + nm], lambda: v.tensor_scalar(col(nm), src, s1, s2, o0, o1) if o1 else v.tensor_scalar(col(nm), src, s1, None, o0))
+
+    def ACOL(nm, src, mul, pl):
+        affine(1, ["FC" + src], ["FC" + nm], col(nm), col(src), mul, pl)
+
+    def EQ(out, src, rd, c, mul, cyc, sl=None, op=A.is_equal):
+        V(cyc, rd + ["FC" + c] + (["FC" + mul] if isinstance(mul, str) else []), [out],
+          lambda: v.tensor_scalar(T[out][:], T[src][:] if sl is None else T[src][:, sl[0]:sl[1]], col(c), col(mul) if isinstance(mul, str) else mul, op, A.mult))
+
+    def SCALE(out, src, mul, cyc):
+        affine(cyc, [src] + (["FC" + mul] if isinstance(mul, str) else []), [out], T[out][:], T[src][:, 0:cyc], col(mul) if isinstance(mul, str) else mul, 0.0, True)
+    pa = T.PI[:, 2:3]
+    V(1, ["P"], ["Pa"], lambda: v.tensor_scalar(pa, T.PI[:, 0:1], 15, None, A.bitwise_and))
+    V(1, ["P"], ["Pg"], lambda: v.tensor_scalar(T.PI[:, 3:5], T.PI[:, 0:2], 112, None, A.bitwise_and))
+    V(1, ["Pa", "Pg"], ["FCa", "FCg", "FCgs"], lambda: v.tensor_copy(T.FC[:, 1:4], T.PI[:, 2:5]))
+    V(256, ["WI"], ["WF0_%d" % h for h in range(NC)], lambda: v.tensor_copy(T.WF0[:], T.WI[:]))
+    COL("a0", pa, ["Pa"], 0.0, None, A.is_equal)
+    ACOL("g15", "g", 1.0, 15.0)
+    EQ("BLK", "GW", ["GW"], "g", 1.0, 64)
+    if PAR["w0"] == "m":
+        EQ("ZX", "X144", ["X144"], "g15", "a0", 72)
+    else:
+        SCALE("S0", "BLK", "a0", 128)
+    EQ("ID", "CW", CWn, "0", 1.0, 64, (16, 144))
+    EQ("NB", "K16", ["K16"], "a", -float(2 ** 24), 64, None, A.not_equal)
+    V(1, ["wt0"], ["Ph"], lambda: v.tensor_scalar(T.PI[:, 5:6], T.wt0[:], 0xFC0, None, A.bitwise_and))
+    V(1, ["wt0"], ["Pl"], lambda: v.tensor_scalar(T.PI[:, 6:7], T.wt0[:], 63, None, A.bitwise_and))
+    V(1, ["Ph", "Pl"], ["FCwH", "FCwL"], lambda: v.tensor_copy(T.FC[:, cn["wH"]:cn["wH"] + 2], T.PI[:, 5:7]))
+    SCALE("BH", "BLK", "wH", 128)
+    SCALE("BL", "BLK", "wL", 128)
+    SCALE("NID", "ID", -1.0, 128)
+    EQ("ZD", "X144", ["X144"], "g15", 16384.0, 72)
+    SCALE("KB", "K16", 1024.0, 128)
+    EQ("EQ0", "E32", ["E32"], "0", 1.0, 128)
     for r in range(16):
-        V(64, ["EQ0"], ["R0_%d" % r], lambda r=r: v.tensor_copy(T.R0[:, r, :], T.EQ0[:, :, r:r + 16]))
-    EQ("EQ1", lambda: T.E32[:], 1, None, 128, ["E32", "FC0"])
-    for r in range(1, 9):
-        V(64, ["EQ1"], ["R1_%d" % r], lambda r=r: v.tensor_copy(T.R1[:, r - 1, :], T.EQ1[:, :, r:r + 16]))
-    EQ("ZG", lambda: T.X144[:], 3, None, 72, ["X144", "FC2"])
-    EQ("BK1", lambda: T.G128[:], 5, None, 64, ["G128", "FC4"])
-    EQ("THd", lambda: T.K16[:], 6, 1.0, 64, ["K16", "FC6", "FC10"], 10)
-    PE(n, ["BK1", "THd"], ["PU0"], [(T.PU0[:, 0:n], T.BK1[:], T.THd[:], True, True)])
-    V(n, [], ["TH", "PU0"], lambda: v.tensor_scalar(T.TH[:], T.PU0[:, 0:n], 2048.0, None, A.add))
-    EQ("HID", lambda: T.U256[:, 0:128], 0, 0.5, 64, ["U256", "FC0"])
-    EQ("UNR", lambda: T.U256[:, 16:144], 0, None, 64, ["U256", "FC0"])
+        affine(128, ["EQ0"], ["R0_%d" % r], T.R0[:, r, :], T.EQ0[:, :, r:r + 16], 1.0, 0.0, True)
+    affine(16, ["FCa"], ["II"], T.II[:], T.II[:], 1.0, col("a"))
+    affine(1, ["FCa", "FCgs"], ["FCps"], col("ps"), col("gs"), 1.0, col("a"))
+    ACOL("gs15", "gs", 1.0, 15.0)
+    EQ("ZG", "X144", ["X144"], "gs15", 1.0, 72)
+    COL("th", T.th0[:], ["th0"], -1.0, 2048.0, A.mult, A.add)
+    EQ("THd", "K16", ["K16"], "a", "th", 64)
+    EQ("BK1", "GW", ["GW"], "gs", 1.0, 64)
+    pooled(n, ["THd", "BK1"], lambda P: [(P[:, 0:n], T.BK1[:], T.THd[:], True, True)], n, [], ["THn"], plus(T.THn[:], n, 0.0)[:1])
+    SCALE("HID", "ID", 0.5, 128)
     V(64, [], ["ONE"], lambda: v.memset(T.ONE[:], 1.0))
-    V(n, ["K16"], ["TM"], lambda: v.tensor_scalar(T.TM[:], T.K16[:], 15.0, None, A.is_equal))
-    V(n, ["FC6"], ["J0"], lambda: v.tensor_scalar(T.J0[:], T.J0[:], col(6), 1.0 / (16 * n), A.add, A.mult))
-    V(n, [], ["J0"], lambda: v.tensor_scalar(T.J0[:], T.J0[:], -8.0, None, A.add))
-    V(2 * n, ["J0", "TM"], ["D1"], lambda: v.tensor_tensor(T.D1[:], T.J0[:], T.TM[:], A.mult))
-    V(n, [], ["D1"], lambda: v.tensor_scalar(T.D1[:], T.D1[:], 0.0625, None, A.add))
-    V(nb, ["IW"], ["ALT"], lambda: v.tensor_scalar(T.ALT[:], T.IW[:], 4096.0, None, A.add))
-    V(nb, ["IW"], ["IDU"], lambda: v.tensor_scalar(T.IDU[:], T.IW[:], 15.0, -4096.0, A.mult, A.add))
-    EQ("SA", lambda: T.CA[:], 1, None, 512, ["CA", "FC0"])
-    EQ("SW", lambda: T.CB[:], 1, None, 512, ["CB", "FC0"])
-    EQ("SE", lambda: T.CD[:], 1, None, 512, ["CD", "FC0"])
+    ACOL("a16", "a", 16.0, 0.0)
+    affine(16, ["FCa16"], ["IW"], T.IW[:], T.IW[:], 1.0, col("a16"))
+    V(64, [], ["D1"], lambda: v.memset(T.D1[:], 0.125))
+    V(nb, ["J0", "FCa"], ["J0"], lambda: v.tensor_scalar(T.J0[:, 15::16], T.J0[:, 15::16], col("a"), 1.0 / (8 * n), A.subtract, A.mult))
+    affine(nb, ["J0"], ["D1"], T.D1[:, 15::16], T.J0[:, 15::16], 1.0, 0.125)
+    EQ("UN", "CU", ["CU0", "CU112"], "0", -8192.0, 64)
+    EQ("SH", "CW", CWn, "0", 1.0, 64, (0, 128))
+    EQ("SR", "T3", ["T30", "T316"], "0", 1.0, 64)
+    EQ("EQ1", "E32", ["E32"], "ps", 1.0, 128)
+    V(32, ["X144", "FCa"], ["GE"], lambda: v.tensor_scalar(T.GE[:], T.X144[:, 0:32], col("a"), None, A.is_le))
+    ge = lambda k: T.GE[:, k:k + 1]
+    for j in range(8):
+        affine(128, ["SH", "GE"], ["SE%d" % j], T.SE[:, j, :], T.SH[:], ge(2 * j), 0.0, True)
+        affine(128, ["SR", "GE"], ["SA%d" % (j + 1)], T.SA[:, j, :], T.SR[:], ge(15 - j), 0.0, True)
+        affine(128, ["EQ1", "GE"], ["SW%d" % (j + 1)], T.SW[:, j, :], T.EQ1[:, :, 14 - 2 * j:30 - 2 * j], ge(15 - j), 0.0, True)
+        if len(PAR["dt"]) < NC:
+            affine(128, ["EQ1"], ["R1_%d" % (j + 1)], T.R1[:, j, :], T.EQ1[:, :, j + 1:j + 17], 1.0, 0.0, True)
 
-    X = lambda: T.X[:, 0:4096]
-    H2 = n // 2
     dst = T.cores[(rank + ST) % len(T.cores)]
     rid, pid, _se = topo.addr(dst)
     eng = topo.engines(core, dst)[:8]
     msk = sum(1 << e for e in eng)
-    pn = [0]
-    P0 = ["P0a", "P0b"]
-    PN = ["PNa", "PNb"]
+    hs = list(range(NC))
+    XV = T.X[:, 0:4096]
+
+    def pcs(nm, h):
+        return ["%s%d_%d" % (nm, h, w) for w in range(NP)]
+
+    def two(nm, pn):
+        return [nm + "a" + pn, nm + "b" + pn]
+
+    def values(buf, lst, lstn, w0, pn, sp):
+        for i in range(sp):
+            lo, hi = w0 + i * H2 // sp, w0 + (i + 1) * H2 // sp
+            gather(16 * (hi - lo), lstn + ["X"], two(buf, pn)[i::sp], T[buf][:, 16 * lo:16 * hi], XV.indirect(T[lst][:, lo:hi]))
+
+    def diffs(src, srcn, sub, subn, w0, nm):
+        for o in range(2):
+            def calls(P, o=o):
+                c = []
+                for kk in range(8):
+                    c.append((P[:, kk::8], T.ID[:], src(8 * o + kk), True, False))
+                    c.append((P[:, kk::8], T.NID[:], sub(8 * o + kk), False, True))
+                return c
+            pooled(16 * H2, srcn + subn + ["ID", "NID"], calls, 8 * H2, [], ["%s_%d" % (nm, o)],
+                   [("A", lambda P, o=o: a.activation(T.AB[:, w0:w0 + H2, 8 * o:8 * o + 8], P[:], AF.Abs))])
+
+    def views(hh):
+        lo, hi = hh[0], hh[-1] + 1
+        cur[0] = lo
+        return (lambda nm: T[nm][:, lo * n:hi * n]), (lambda nm: T[nm][:, lo * nb:hi * nb]), (lambda *nms: [x + str(h) for x in nms for h in hh])
+
+    def table(h, js, rd, terms):
+        def calls(P):
+            return [(P[:, i * n:(i + 1) * n], m, x_, z == 0, z == len(terms(j)) - 1) for i, j in enumerate(js) for z, (m, x_) in enumerate(terms(j))]
+        k = len(js)
+        pooled(n * sum(len(terms(j)) for j in js), rd, calls, k * n, [], ["NT%d_%d" % (h, js[0])],
+               plus(T.NT[:, (17 * h + js[0]) * n:(17 * h + js[0] + k) * n], k * n, 2048.0))
+
+    def head(vis, h):
+        N_, Wd, x = views([h])
+        c0, c1 = h * n, (h + 1) * n
+        PC, pc = T["PC%d" % h], "PC%d" % h
+        wf, wfn = "WF%d" % vis, "WF%d_%d" % (vis, h)
+        V(n / 2, [wfn], x("W16"), lambda: v.tensor_scalar(N_("W16"), N_(wf), -2048.0, None, A.add))
+        if PAR["w0"] == "m":
+            pooled(64 * 16, x("W16") + ["ZX"], lambda P: [(P[:, 0:nb], T.ZX[:, 15 - m:143 - m], T.W16[:, c0 + m:c1:16], m == 0, m == 15) for m in range(16)],
+                   nb, [], x("W0u"), plus(Wd("W0u"), nb, 2048.0)[:1])
+        else:
+            pooled(2 * n, x("W16") + ["ID", "NB", "S0"], lambda P: [(P[:, 0:n], T.ID[:], T.NB[:], True, False), (P[:, 0:n], T.S0[:], N_("W16"), False, True)],
+                   n, ["C0"], x("S1"), most(N_("S1"), n))
+            V(nb, x("S1"), x("W0u"), lambda: v.tensor_scalar(Wd("W0u"), T.S1[:, c0 + 15:c1:16], 2048.0, None, A.add))
+        gather(n, x("W0u") + ["X"], x("X0"), N_("X0"), XV.indirect(Wd("W0u")))
+        pooled(3 * n, x("X0") + ["BH", "BL", "ID", "NB"],
+               lambda P: [(P[:, 0:n], T.ID[:], T.NB[:], True, False), (P[:, 0:n], T.BH[:], N_("X0"), False, False), (P[:, 0:n], T.BL[:], N_("X0"), False, True)],
+               n, ["C0"], x("SU"), most(N_("SU"), n))
+        V(nb, x("SU"), x("U"), lambda: v.tensor_scalar(Wd("U"), T.SU[:, c0 + 15:c1:16], 4095, None, A.bitwise_and))
+        V(nb, x("U"), x("vv"), lambda: v.tensor_scalar(Wd("vv"), Wd("U"), 592.0, None, A.add))
+        V(nb, x("vv"), x("sq"), lambda: v.tensor_tensor(Wd("sq"), Wd("vv"), Wd("vv"), A.mult))
+        V(nb, x("sq"), x("CC"), lambda: v.tensor_scalar(Wd("CC"), Wd("sq"), 5, 1023, A.arith_shift_right, A.bitwise_and))
+        V(nb, x("CC"), x("c16"), lambda: v.tensor_copy(Wd("c16"), Wd("CC")))
+        V(GA * n, x("c16") + ["RT"], x("Ro"), lambda: v.tensor_copy(N_("Ro"), T.RT2[:, 0:1024].indirect(Wd("c16"))))
+        own = vis in PAR["rd"]
+        rdn = ["RT", "RS"]
+        if own:
+            V(n / 2, x("Ro"), x("R16"), lambda: v.tensor_scalar(N_("R16"), N_("Ro"), -2048.0, None, A.add))
+            rdn = ["RD%d_%d" % (h, r4) for r4 in range(4)]
+            for r4 in range(4):
+                pooled(4 * n, x("R16") + ["R0_%d" % r for r in range(4 * r4, 4 * r4 + 4)],
+                       lambda P, r4=r4: [(P[:, i * n:(i + 1) * n], T.R0[:, 4 * r4 + i, :], N_("R16"), True, True) for i in range(4)],
+                       4 * n, [], [rdn[r4]], plus(T.RD[:, (16 * h + 4 * r4) * n:(16 * h + 4 * r4 + 4) * n], 4 * n, 2048.0))
+        for w in range(NP):
+            w0 = c0 + w * H2
+            pn = "%d_%d" % (h, w)
+            values("XW", wf, [wfn], w0, pn, PAR["ws"][h * NP + w])
+            values("XR", "Ro", x("Ro"), w0, pn, PAR["xs"][h * NP + w])
+            diffs(lambda k, w0=w0: T.XR[:, 16 * w0 + k:16 * (w0 + H2):16], two("XR", pn), lambda k, w0=w0: T.X0[:, w0:w0 + H2], x("X0"), w0, "AB" + pn)
+            keys = lambda o_, w=w, w0=w0: ([(o_, T.ID[:], T.KB[:, 0:H2], True, False)] +
+                                           [(o_, T.ZD[:, 15 - m:143 - m], T.AB[:, w0 + m:w0 + H2:16, :], False, m == 15) for m in range(16)])
+            rd = ["AB%s_0" % pn, "AB%s_1" % pn, "ZD", "KB", "ID"]
+            if PAR["ps"][h]:
+                pooled(17 * H2, rd, lambda P, keys=keys: keys(P[:, 0:H2]), H2, ["C1"], ["SK" + pn], least(T.SK[:, w0:w0 + H2], H2))
+            else:
+                PE(17 * H2, rd, [pc], keys(PC[:, w * H2:(w + 1) * H2]))
+        if not PAR["ps"][h]:
+            V(n, ["C1"], [pc] + pcs("SK", h), lambda: v.tensor_tensor_scan(N_("SK"), T.C1[:], PC[:, 0:n], 0.0, A.max, A.min))
+        for ww in ([[w] for w in range(NP)] if PAR["ps"][h] else [list(range(NP))]):
+            lo, hi = c0 + ww[0] * H2, c0 + (ww[-1] + 1) * H2
+            y = lambda nm, ww=ww: ["%s%d_%d" % (nm, h, w) for w in ww]
+            b = lambda nm, lo=lo, hi=hi: T[nm][:, lo // 16:hi // 16]
+            sk = T.SK[:, lo + 15:hi:16]
+            if own:
+                V(nb, y("SK"), y("s10"), lambda b=b, sk=sk: v.tensor_scalar(b("s10"), sk, 0x3C00, 11 - n.bit_length(), A.bitwise_and, A.arith_shift_right))
+                V(nb, y("s10") + ["II"], y("qi"), lambda b=b, lo=lo, hi=hi: v.tensor_tensor(b("qi"), b("s10"), T.II[:, (lo - c0) // 16:(hi - c0) // 16], A.add))
+                win = T.RD[:, 16 * c0:16 * c1]
+            else:
+                V(nb, y("SK"), y("s10"), lambda b=b, sk=sk: v.tensor_scalar(b("s10"), sk, 0x3C00, None, A.bitwise_and))
+                V(nb, y("s10") + x("CC"), y("qi"), lambda b=b: v.tensor_tensor(b("qi"), b("s10"), b("CC"), A.add))
+                win = T.RT2[:]
+            V(nb, y("qi"), y("qo"), lambda b=b: v.tensor_copy(b("qo"), b("qi")))
+            V(GA * (hi - lo), y("qo") + rdn, y("Qo"), lambda b=b, lo=lo, hi=hi, win=win: v.tensor_copy(T.Qo[:, lo:hi], win.indirect(b("qo"))))
+        if h in PAR["dt"]:
+            D = T["sW%d" % h]
+            V(n, [wfn], x("W32"), lambda: v.tensor_copy(N_("W32"), N_(wf)))
+            DMA(3.0, x("W32"), x("sW"), [pr_ for par, lo in ((0, 8), (1, 0), (1, 16)) for pr_ in
+                                         ((D[2 + par::2, lo:lo + 16, :], T.W32[0:112, c0:c1]), (D[par, lo:lo + 16, :], T.W32[112:128, c0:c1]))])
+            DMA(4.0, x("sW"), ["NT%d_0" % h, "NT%d_4" % h], [(T.NT[k::8, 17 * c0:17 * c0 + 8 * n], D[:, 9 + k:17 + k, :]) for k in range(8)])
+        else:
+            for l4 in (0, 4):
+                table(h, range(l4, l4 + 4), x("W16") + ["R1_%d" % (l + 1) for l in range(l4, l4 + 4)], lambda l: [(T.R1[:, l, :], N_("W16"))])
+
+    def upart(vis, hh):
+        N_, Wd, x = views(hh)
+        V(1, x("U"), x("u16"), lambda: v.tensor_copy(Wd("u16"), Wd("U")))
+        V(1, x("U"), x("u15"), lambda: v.tensor_scalar(Wd("u15"), Wd("U"), 15, None, A.bitwise_and))
+        V(1, x("u15") + ["IW"], x("oT"), lambda: v.tensor_tensor(Wd("oT"), Wd("u15"), Wd("IW"), A.add))
+
+    def qpart(vis, h):
+        N_, Wd, x = views([h])
+        V(n, pcs("Qo", h), x("Qi"), lambda: v.tensor_copy(N_("Qi"), N_("Qo")))
+        V(GA * n, x("Qi", "u16") + IOTn, x("pr"), lambda: v.tensor_tensor(N_("pr"), T.IOT[:].indirect(Wd("u16")), N_("Qi"), A.mult))
+        V(n, x("pr"), x("ps"), lambda: v.tensor_scalar(N_("ps"), N_("pr"), 5, None, A.arith_shift_right))
+        V(2 * n, x("Qi", "ps"), x("pr"), lambda: v.tensor_tensor(N_("pr"), N_("ps"), N_("Qi"), A.add))
+        V(n, x("pr"), x("ps"), lambda: v.tensor_scalar(N_("ps"), N_("pr"), 4095, None, A.bitwise_and))
+        V(n, x("ps"), x("F16"), lambda: v.tensor_scalar(N_("F16"), N_("ps"), -2048.0, None, A.add))
+        V(n, x("Qi"), x("q1"), lambda: v.tensor_scalar(N_("q1"), N_("Qi"), 1, None, A.bitwise_and))
+        V(n, x("q1"), x("ee"), lambda: v.tensor_scalar(N_("ee"), N_("q1"), -2.0, -2047.0, A.mult, A.add))
+        V(2 * n, x("ee", "Qi"), x("CQ"), lambda: v.tensor_tensor(N_("CQ"), N_("ee"), N_("Qi"), A.add))
+
+        def terms(l):
+            j = 16 - l
+            return ([(T.SW[:, j - 1, :], N_("W16")), (T.SA[:, j - 1, :], N_("CQ"))] if j else []) + ([(T.SE[:, j, :], N_("F16"))] if j < 8 else [])
+        for ls in ((8, 9, 10, 11), (12, 13, 14), (15, 16)):
+            table(h, ls, x("W16", "CQ", "F16") + ["S%s%d" % (c, 16 - l) for l in ls for c in ("WA" if l < 16 else "") + ("E" if l > 8 else "")], terms)
+
+    def gaps(vis, h):
+        N_, Wd, x = views([h])
+        c0, c1 = h * n, (h + 1) * n
+        PC, pc = T["PC%d" % h], "PC%d" % h
+        PE(n, ["ID", "THn"], [pc], [(PC[:, 0:n], T.ID[:], T.THn[:], True, False)])
+        av = []
+        for w in range(NP):
+            w0 = h * n + w * H2
+            pn = "%d_%d" % (h, w)
+            way = PAR["way"][h * NP + w]
+            win = XV.indirect(T.Qo[:, w0:w0 + H2])
+            dd, ab = T.DD[:, 16 * w0:16 * (w0 + H2)], T.AB[:, w0:w0 + H2, :]
+            abn = ["AB%s_0" % pn, "AB%s_1" % pn]
+            at = lambda buf, k, w0=w0: T[buf][:, 16 * w0 + k:16 * (w0 + H2):16]
+            if way == "A":
+                ACT(GA * 16 * H2, ["Qo" + pn, "X"], ["DD" + pn], lambda dd=dd, win=win: a.activation(dd, win, AF.Identity))
+                diffs(lambda k, at=at: at("DD", k), ["DD" + pn], lambda k, at=at: at("XW", k), two("XW", pn), w0, "AB" + pn)
+            else:
+                V(GA * 16 * H2, ["Qo" + pn, "X"] + two("XW", pn), ["DD" + pn],
+                  lambda dd=dd, win=win, w0=w0: v.tensor_tensor(dd, win, T.XW[:, 16 * w0:16 * (w0 + H2)], A.subtract))
+                ACT(16 * H2, ["DD" + pn], abn, lambda dd=dd, ab=ab: a.activation(ab, dd, AF.Abs))
+            PE(16 * H2, abn + ["ZG"], [pc],
+               [(PC[:, w * H2:(w + 1) * H2], T.ZG[:, 15 - m:143 - m], T.AB[:, w0 + m:w0 + H2:16, :], False, m == 15 and w == NP - 1) for m in range(16)], acc=True)
+            av += [(w, at("DD", 15))] + ([(w, at("XW", 15))] if way != "A" else [])
+        pooled(n + H2 * len(av), x("X0") + pcs("DD", h) + [y for w in range(NP) for y in two("XW", "%d_%d" % (h, w))] + ["HID"],
+               lambda P: [(P[:, 0:n], T.HID[:], N_("X0"), True, False)] +
+                         [(P[:, w * H2:(w + 1) * H2], T.HID[:], r_, False, i == len(av) - 1) for i, (w, r_) in enumerate(av)],
+               n, [], x("AV"), plus(N_("AV"), n, -0.25)[:1])
+        ACT(n, ["BA"] if vis else [], [pc] + x("Zs"), lambda: a.activation(N_("Zs"), PC[:, 0:n], AF.Sign, bias=T.BA[:] if vis else -2048.5))
+        V(n, x("Zs") + ["D1"], x("LS"), lambda: v.tensor_tensor_scan(N_("LS"), N_("Zs"), T.D1[:], -8.0, A.max, A.add))
+        V(nb, x("LS"), x("no"), lambda: v.tensor_scalar(Wd("no"), T.LS[:, c0 + 15:c1:16], -8.0 * n, -40.0 * n, A.mult, A.add))
+        V(nb, x("LS"), x("rep"), lambda: v.tensor_scalar(Wd("rep"), T.LS[:, c0 + 15:c1:16], -5.9995, None, A.is_lt))
+        pooled(128, x("rep") + ["UN", "ID", "II"], lambda P: [(P[:, 0:nb], T.ID[:], Wd("II"), True, False), (P[:, 0:nb], T.UN[:], Wd("rep"), False, True)],
+               nb, x("oT"), x("of"), [("V", lambda P: v.tensor_tensor(Wd("of"), Wd("oT"), P[:, 0:nb], A.max))])
+        V(nb, x("of"), x("oo"), lambda: v.tensor_scalar(Wd("oo"), Wd("of"), 4096.0, None, A.add))
+
+    def tail(vis, h):
+        N_, Wd, x = views([h])
+        c0, c1 = h * n, (h + 1) * n
+        last = vis == VIS - 1
+        xn = "XO" if last and h == 0 else "X"
+        V(SCA * n, x("AV", "oo"), [xn], lambda: v.tensor_copy(T[xn][:].indirect(Wd("oo")), N_("AV")))
+        ntn = x("no") + ["NT%d_%d" % (h, j) for j in (0, 4, 8, 12, 15)]
+        win = T.NT[:, 17 * c0:17 * c1].indirect(Wd("no"))
+        if last:
+            DMA(3.0, [xn], x("yx"), [(T.yx[:, 16 * c0:16 * c1], T[xn][:, 16 * c0:16 * c1])])
+            gather(n, ntn, x("NF"), N_("NF"), win)
+            DMA(2.0, x("NF"), x("yw"), [(T.yw[0:112, c0:c1], T.NF[16:128, c0:c1]), (T.yw[112:128, c0:c1], T.NF[0:16, c0:c1])], "D")
+        else:
+            st, nx = "ST%d" % (vis + 1), "WF%d" % (vis + 1)
+            V(GA * n, ntn, ["%s_%d" % (st, h)], lambda: v.tensor_copy(N_(st), win))
+            tag = "ar%d_%d" % (vis + 1, h)
+            add([("R", 1.0, lambda: g.remote_dma(N_(nx), N_(st), T.sem[tag], T.sem.ls, pid, rid, msk))],
+                ["%s_%d" % (st, h)], ["%s_%d" % (nx, h)], lat=PAR["rl"], tag=tag)
 
     for vis in range(VIS):
-        last = vis == VIS - 1
-        for h in range(NC):
-            hs = str(h)
-            W = lambda h=h, vis=vis: T["Wo%d" % vis][:, h * n:(h + 1) * n]
-            for q in range(2):
-                AV(GA * 8 * n, ["Wo%d_%d" % (vis, h), "X"], ["XW%s_%d" % (hs, q)],
-                   lambda h=h, q=q, vis=vis, hs=hs: v.tensor_copy(T["XW" + hs][:, q * 8 * n:(q + 1) * 8 * n], X().indirect(T["Wo%d" % vis][:, h * n + q * H2:h * n + (q + 1) * H2])),
-                   lambda h=h, q=q, vis=vis, hs=hs: a.activation(T["XW" + hs][:, q * 8 * n:(q + 1) * 8 * n], X().indirect(T["Wo%d" % vis][:, h * n + q * H2:h * n + (q + 1) * H2]), AF.Identity))
-        for h in range(NC):
-            hs = str(h)
-            b = lambda nm, hs=hs: T[AL.get(nm, nm) + hs]
-            UU = lambda h=h: T.UU[:, h * nb:(h + 1) * nb]
-            uun = "UU" + hs
-            V(n * 0.5, ["Wo%d_%d" % (vis, h)], ["W16" + hs],
-              lambda b=b, h=h, vis=vis: v.tensor_scalar(b("W16")[:], T["Wo%d" % vis][:, h * n:(h + 1) * n], -2048.0, None, A.add))
-            PE(64 * 16, ["W16" + hs, "ZX"], ["PU" + hs],
-               [(b("PU")[:, 496:496 + nb], T.ZX[:, 15 - m:143 - m], b("W16")[:, m::16], m == 0, m == 15) for m in range(16)])
-            V(nb, [], ["PU" + hs, "W0u" + hs], lambda b=b: v.tensor_scalar(b("W0u")[:], b("PU")[:, 496:496 + nb], 2048.0, None, A.add))
-            AV(GA * n, ["W0u" + hs, "X"], ["x0" + hs], lambda b=b: v.tensor_copy(b("x0")[:], X().indirect(b("W0u")[:])),
-               lambda b=b: a.activation(b("x0")[:], X().indirect(b("W0u")[:]), AF.Identity))
-            calls = []
-            for m in range(16):
-                for z in ("ZH", "ZL"):
-                    calls.append((b("PU")[:, 0:nb], T[z][:, 15 - m:143 - m], b("x0")[:, m::16], m == 0 and z == "ZH", m == 15 and z == "ZL"))
-            PE(64 * 32, ["x0" + hs, "ZH", "ZL"], ["PU" + hs], calls)
-            V(nb, [], ["PU" + hs, "ui" + hs], lambda b=b: v.tensor_copy(b("ui")[:], b("PU")[:, 0:nb]))
-            V(nb, ["ui" + hs], [uun], lambda b=b, UU=UU: v.tensor_scalar(UU(), b("ui")[:], 4095, None, A.bitwise_and))
-            V(nb, [uun], ["vv" + hs], lambda b=b, UU=UU: v.tensor_scalar(b("vv")[:], UU(), 592.0, None, A.add))
-            V(nb, ["vv" + hs], ["sq" + hs], lambda b=b: v.tensor_tensor(b("sq")[:], b("vv")[:], b("vv")[:], A.mult))
-            V(nb, ["sq" + hs], ["cc" + hs], lambda b=b: v.tensor_scalar(b("cc")[:], b("sq")[:], 5, 1023, A.arith_shift_right, A.bitwise_and))
-            V(nb, ["cc" + hs], ["c16" + hs], lambda b=b: v.tensor_copy(b("c16")[:], b("cc")[:]))
-            V(GA * n, ["c16" + hs, "RTa", "RTb"], ["Ro" + hs], lambda b=b: v.tensor_copy(b("Ro")[:], T.RT2[:, 0:1024].indirect(b("c16")[:])))
-            PE(2 * n, ["x0" + hs, "BH", "BL"], ["PU" + hs], [(b("PU")[:, n:2 * n], T.BH[:], b("x0")[:], True, False),
-                                                           (b("PU")[:, n:2 * n], T.BL[:], b("x0")[:], False, True)])
-            V(n, [], ["PU" + hs, "SN" + hs], lambda b=b: v.tensor_copy(b("SN")[:], b("PU")[:, n:2 * n]))
-            V(n, ["SN" + hs], ["un" + hs], lambda b=b: v.tensor_scalar(b("un")[:], b("SN")[:], 4095, None, A.bitwise_and))
-        V(NC * nb, ["UU%d" % h for h in range(NC)], ["u15"], lambda: v.tensor_scalar(T.u15[:], T.UU[:], 15, None, A.bitwise_and))
-        if not last:
-            V(2 * NC * nb, ["u15", "IDU"], ["DU"], lambda: v.tensor_tensor(T.DU[:], T.u15[:], T.IDU[:], A.add))
-        else:
-            for h in range(NC):
-                V(2 * nb, ["u15", "IDU"], ["DU%d" % h, "DU"], lambda h=h: v.tensor_tensor(T.DU[:, h * nb:(h + 1) * nb], T.u15[:, h * nb:(h + 1) * nb], T.IDU[:, 0:nb], A.add))
-        for h in range(NC):
-            hs = str(h)
-            b = lambda nm, hs=hs: T[AL.get(nm, nm) + hs]
-            if vis == 0:
-                V(n * 0.5, ["Ro" + hs], ["R16" + hs], lambda b=b: v.tensor_scalar(b("R16")[:], b("Ro")[:], -2048.0, None, A.add))
-                for r4 in range(4):
-                    p = PN[pn[0] % 2]
-                    pn[0] += 1
-                    PE(4 * n, ["R16" + hs] + ["R0_%d" % r for r in range(4 * r4, 4 * r4 + 4)], [p],
-                       [(T[p][:, i, :], T.R0[:, 4 * r4 + i, :], b("R16")[:], True, True) for i in range(4)])
-                    AV(4 * n, [], [p, "RD%s_%d" % (hs, r4)],
-                       lambda b=b, p=p, r4=r4: v.tensor_scalar(b("RD")[:, 4 * n * r4:4 * n * (r4 + 1)], T[p][:], 2048.0, None, A.add),
-                       lambda b=b, p=p, r4=r4: a.activation(b("RD")[:, 4 * n * r4:4 * n * (r4 + 1)], T[p][:], AF.Identity, bias=2048.0))
-            for q in range(2):
-                AV(GA * 8 * n, ["Ro" + hs, "X"], ["XR%s_%d" % (hs, q)],
-                   lambda b=b, q=q: v.tensor_copy(b("XR")[:, q * 8 * n:(q + 1) * 8 * n], X().indirect(b("Ro")[:, q * H2:(q + 1) * H2])),
-                   lambda b=b, q=q: a.activation(b("XR")[:, q * 8 * n:(q + 1) * 8 * n], X().indirect(b("Ro")[:, q * H2:(q + 1) * H2]), AF.Identity))
-            for w in range(2):
-                w0, w1 = w * H2, (w + 1) * H2
-                for o in range(2):
-                    p = P0[o]
-                    calls = []
-                    for kk in range(8):
-                        calls.append((T[p][:, :, kk], T.ID[:], b("XR")[:, 16 * w0 + 8 * o + kk:16 * w1:16], True, False))
-                        calls.append((T[p][:, :, kk], T.NID[:], b("x0")[:, w0:w1], False, True))
-                    PE(8 * n, ["XR%s_%d" % (hs, w), "x0" + hs, "ID", "NID"], [p], calls)
-                    ACT(4 * n, [], [p, "AB%s_%d%d" % (hs, w, o)],
-                        lambda b=b, p=p, o=o, w0=w0, w1=w1: a.activation(b("AB")[:, w0:w1, 8 * o:8 * o + 8], T[p][:], AF.Abs))
-                calls = [(b("PD")[:, w0:w1], T.ID[:], T.KB[:, w0:w1], True, False)]
-                for m in range(16):
-                    calls.append((b("PD")[:, w0:w1], T.ZD[:, 15 - m:143 - m], b("AB")[:, w0 + m:w1:16, :], False, m == 15))
-                PE(17 * H2, ["AB%s_%d%d" % (hs, w, o) for o in range(2)] + ["ZD", "KB", "ID"], ["PD" + hs], calls)
-            V(n, ["C0"], ["PD" + hs, "SC" + hs], lambda b=b: v.tensor_tensor_scan(b("SC")[:], T.C0[:], b("PD")[:, 0:n], 0.0, A.max, A.min))
-            if vis == 0:
-                sh = 10 - (n.bit_length() - 1)
-                V(nb, ["SC" + hs], ["s10" + hs], lambda b=b: v.tensor_scalar(b("s10")[:], b("SC")[:, 15::16], 0x3C00, sh, A.bitwise_and, A.arith_shift_right))
-                V(2 * nb, ["s10" + hs, "IW"], ["qi" + hs], lambda b=b: v.tensor_tensor(b("qi")[:], b("s10")[:], T.IW[:, 0:nb], A.add))
-            else:
-                V(nb, ["SC" + hs], ["s10" + hs], lambda b=b: v.tensor_scalar(b("s10")[:], b("SC")[:, 15::16], 0x3C00, None, A.bitwise_and))
-                V(2 * nb, ["s10" + hs, "cc" + hs], ["qi" + hs], lambda b=b: v.tensor_tensor(b("qi")[:], b("s10")[:], b("cc")[:], A.add))
-            V(nb, ["qi" + hs], ["qo" + hs], lambda b=b: v.tensor_copy(b("qo")[:], b("qi")[:]))
-            if vis == 0:
-                V(GA * n, ["qo" + hs] + ["RD%s_%d" % (hs, r4) for r4 in range(4)], ["Qo" + hs], lambda b=b: v.tensor_copy(b("Qo")[:], b("RD")[:].indirect(b("qo")[:])))
-            else:
-                V(GA * n, ["qo" + hs] + RTALL, ["Qo" + hs], lambda b=b: v.tensor_copy(b("Qo")[:], T.RT2[:].indirect(b("qo")[:])))
-        for h in range(NC):
-            hs = str(h)
-            b = lambda nm, hs=hs: T[nm + hs]
-            for j4 in (9, 13):
-                p = PN[pn[0] % 2]
-                pn[0] += 1
-                PE(4 * n, ["W16" + hs] + ["R1_%d" % (17 - j) for j in range(j4, j4 + 4)], [p],
-                   [(T[p][:, i, :], T.R1[:, 16 - (j4 + i), :], b("W16")[:], True, True) for i in range(4)])
-                AV(4 * n, [], [p, "NT%s_%d" % (hs, j4)],
-                   lambda b=b, p=p, j4=j4: v.tensor_scalar(b("NT")[:, n * j4:n * (j4 + 4)], T[p][:], 2048.0, None, A.add),
-                   lambda b=b, p=p, j4=j4: a.activation(b("NT")[:, n * j4:n * (j4 + 4)], T[p][:], AF.Identity, bias=2048.0))
-        for h in range(NC):
-            hs = str(h)
-            b = lambda nm, hs=hs: T[AL.get(nm, nm) + hs]
-            for q in range(2):
-                w0, w1 = q * H2, (q + 1) * H2
-                if q < SPL:
-                    V(GA * 8 * n, ["Qo" + hs, "X", "XW%s_%d" % (hs, q)], ["DD%s_%d" % (hs, q)],
-                      lambda b=b, q=q: v.tensor_tensor(b("DD")[:, q * 8 * n:(q + 1) * 8 * n], X().indirect(b("Qo")[:, q * H2:(q + 1) * H2]), b("XW")[:, q * 8 * n:(q + 1) * 8 * n], A.subtract))
-                    ACT(8 * n, ["DD%s_%d" % (hs, q)], ["AB%s_%d0" % (hs, q), "AB%s_%d1" % (hs, q)],
-                        lambda b=b, q=q: a.activation(b("AB")[:, q * H2:(q + 1) * H2, :], b("DD")[:, q * 8 * n:(q + 1) * 8 * n], AF.Abs))
-                else:
-                    ACT(GA * 8 * n, ["Qo" + hs, "X"], ["DD%s_%d" % (hs, q)],
-                        lambda b=b, q=q: a.activation(b("DD")[:, q * 8 * n:(q + 1) * 8 * n], X().indirect(b("Qo")[:, q * H2:(q + 1) * H2]), AF.Identity))
-                    for o in range(2):
-                        p = P0[o]
-                        calls = []
-                        for kk in range(8):
-                            calls.append((T[p][:, :, kk], T.ID[:], b("DD")[:, 16 * w0 + 8 * o + kk:16 * w1:16], True, False))
-                            calls.append((T[p][:, :, kk], T.NID[:], b("XW")[:, 16 * w0 + 8 * o + kk:16 * w1:16], False, True))
-                        PE(8 * n, ["DD%s_%d" % (hs, q), "XW%s_%d" % (hs, q), "ID", "NID"], [p], calls)
-                        ACT(4 * n, [], [p, "AB%s_%d%d" % (hs, q, o)],
-                            lambda b=b, p=p, o=o, w0=w0, w1=w1: a.activation(b("AB")[:, w0:w1, 8 * o:8 * o + 8], T[p][:], AF.Abs))
-                calls = []
-                for m in range(16):
-                    calls.append((b("PD")[:, q * H2:(q + 1) * H2], T.ZG[:, 15 - m:143 - m], b("AB")[:, q * H2 + m:(q + 1) * H2:16, :], m == 0, m == 15))
-                PE(16 * H2, ["AB%s_%d%d" % (hs, q, i) for i in range(2)] + ["ZG"], ["PD" + hs], calls)
-            DDr = ["DD%s_0" % hs, "DD%s_1" % hs]
-            XWr = ["XW%s_0" % hs, "XW%s_1" % hs]
-            V(n, ["Qo" + hs], ["Qi" + hs], lambda b=b: v.tensor_copy(b("Qi")[:], b("Qo")[:]))
-            V(2 * n, ["Qi" + hs, "un" + hs], ["pr" + hs], lambda b=b: v.tensor_tensor(b("pr")[:], b("Qi")[:], b("un")[:], A.mult))
-            V(n, ["pr" + hs], ["ps" + hs], lambda b=b: v.tensor_scalar(b("ps")[:], b("pr")[:], 5, None, A.arith_shift_right))
-            V(2 * n, ["ps" + hs, "Qi" + hs], ["fs" + hs], lambda b=b: v.tensor_tensor(b("fs")[:], b("ps")[:], b("Qi")[:], A.add))
-            V(n, ["fs" + hs], ["f12" + hs], lambda b=b: v.tensor_scalar(b("f12")[:], b("fs")[:], 4095, None, A.bitwise_and))
-            V(n, ["f12" + hs], ["F16" + hs], lambda b=b: v.tensor_scalar(b("F16")[:], b("f12")[:], -2048.0, None, A.add))
-            V(n, ["Qi" + hs], ["q1" + hs], lambda b=b: v.tensor_scalar(b("q1")[:], b("Qi")[:], 1, None, A.bitwise_and))
-            V(n, ["q1" + hs], ["ee" + hs], lambda b=b: v.tensor_scalar(b("ee")[:], b("q1")[:], -2.0, -2047.0, A.mult, A.add))
-            V(2 * n, ["ee" + hs, "Qi" + hs], ["CQ" + hs], lambda b=b: v.tensor_tensor(b("CQ")[:], b("ee")[:], b("Qi")[:], A.add))
-            for js in ((0, 1, 2, 3), (4, 5, 6, 7), (8,)):
-                p = PN[pn[0] % 2]
-                pn[0] += 1
-                calls = []
-                for i, j in enumerate(js):
-                    lst = []
-                    if j > 0:
-                        lst.append((T.SW[:, 128 * (j - 1):128 * j], b("W16")[:]))
-                        lst.append((T.SA[:, 128 * (j - 1):128 * j], b("CQ")[:]))
-                    if j < 8:
-                        lst.append((T.SE[:, 128 * j:128 * (j + 1)], b("F16")[:]))
-                    for z, (l_, r_) in enumerate(lst):
-                        calls.append((T[p][:, i, :], l_, r_, z == 0, z == len(lst) - 1))
-                PE(len(calls) * n, ["W16" + hs, "CQ" + hs, "F16" + hs, "SA", "SW", "SE"], [p], calls)
-                k = len(js)
-                AV(k * n, [], [p, "NT%s_%d" % (hs, js[0])],
-                   lambda b=b, p=p, k=k, j=js[0]: v.tensor_scalar(b("NT")[:, n * j:n * (j + k)], T[p][:, 0:k, :], 2048.0, None, A.add),
-                   lambda b=b, p=p, k=k, j=js[0]: a.activation(b("NT")[:, n * j:n * (j + k)], T[p][:, 0:k, :], AF.Identity, bias=2048.0))
-            calls = []
-            for q in range(2):
-                o_ = b("PU")[:, 2 * n + q * H2:2 * n + (q + 1) * H2]
-                calls.append((o_, T.HID[:], b("DD")[:, 8 * n * q + 15:8 * n * (q + 1):16], True, False))
-                if q < SPL:
-                    calls.append((o_, T.HID[:], b("XW")[:, 8 * n * q + 15:8 * n * (q + 1):16], False, False))
-                calls.append((o_, T.HID[:], b("x0")[:, q * H2:(q + 1) * H2], False, True))
-            PE(3 * n, DDr + XWr + ["HID", "x0" + hs], ["PU" + hs], calls)
-            V(n, [], ["PU" + hs, "AV" + hs], lambda b=b, h=h: v.tensor_scalar(T.AV[:, h * n:(h + 1) * n], b("PU")[:, 2 * n:3 * n], -0.25, None, A.add))
-        thn = "TH" if vis == 0 else "THt"
-        for h in range(NC):
-            hs = str(h)
-            b = lambda nm, hs=hs: T[AL.get(nm, nm) + hs]
-            V(n, [thn], ["PD" + hs, "ff" + hs], lambda b=b, thn=thn: v.tensor_tensor(b("ff")[:], b("PD")[:, 0:n], T[thn][:], A.is_gt))
-            V(n, ["ff" + hs, "D1"], ["LS" + hs], lambda b=b, h=h: v.tensor_tensor_scan(T.LS[:, h * n:(h + 1) * n], b("ff")[:], T.D1[:], -8.0, A.max, A.add))
-            V(nb, ["LS" + hs], ["no" + hs], lambda b=b, h=h: v.tensor_scalar(b("no")[:], T.LS[:, h * n + 15:(h + 1) * n:16], 16.0 * n, 7.0 * 16 * n, A.mult, A.add))
-            NTr = ["NT%s_%d" % (hs, j) for j in (0, 4, 8, 9, 13)]
-            if last:
-                V(GA * n, ["no" + hs] + NTr, ["NF" + hs], lambda b=b: v.tensor_copy(b("NF")[:], b("NT")[:].indirect(b("no")[:])))
-                DMA(2.0, ["NF" + hs], ["yw%s_0" % hs], lambda b=b, h=h: g.sync.dma_start(T.yw[0:112, h * n:(h + 1) * n], b("NF")[16:128, :]))
-                DMA(2.0, ["NF" + hs], ["yw%s_1" % hs], lambda b=b, h=h: g.sync.dma_start(T.yw[112:128, h * n:(h + 1) * n], b("NF")[0:16, :]))
-            else:
-                st = "ST%d_%d" % (vis + 1, h)
-                V(GA * n, ["no" + hs] + NTr, [st], lambda b=b, h=h, vis=vis: v.tensor_copy(T["ST%d" % (vis + 1)][:, h * n:(h + 1) * n], b("NT")[:].indirect(b("no")[:])))
-                add([("R", 1.0, lambda h=h, vis=vis: g.remote_dma(T["Wo%d" % (vis + 1)][:, h * n:(h + 1) * n], T["ST%d" % (vis + 1)][:, h * n:(h + 1) * n], T.sem["ar%d_%d" % (vis + 1, h)],
-                                                                        T.sem.ls, pid, rid, msk))], [st], ["Wo%d_%d" % (vis + 1, h)], lat=3.0, tag="ar%d_%d" % (vis + 1, h))
-        for hh in ([(h,) for h in range(NC)] if last else [tuple(range(NC))]):
-            lo, hi = hh[0], hh[-1] + 1
-            rn = ["rep%d" % h for h in hh]
-            hx = str(hh[-1])
-            P = "PU" + hx
-            c0, c1 = lo * nb, hi * nb
-            at = 0 if last else c0
-            V(c1 - c0, ["LS%d" % h for h in hh], rn, lambda c0=c0, c1=c1: v.tensor_scalar(T.rep[:, c0:c1], T.LS[:, 16 * c0 + 15:16 * c1:16], -6.4375, None, A.is_lt))
-            PE(64, rn + ["UNR"], [P], [(T[P][:, 400:400 + c1 - c0], T.UNR[:], T.rep[:, c0:c1], True, True)])
-            V(c1 - c0, ["DU"] + (["DU%d" % h for h in hh] if last else []), [P, "ot" + hx], lambda c0=c0, c1=c1, P=P: v.tensor_tensor(T.ot[:, c0:c1], T[P][:, 400:400 + c1 - c0], T.DU[:, c0:c1], A.mult))
-            V(2 * (c1 - c0), ["ot" + hx, "ALT"], ["of" + hx], lambda c0=c0, c1=c1, at=at: v.tensor_tensor(T.of[:, c0:c1], T.ot[:, c0:c1], T.ALT[:, at:at + c1 - c0], A.add))
-            V(c1 - c0, ["of" + hx], ["oo" + hx], lambda c0=c0, c1=c1: v.tensor_copy(T.oo[:, c0:c1], T.of[:, c0:c1]))
-            if not last:
-                V(3 * n * NC, ["AV%d" % h for h in hh] + ["oo" + hx], ["X"], lambda: v.tensor_copy(T.X[:].indirect(T.oo[:]), T.AV[:]))
-        if last:
-            for h in range(NC):
-                hs = str(h)
-                b = lambda nm, hs=hs: T[nm + hs]
-                DMA(3.5, ["X"], ["XO" + hs], lambda b=b, h=h: g.sync.dma_start(b("XO")[:, 0:CWID], T.X[:, h * CWID:(h + 1) * CWID]))
-                V(3 * n, ["AV" + hs, "oo" + hs], ["XO" + hs], lambda b=b, h=h: v.tensor_copy(b("XO")[:].indirect(T.oo[:, h * nb:(h + 1) * nb]), T.AV[:, h * n:(h + 1) * n]))
-                DMA(3.0, ["XO" + hs], ["yx" + hs], lambda b=b, h=h: g.sync.dma_start(T.yx[:, h * CWID:(h + 1) * CWID], b("XO")[:, 0:CWID]))
-        else:
-            PE(64, ["rep%d" % h for h in range(NC)] + ["ONE"], ["PU0"], [(T.PU0[:, 432:432 + NC * nb], T.ONE[:], T.rep[:], True, True)])
-            V(nb, [], ["PU0", "RSUM"], lambda: v.tensor_reduce(T.RSUM[:], T.PU0[:, 432:432 + NC * nb], AxisListType.X, A.add))
-            V(1, ["RSUM"], ["RI"], lambda: v.tensor_copy(T.RI[:], T.RSUM[:]))
-            V(1, [], ["RI"], lambda: v.tensor_scalar(T.RI[:], T.RI[:], 31, None, A.bitwise_and))
-            V(1, ["RI"], ["RA"], lambda: v.tensor_scalar(T.RA[:], T.RI[:], 8.0, None, A.mult))
-            V(n, ["TH", "RA"], ["THt"], lambda: v.tensor_scalar(T.THt[:], T.TH[:], T.RA[:, 0:1], None, A.add))
+        cur[2] = vis
+        for h in hs:
+            head(vis, h)
+        for hh in ([hs] if "u" in PAR["sh"] else [[h] for h in hs]):
+            upart(vis, hh)
+        for h in hs:
+            qpart(vis, h)
+        if vis == VIS - 1:
+            DMA(3.0, ["X"], ["XO"], [(T.XO[:, 0:2048], T.X[:, 0:2048])])
+        cur[1] = "g"
+        for h in hs:
+            gaps(vis, h)
+        cur[1] = ""
+        for h in hs:
+            tail(vis, h)
+        if vis < VIS - 1:
+            cur[0] = 0
+            pooled(64, ["grep%d" % h for h in ()] + ["rep%d" % h for h in hs] + ["ONE"], lambda P: [(P[:, 0:16], T.ONE[:], T.rep[:], True, True)],
+                   40, [], ["AC", "AS"], [("A", lambda P: a.activation(T.AC[:], P[:, 0:16], AF.Identity, accum_out=T.AS[:]))])
+            V(1, ["AS"], ["AI"], lambda: v.tensor_copy(T.AI[:, 0:1], T.AS[:]))
+            V(1, ["AI"], ["AJ"], lambda: v.tensor_scalar(T.AI[:, 1:2], T.AI[:, 0:1], 31, None, A.bitwise_and))
+            V(1, ["AJ"], ["BA"], lambda: v.tensor_scalar(T.BA[:], T.AI[:, 1:2], -8.0, -2048.5, A.mult, A.add))
     return ops, len(eng)
-
-
-SPL = 1
-LOOK = 0.1
-VBIAS = 1.0
-EN = {"XR1_1": "V", "XR0_0": "V", "NT0_9": "V", "NT1_9": "A", "RD0_2": "A", "XW0_1": "A", "RD0_0": "A", "RD1_0": "V", "NT1_4": "V"}
-TW = {"AV0": 0.1, "F161": -1.7, "ONE": -2.6, "LS0": 0.1, "DU": -4.5, "ui1": 3.9, "AB1_01": 0.1, "BH": -1.8, "CA": 5.5, "XR1_1": -2.1, "AB0_10": 0.5, "TM": 3.1,
-      "SE": 0.7, "EQ0": 6.4, "XR0_0": -1.6, "un0": -0.2, "Qo0": 2.0, "BK1": -0.7, "EQ1": 1.3, "ZH": -5.3, "th0": -3.9, "XW1_0": 5.5, "NT0_9": -0.6, "KB": 3.7,
-      "q10": 2.1, "ST1_1": -0.2, "SC0": -3.8, "DD0_0": -1.3, "ui0": -0.1, "RA": 2.1, "SA": 1.3, "Ro1": 1.2, "oo0": 1.8, "PNb": -1.1, "P0a": 3.5, "XW1_1": -2.9,
-      "RD0_1": -0.9, "RD0_2": -5.3, "Ro0": -0.6, "ST3_0": -1.4, "Qi1": 1.1, "DD1_0": -0.5, "q11": 0.3, "RD1_1": 0.9, "u15": 4.1, "qo0": 1.6, "c161": -0.5,
-      "yx1": -3.5, "ST3_1": -1.4, "ST2_1": -1.5, "CD": -4.0, "NID": 1.3, "C0": -3.8, "NT1_8": -2.8, "AB1_00": 3.3, "DD1_1": -0.2, "rep0": -1.0, "Wo2_0": -1.9}
 
 
 PHYS = {"V": "V", "A": "A", "D": "A", "T": "T", "G": "G", "R": "G", "S": "S"}
 
 
-def schedule(ops):
-    N = len(ops)
+def name(o):
+    return o["ph"] + ((o["pre"][-1] + "*") if o["take"] else o["rd"][0] + ">" if o["wr"][-1][:2] == "PC" else o["wr"][-1])
+
+
+ORDER = """SU0* Ro0@ AS+ sq1@ SU0 R160@ IOT2048@ CC1@ rs2@ XRb0_0@=A XRa0_0@=V RD0_1*@ U0 NT1_4@ vv0 AI+ sq0 CC0 c161@ SE3@=V AB0_0_0*@ c160 Ro1@ AJ+ Ro0 R0_3@=V R161@ AB0_0_1*@ XRa0_1@=V XRa0_0=V XRb0_0=A R0_2@=A XRb0_1@=A IW@ AB0_0_0@ RD1_0*@ IOT3072@ XRb1_0@=V XRb0_1=V XRa0_1=A AB0_1_0*@ AB0_0_1* AB0_0_1@ RD1_1*@ AB0_0_0* R0_10@=A W161 XWb1_0=A AB0_1_0@ W320 RD0_2*@ sW0 AB0_1_1*@ SE4@=A RD1_1@=V W0u1* RD0_2@=A AB0_0_0 AB0_1_1* T316@ SK0_0*@ W0u1 RS@ X01=V u151@ AB0_1_1@ AB0_0_1 J0@ RD1_0@=V W321 AB1_0_1*@ BA+ SU1* T30@ sW1 XRb1_1@=A AB0_1_1 CU0@ SK0_0@ SU1 SW4@=V SK0_0* J0'@ RD0_0*@ u161@ U1 XWa1_0@=V CU112@ SK0_1*@ XWa1_0=A vv1 AB0_1_0* u151 sq1 u161 RD1_3*@ CC1 s100_0@ SK0_0 SK0_1@ c161 AB0_1_0 RD0_3*@ SR@ s100_0 s100_1@ RD0_1@=A Ro1 RD0_0@=V AB1_1_0*@ XWb0_1=V XRb1_0=A SK0_1* RD0_3@=A AB1_0_0*@ qi0_0@ qi0_1@ AB1_1_0@ SA1@=V AB1_1_1@ qo0_0@ XWb1_0@=A AB1_1_1 AB1_0_1 AB1_0_0 qo0_1@ AB1_1_1*@ Qo0_0@ Qo0_1@ SA7@=V SA8@=V SA4@=V RD1_2*@ SK0_1 Qi0@ D1'@=A qi0_0 XRb1_1=A gDD0_0@ SA6@=A s100_1 NT1_4 AB1_0_0* AB1_0_0@ qo0_0 qi0_1 Qo0_0 qo0_1 AB1_0_1* gDD0_0 NT0_4 AB1_0_1@ gDD0_1@ AB1_1_1* gAB0_0_1@ AB1_0_0>@ AB1_1_0* Qo0_1 pr0@ Qi0 gDD0_1 AB1_0_0> SA2@=V AB1_1_0 XWb1_1@=A q10@ AB1_1_0>@ ps0@ gAB0_0_1 AB1_1_0> pr0'@ gAV0*@ pr0 ee0@ gAB0_1_1@ gAV0* SK1_1 SK1_1@ ps0'@ ps0 UN@ gAB0_1_1 s101_1@ gID>1@ gAB0_0_0> s101_1 RD1_3@=V gAB0_0_0>@ pr0' qi1_1 SA3@=A RD1_2@=A qi1_1@ gAB0_1_0>@ ps0' F160@ q10 qo1_1 XWa1_1=A qo1_1@ F160 ee0 gAB0_1_0> CQ0@ XWa1_1@=A Qo1_1@ NT0_15*@ Qo1_1 SA5@=V CQ0 IW'@=V gDD1_0@ gZs0 NT0_8*@ gDD1_0 gDD1_1 gID>0- gZs0@ NT0_8* NT0_12@=A gDD1_1@ gLS0@ NT0_12*@ WI@- X0@- CW16@- D1@- RT@- th0@- ONE@- wt0@- NT0_15* P@- NT0_12* FC0@- oT1@ Pa@- GW@- gLS0 Pg@- NT0_8=A NT0_8@=V XWb1_1=V FCgs@- CW0@- FCa0@- FCg15@-=A E32@- gAB1_1_0*@ NT0_12=A FCps@-=A gno0@ SH@- NT0_15@=V FCa16@-=A BK1@- gAB1_1_0 ID@- gAB1_0_1@ FCgs15@-=V gAB1_0_1 Qi1@ NT0_15=V gAB1_1_0* HID@-=A gAB1_1_1*@ X144@- ST_0@ gno0 EQ1@- NID@-=A q11@ Qi1 WF_1@- ST_0 K16@- gAB1_1_1* q11 Pl@- gAV0@ WF_0@ gAB1_1_1@ ZD@- WF_0 pr1 C0@- GE@- gAB1_0_0>@ pr1@ KB@-=A EQ0@- gAV1* ee1 grep0@ W161@- SW8@-=A grep0 gID>1 ps1@ BLK@- gAB1_1_0@ oT1 R0_1@-=A C0'@- gof0* gAV1*@ ps1 ZX@- gAB1_1_1 Ph@- R0_9@-=A pr1'@ CQ1 SE2@-=V gof0*@ W0u1*@- gAB1_0_0> SE5@-=A R0_13@-=V IOT0@- W160@- gof0@ R0_15@-=A pr1' SW2@-=V ee1@ gAB1_1_0>@ NF0=A FCth@- SW6@-=A ps1'@ W0u0*@- NB@- gof0 gAB1_1_0> SE0@-=A W0u1@- ps1' W320@- F161@ R0_4@-=A gAV1 W321@- CQ1@ gZs1@ R0_12@-=A F161 sW0@- FCwL@- SW5@-=V SW3@-=A goo0 gZs1 NT1_8=A gAV0 gLS1@ NT1_8* R0_5@-=V BH@-=A NT1_15*@ goo0@ gLS1 R0_0@-=V sW1@- R0_8@-=A grep1@ AS*@ W0u0@- SW7@-=A R0_14@-=V SE6@-=V gof1*@ grep1 XO0 SW1@-=V SE7@-=A X0 R0_7@-=V NT1_8*@ R0_11@-=V gof1@ gof1* ZG@- R0_6@-=A AS@ C1@- X0'@ AS* NT1_12* NT1_15@=A XWb0_0@-=A THd@- gof1 yx0 BL@-=V X00@-=V THn*@- goo1@ goo1 C1'@- AI@ gno1 NT1_12*@ X01@-=V gno1@ X1 NT1_15* NT1_8@=A SU0*@- AJ@ NT1_12=A THn@- gAV1@ II@- SU1*@- IOT1024@- yx1 W160- XO1- gID>0@- XWb0_0-=A BA@ SE1@-=V NT1_12@=A NT1_15=V SU0@- X1@ SU1@- NF1=A W0u0*- U0@- XWb0_1@-=A ST_1 yw1 vv0@- ST_1@ yw0 sq0@- WF_1 W0u0- U1@- WF_1'@ CC0@- X00-=V vv1@- c160@- NT0_4@- II'@-=V"""
+ORDER = """SU0* AJ@+ U0 c161@ SU0 Ro0@ rs2@ AS+ Ro1@ vv0 SA5@=V R160@ R161@ XRb0_1@=V sq0 sW0 RD0_3*@ BA@+ AI+ CC0 AJ+ RD0_2*@ IOT1024@ c160 BA+ XRb0_0=A NT1_4@ XRa0_0=V AB0_0_1@ XWb1_0@=A AB0_0_1*@ Ro0 SA1@=V XRa0_1@=V XRb1_1@=V W0u1* AB0_0_0* AB0_0_1* XRb0_1=V XRa0_1=A AB0_0_0*@ XWb1_0=A sW1 RD1_0@=V IOT2048@ RD1_0*@ RD0_3@=A W161 XWa1_0=V RD1_2*@ u161@ AB1_1_0*@ AB0_0_0@ AB0_0_1 AB0_1_0* RS@ W0u1 RD0_0*@ X01=V XRb1_0@=V SW5@=V W321 AB0_0_0 RD0_1*@ SK0_0*@ RD0_0@=A AB0_1_1*@ SU1* CU112@ XWb1_1=A SU1 SK0_0* CU0@ SK0_0@ U1 NT0_4 RD0_1@=A vv1 AB0_1_1* AB0_1_0 sq1 u151@ u151 II'@=A s100_0@ CC1 SA7@=V oT1 AB0_1_0*@ c161 AB0_1_1 IW'@=A AB0_1_1@ AB1_0_0*@ SK0_0 SE0@=V Ro1 RD1_1*@ qi0_0@ SW2@=V XWb0_1=V RD1_3*@ qo0_0@ XRb1_0=A AB0_1_0@ AB1_1_0@ AB1_0_0@ SK0_1* RD1_1@=A Qo0_0@ XWa1_0@=V AB1_1_1*@ AB1_0_1 gDD0_0@ SK0_1*@ SK0_1 s100_0 XRb1_1=A s100_1 NT1_4 qi0_0 AB1_1_1 AB1_0_1*@ qi0_1 SK0_1@ qo0_0 SW3@=V qo0_1 s100_1@ AB1_0_1* Qo0_0 RD1_3@=A Qo0_1 AB1_0_0* u161 gDD0_0 Qi0 AB1_0_0 AB1_0_1@ D1'@=A qi0_1@ AB1_1_1* AB1_1_1@ SA6@=V qo0_1@ SA2@=V AB1_0_0>@ Qo0_1@ AB1_1_0* SA4@=V SK1_1@ gDD0_1@ AB1_1_0>@ AB1_0_0> gDD0_1 pr0 AB1_1_0 gAB0_0_1@ RD1_2@=A gAB0_0_1 AB1_1_0> gAV0*@ Qi0@ s101_1@ gAB0_0_0>@ pr0@ q10@ ps0@ gAB0_0_0> q10 ps0 SK1_1 XWa1_1@=A SE4@=A gAB0_1_1@ pr0' qi1_1@ ee0@ gAB0_1_0>@ pr0'@ NT0_15=A gDD1_1 gDD1_1@ CQ0@ s101_1 ps0' gAB0_1_1 qo1_1@ gZs0 qi1_1 gID>1@ XWa1_1=A ee0 NT0_12*@ gAB0_1_0> ps0'@ NT0_8*@ qo1_1 F160 XWb1_1@=A gZs0@ Qo1_1@ Qo1_1 F160@ gAV0* CQ0 gDD1_0@ gDD1_0 FC0@- NT0_12* WI@- X0@- P@- ONE@- RT@- th0@- D1@- wt0@- NT0_12=A Pa@- NT0_8* FCa0@- Pg@- FCgs@- FCg15@-=A E32@- FCa16@-=A NT0_15*@ FCps@-=A NT0_12@=V NT0_15* gLS0 X144@- EQ0@- NT0_8@=A NT0_8=V gAB1_1_1* gLS0@ CW16@- gAB1_1_0*@ NT0_15@=V R0_6@-=A R0_11@-=V CW0@- R0_13@-=A GE@- C0@- gno0@ gAB1_0_1@ gno0 gID>1 SH@- gAB1_0_1 R0_14@-=A gAB1_1_1*@ gAB1_1_0* ST_0 WF_1@- R0_1@-=A K16@- Qi1@ R0_2@-=A Qi1 ST_0@ ID@- WF_0@ gID>0- WF_0 oT1@ gAV1*@ SE6@-=A ZX@- gAV1* GW@- grep0@ pr1 Ph@- gAV0 q11@ R0_7@-=V R0_0@-=A FCth@- pr1@ EQ1@- grep0 gAB1_1_1@ SE5@-=A gAB1_0_0>@ gAB1_0_0> R0_12@-=A FCgs15@-=A SE3@-=V ps1 ps1@ W320@- SW7@-=V HID@-=A q11 gAB1_1_0@ R0_10@-=A W160@- pr1' pr1'@ R0_3@-=A gof0* SE1@-=A Pl@- W0u0*@- IW@- J0@- ee1@ NID@-=A C0'@- ps1' IOT0@- UN@ SW1@-=A ee1 ps1'@ gAB1_1_0>@ SW4@-=V R0_9@-=V ZG@- gAB1_1_0> SE2@-=A sW0@- gof0 CQ1@ FCwL@- F161 THd@- W161@- gAB1_1_1 CQ1 F161@ BH@-=A gof0*@ gAB1_1_0 BLK@- W0u1*@- XO0 gAV0@ BK1@- R0_5@-=A NB@- SE7@-=A gZs1@ W0u0@- goo0 gZs1 NT1_8*@ SW6@-=V gAV1@ NT1_8* BL@-=V gLS1@ ZD@- KB@-=A gLS1 THn*@- yx0 gof0@ W0u1@- R0_15@-=V grep1@ grep1 goo0@ gAV1 THn@- gno1@ SW8@-=A R0_4@-=V NT1_15*@ NT1_8@=A XWb0_0@-=A gno1 NT1_15=A X01@-=V NT1_8=A AS*@ X0 gof1 J0'@- X0'@ gof1* X00@-=V gof1*@ SA8@-=A T30@- NT1_15* NT1_12* NT1_12*@ SU1*@- XWb0_1@-=A T316@- gof1@ AS@ RD0_2@-=A XRa0_0@-=A XRb0_0@-=A W321@- SU0*@- NT1_15@=A goo1@ goo1 SU1@- C1@- gID>0@- sW1@- AS* SR@- W160- X1@ SU0@- NT1_12=A NT1_12@=A X1 NF0=V W0u0*- U1@- yx1 C1'@- AI@ U0@- yw0 vv1@- XO1- XWb0_0-=A ST_1 SA3@-=V ST_1@ NF1=A vv0@- II@- sq1@- W0u0- IOT3072@- sq0@- WF_1 WF_1'@ yw1 X00-=V CC0@- NT0_4@- CC1@- R0_8@-=V W320- c160@-"""
+
+
+def classes(ops):
+    seen, out = {}, []
+    for o in ops:
+        c = name(o)
+        if c[:2] in ("ST", "WF") and c[3:4] == "_":
+            c = c[:2] + c[3:]
+        if c in ("X", "gID>", "XO"):
+            c += str(o["ch"])
+        seen[c, o["v"]] = seen.get((c, o["v"]), -1) + 1
+        out.append(c + "'" * seen[c, o["v"]] + ("@" if o["v"] == 0 else ""))
+    return out
+
+
+def places(text):
+    words = text.split()
+    out = {}
+    for r, x in enumerate(words):
+        x, _, q = x.partition("=")
+        c = x.rstrip("+-")
+        out[c] = (r + len(words) * (x.count("+") - x.count("-")), q)
+    return out
+
+
+def ordered(ops, bank):
     lastw, readers = {}, {}
     for i, o in enumerate(ops):
-        d = set()
-        for r in o["rd"]:
-            if r in lastw:
-                d.add(lastw[r])
-        for w in o["wr"]:
+        d = set(lastw[r] for r in o["rd"] if r in lastw)
+        for w in o["wr"] + o["pre"]:
             if w in lastw:
                 d.add(lastw[w])
             d.update(readers.get(w, ()))
-        d.discard(i)
-        o["dep"] = sorted(d)
+        o["dep"] = sorted(d - {i})
         for r in o["rd"]:
             readers.setdefault(r, []).append(i)
         for w in o["wr"]:
             lastw[w] = i
             readers[w] = []
-    succ = [[] for _ in range(N)]
-    for i, o in enumerate(ops):
-        for d in o["dep"]:
-            succ[d].append(i)
-    pri = [0.0] * N
-    for i in range(N - 1, -1, -1):
+    place = places(ORDER)
+    key = []
+    for o, c in zip(ops, classes(ops)):
+        x = [y for y in o["alts"] if y[0] == place[c][1]] or o["alts"]
+        o["q"], o["us"], o["fn"] = x[0]
+        key.append(place[c][0] + len(place) * o["v"])
+    free, fin, order = {q: 0.0 for q in "VATGS"}, {}, []
+    rel = {b: (0.0, None) for b in POOL}
+    todo = sorted(range(len(ops)), key=lambda i: (key[i], i))
+    while todo:
+        i = next(i for i in todo if all(d in fin for d in ops[i]["dep"]) and (rel or not ops[i]["take"]))
         o = ops[i]
-        pri[i] = min(x[1] for x in o["alts"]) + o["lat"] + max([pri[s] + HOP for s in succ[i]], default=0.0)
-    for i, o in enumerate(ops):
-        pri[i] += TW.get(o["wr"][-1], 0.0)
-    left = [len(o["dep"]) for o in ops]
-    fin = [0.0] * N
-    free = {"V": 0.0, "A": 0.0, "T": 0.0, "G": 0.0, "S": 0.0}
-    cand = [i for i in range(N) if left[i] == 0]
-    rdy = {i: 0.0 for i in cand}
-    order = []
-    while cand:
-        best = None
-        ests = []
-        for i in cand:
-            for x in ops[i]["alts"]:
-                if EN.get(ops[i]["wr"][-1], x[0]) != x[0]:
-                    continue
-                st = max(free[PHYS[x[0]]], rdy[i])
-                ests.append((st, st + x[1], i, x))
-        bi = {}
-        for e in ests:
-            w = e[1] + (VBIAS if e[3][0] == "V" else 0.0)
-            if e[2] not in bi or w < bi[e[2]][0]:
-                bi[e[2]] = (w, e)
-        bi = [x[1] for x in bi.values()]
-        tmin = min(e[0] for e in bi)
-        best = max((e for e in bi if e[0] <= tmin + LOOK), key=lambda e: (pri[e[2]], -e[2]))
-        st, en, i, x = best
-        cand.remove(i)
-        ops[i]["q"], ops[i]["fn"], ops[i]["start"] = x[0], x[2], st
-        free[PHYS[x[0]]] = en
-        fin[i] = en + ops[i]["lat"]
+        if o["take"]:
+            b = min(rel, key=lambda k: (rel[k][0], k))
+            if rel[b][1] is not None:
+                o["dep"] = sorted(set(o["dep"] + [rel[b][1]]))
+            bank[o["take"]] = b
+            del rel[b]
+        q = PHYS[o["q"]]
+        o["start"] = max([free[q]] + [fin[d] + (0.0 if o["acc"] and ops[d]["q"] == "T" else HOP) for d in o["dep"]])
+        free[q] = o["start"] + o["us"]
+        fin[i] = free[q] + o["lat"]
+        if o["give"]:
+            rel[bank[o["give"]]] = (fin[i], i)
+        todo.remove(i)
         order.append(i)
-        for s in succ[i]:
-            left[s] -= 1
-            if left[s] == 0:
-                cand.append(s)
-                rdy[s] = max(fin[d] for d in ops[s]["dep"]) + HOP
-    return order, max(fin)
+    return order, max(fin.values())
 
 
 def rank_program(g, core, T, topo):
     rank = T.rank_of(core)
     if rank is None:
         return
-    ops, neng = build(g, core, rank, T, topo)
-    order, _ = schedule(ops)
+    bank = {}
+    ops, neng = build(g, core, rank, T, topo, bank)
+    order, _ = ordered(ops, bank)
     S = T.sem
     handle = {"V": g.vector, "A": g.scalar, "T": g.tensor, "G": g, "S": g.sync}
     cnt = {"V": 0, "A": 0, "T": 0, "G": 0}
@@ -519,6 +542,8 @@ def rank_program(g, core, T, topo):
         need = {}
         for d in o["dep"]:
             sm, val = ops[d]["done"]
+            if o["acc"] and sm == "qT":
+                continue
             if kn.get(sm, 0) < val:
                 need[sm] = max(need.get(sm, 0), val)
         items = sorted(need.items(), key=lambda kv: -max(ops[d]["start"] for d in o["dep"] if ops[d]["done"][0] == kv[0]))
@@ -536,9 +561,10 @@ def rank_program(g, core, T, topo):
         if o["q"] in ("S", "D"):
             sm = "d%d" % nd
             nd += 1
-            ins.then_inc(S[sm], 16)
-            o["done"] = (sm, 16)
-            used[sm] = 16
+            for one in ins:
+                one.then_inc(S[sm], 16)
+            o["done"] = (sm, 16 * len(ins))
+            used[sm] = 16 * len(ins)
         elif o["q"] == "R":
             nsend += 1
             o["done"] = (o["tag"], neng)

from concourse.mybir import dt, AluOpType, AxisListType, ActivationFunctionType as AF

NC = 2
n = 256 // NC
nb = n // 16
H2 = 64
NP = n // H2
VIS, ST = 4, 3
ROT = 712
BF, FP, F16, I32, U16 = "bfloat16", "float32", "float16", "int32", "uint16"
PAR = {'ps': [1, 0], 'xs': [2, 2, 1, 1], 'ws': [1, 1, 2, 2], 'way': 'MMMA', 'sh': 'u', 'rl': 3.0, 'w0': 'm', 'rd': [0], 'dt': [0, 1]}

SCRATCH = {
    "X": ("sbuf", [128, 4096 + 256], BF), "XO": ("sbuf", [128, 4096 + 256], BF),
    "RT2": ("sbuf", [128, 16384], I32), "rs2": ("dram", [8, 32, 1024], I32), "IOT": ("sbuf", [128, 4096], FP),
    "WI": ("sbuf", [128, 256], I32), "wt0": ("sbuf", [128, 1], I32), "th0": ("sbuf", [128, 1], I32),
    "PI": ("sbuf", [128, 8], I32), "FC": ("sbuf", [128, 16], FP), "GE": ("sbuf", [128, 32], FP),
    "X144": ("sbuf", [128, 144], BF), "CW": ("sbuf", [128, 144], BF), "CU": ("sbuf", [128, 128], BF), "GW": ("sbuf", [128, 128], BF), "T3": ("sbuf", [128, 128], BF),
    "K16": ("sbuf", [128, n], BF), "KB": ("sbuf", [128, n], BF), "C0": ("sbuf", [128, n], FP), "C1": ("sbuf", [128, n], FP), "NB": ("sbuf", [128, n], BF),
    "E32": ("sbuf", [128, 8, 32], BF), "EQ0": ("sbuf", [128, 8, 32], BF), "EQ1": ("sbuf", [128, 8, 32], BF),
    "R0": ("sbuf", [128, 16, 128], BF), "R1": ("sbuf", [128, 8, 128], BF), "SA": ("sbuf", [128, 8, 128], BF), "SW": ("sbuf", [128, 8, 128], BF), "SE": ("sbuf", [128, 8, 128], BF),
    "IW": ("sbuf", [128, 16], FP), "II": ("sbuf", [128, 16], BF), "ONE": ("sbuf", [128, 128], BF), "J0": ("sbuf", [128, n], FP), "D1": ("sbuf", [128, n], FP),
    "ZX": ("sbuf", [128, 144], BF), "ZD": ("sbuf", [128, 144], BF), "ZG": ("sbuf", [128, 144], BF),
    "ID": ("sbuf", [128, 128], BF), "NID": ("sbuf", [128, 128], BF), "HID": ("sbuf", [128, 128], BF), "SH": ("sbuf", [128, 128], BF), "SR": ("sbuf", [128, 128], BF),
    "UN": ("sbuf", [128, 128], BF), "BLK": ("sbuf", [128, 128], BF), "BH": ("sbuf", [128, 128], BF), "BL": ("sbuf", [128, 128], BF), "BK1": ("sbuf", [128, 128], BF),
    "S0": ("sbuf", [128, 128], BF), "THd": ("sbuf", [128, n], F16), "THn": ("sbuf", [128, n], F16),
    "XW": ("sbuf", [128, 4096], BF), "XR": ("sbuf", [128, 4096], BF), "AB": ("sbuf", [128, 256, 16], BF), "DD": ("sbuf", [128, 4096], BF),
    "NT": ("sbuf", [128, 17 * 256], FP), "RD": ("sbuf", [128, 4096], FP),
    "W16": ("sbuf", [128, 256], F16), "S1": ("sbuf", [128, 256], FP), "W0u": ("sbuf", [128, 16], U16), "X0": ("sbuf", [128, 256], BF),
    "SU": ("sbuf", [128, 256], I32), "SK": ("sbuf", [128, 256], I32),
    "U": ("sbuf", [128, 16], I32), "vv": ("sbuf", [128, 16], I32), "sq": ("sbuf", [128, 16], I32), "CC": ("sbuf", [128, 16], I32), "c16": ("sbuf", [128, 16], U16),
    "Ro": ("sbuf", [128, 256], U16), "R16": ("sbuf", [128, 256], F16), "s10": ("sbuf", [128, 16], I32), "qi": ("sbuf", [128, 16], FP), "qo": ("sbuf", [128, 16], U16),
    "Qo": ("sbuf", [128, 256], U16), "Qi": ("sbuf", [128, 256], I32), "pr": ("sbuf", [128, 256], I32), "ps": ("sbuf", [128, 256], I32),
    "F16": ("sbuf", [128, 256], F16), "q1": ("sbuf", [128, 256], I32), "ee": ("sbuf", [128, 256], FP), "CQ": ("sbuf", [128, 256], F16),
    "Zs": ("sbuf", [128, 256], BF), "LS": ("sbuf", [128, 256], FP), "no": ("sbuf", [128, 16], U16), "NF": ("sbuf", [128, 256], FP),
    "u16": ("sbuf", [128, 16], U16), "u15": ("sbuf", [128, 16], I32), "oT": ("sbuf", [128, 16], FP),
    "rep": ("sbuf", [128, 16], BF), "of": ("sbuf", [128, 16], FP), "oo": ("sbuf", [128, 16], U16), "AV": ("sbuf", [128, 256], I32),
    "AC": ("sbuf", [128, 16], FP), "AS": ("sbuf", [128, 1], FP), "AI": ("sbuf", [128, 2], I32), "BA": ("sbuf", [128, 1], FP),
    "W32": ("sbuf", [128, 256], FP), "sW0": ("dram", [16, 32, n], FP), "sW1": ("dram", [16, 32, n], FP),
    "PC0": ("psum", [128, 512], FP), "PC1": ("psum", [128, 512], FP),
}
POOL = ["B%d" % _b for _b in range(6)]
for _b in POOL:
    SCRATCH[_b] = ("psum", [128, 512], FP)
for _t in range(VIS):
    SCRATCH["WF%d" % _t] = ("sbuf", [128, 256], U16)
    if _t:
        SCRATCH["ST%d" % _t] = ("sbuf", [128, 256], U16)

NDMA = 32
SEMAPHORES = ["qV", "qA", "qT", "qG", "ls"] + ["d%d" % i for i in range(NDMA)] + ["ar%d_%d" % (t, h) for t in range(1, VIS) for h in range(NC)]

CY = 0.00083 * 1.12
PEC = 0.00042 * 1.12
GA = 1.5
SCA = 3.0
HOP = 0.12


def cv(cyc):
    return 0.05 + max(64, cyc) * CY


def ca(cyc):
    return 0.065 + max(64, cyc) * CY


def build(g, core, rank, T, topo, bank):
    ops = []
    A = AluOpType
    v, a, t = g.vector, g.scalar, g.tensor
    cur = [0, "", 0]

    def add(alts, rd, wr, lat=0.0, tag="", take=None, give=None, pre=(), acc=False):
        ops.append({"v": cur[2], "ch": cur[0], "ph": cur[1], "acc": acc, "alts": alts, "rd": list(rd), "wr": list(wr), "lat": lat, "tag": tag,
                    "take": take, "give": give, "pre": list(pre)})

    def V(cyc, rd, wr, fn):
        add([("V", cv(cyc), fn)], rd, wr)

    def ACT(cyc, rd, wr, fn):
        add([("A", ca(cyc), fn)], rd, wr)

    def AV(cyc, rd, wr, fv, fa, half=False):
        add([("V", cv(cyc / 2 if half else cyc), fv), ("A", ca(cyc), fa)], rd, wr)

    def PE(cols, rd, wr, calls, **k):
        def fn():
            ins = None
            for c in (calls() if "take" in k else calls):
                ins = t.matmul(*c)
            return ins
        add([("T", cols * PEC + 0.05, fn)], rd, wr, **k)

    def DMA(us, rd, wr, pairs, q="S"):
        eng_ = g.sync if q == "S" else g.scalar
        add([(q, 0.08 * len(pairs), lambda: [eng_.dma_start(o, i) for o, i in pairs])], rd, wr, lat=us)

    def G(cnt, wr, fn, rd=()):
        add([("G", 0.15 + 2 * cnt * CY, fn)], list(rd), wr)

    def gather(cnt, rd, wr, out, win):
        AV(GA * cnt, rd, wr, lambda: v.tensor_copy(out, win), lambda: a.activation(out, win, AF.Identity))

    def affine(cyc, rd, wr, out, src, mul, plus, half=False):
        AV(cyc, rd, wr, lambda: v.tensor_scalar(out, src, mul, plus, A.mult, A.add), lambda: a.activation(out, src, AF.Identity, bias=plus, scale=mul), half)

    nk = [0]

    def pooled(cols, rd, calls, cyc, crd, wr, use):
        nk[0] += 1
        key = "k%d" % nk[0]
        PE(cols, rd + crd, [key], lambda: calls(T[bank[key]]), take=key, pre=wr)
        add([(q, cv(cyc) if q == "V" else ca(cyc), (lambda f=f: f(T[bank[key]]))) for q, f in use], [key] + crd, wr, give=key)

    def plus(out, w, c):
        return [("V", lambda P: v.tensor_scalar(out, P[:, 0:w], c, None, A.add)), ("A", lambda P: a.activation(out, P[:, 0:w], AF.Identity, bias=c))]

    def most(out, w):
        return [("V", lambda P: v.tensor_tensor_scan(out, T.C0[:, 0:w], P[:, 0:w], 0.0, A.min, A.max))]

    def least(out, w):
        return [("V", lambda P: v.tensor_tensor_scan(out, T.C1[:, 0:w], P[:, 0:w], 0.0, A.max, A.min))]

    fl = {"allow_small_or_imprecise_dtypes": True}
    DMA(2.0, [], ["WI"], [(T.WI[:], T.wd[:, :])], "D")
    DMA(5.5, [], ["X"], [(T.X[:, 0:4096], T.x[:, :])])
    DMA(2.0, [], ["wt0"], [(T.wt0[:], T.wt[:, :])], "D")
    DMA(7.5, [], ["RT"], [(T.RT2[:, ROT:1024], T.rt[:, 0:1024 - ROT]), (T.RT2[:, 0:ROT], T.rt[:, 1024 - ROT:1024])])
    DMA(2.0, [], ["th0"], [(T.th0[:], T.th[:, :])], "D")
    DMA(4.0, ["RT"], ["rs2"], [(T.rs2[:, rr:rr + 16, :], T.RT2[:, 0:1024]) for rr in (0, 16)])
    DMA(24.0, ["rs2"], ["RS"], [(T.RT2[k::16, 1024:16384], T.rs2[:, k + 1:k + 16, :]) for k in range(16)])

    def IO(nm, pat, base, cnt, sl=None, cm=0):
        G(cnt, [nm if sl is None else nm + str(sl[0])], lambda: g.iota(T[nm][:] if sl is None else T[nm][:, sl[0]:sl[1]], pat, base, cm, **fl))
    G(2, ["P"], lambda: g.iota(T.PI[:, 0:2], [[16, 2]], 0, 1))
    IO("FC", [[0, 1]], 0, 1, (0, 1), 1)
    IO("X144", [[1, 144]], 0, 144)
    IO("GW", [[16, 8], [0, 16]], 0, 128)
    IO("K16", [[0, nb], [1, 16]], 0, n)
    IO("CW", [[1, 16]], 112, 16, (0, 16))
    IO("CW", [[1, 128]], 0, 128, (16, 144))
    CWn = ["CW0", "CW16"]
    IO("C0", [[0, n]], 2 ** 24 - 1, n)
    G(n, ["C0"], lambda: g.affine_select(T.C0[:], T.C0[:], [[0, nb], [1, 16]], A.not_equal, -float(2 ** 30), 0, 0))
    IO("E32", [[16, 8], [0, 2], [1, 16]], 0, 256)
    IO("C1", [[0, n]], 0, n)
    G(n, ["C1"], lambda: g.affine_select(T.C1[:], T.C1[:], [[0, nb], [1, 16]], A.not_equal, float(2 ** 30), 0, 0))
    IO("IW", [[256, 16]], -4096, 16)
    IO("II", [[16, 16]], 0, 16)
    IO("T3", [[-1, 16]], 127, 16, (0, 16))
    IO("T3", [[16, 7], [-1, 16]], 15, 112, (16, 128))
    IO("CU", [[1, 112]], 16, 112, (0, 112))
    IO("CU", [[1, 16]], 0, 16, (112, 128))
    IO("J0", [[-16, nb], [0, 16]], -64 * n, n)
    for i in range(4):
        IO("IOT", [[1, 1024]], 1024 * i, 1024, (1024 * i, 1024 * i + 1024))
    IOTn = ["IOT%d" % (1024 * i) for i in range(4)]

    cn = {nm: i for i, nm in enumerate(("0", "a", "g", "gs", "ps", "g15", "gs15", "a0", "wH", "wL", "a16", "th"))}

    def col(nm):
        return T.FC[:, cn[nm]:cn[nm] + 1]

    def COL(nm, src, rd, s1, s2, o0, o1=None):
        V(1, rd, ["FC" + nm], lambda: v.tensor_scalar(col(nm), src, s1, s2, o0, o1) if o1 else v.tensor_scalar(col(nm), src, s1, None, o0))

    def ACOL(nm, src, mul, pl):
        affine(1, ["FC" + src], ["FC" + nm], col(nm), col(src), mul, pl)

    def EQ(out, src, rd, c, mul, cyc, sl=None, op=A.is_equal):
        V(cyc, rd + ["FC" + c] + (["FC" + mul] if isinstance(mul, str) else []), [out],
          lambda: v.tensor_scalar(T[out][:], T[src][:] if sl is None else T[src][:, sl[0]:sl[1]], col(c), col(mul) if isinstance(mul, str) else mul, op, A.mult))

    def SCALE(out, src, mul, cyc):
        affine(cyc, [src] + (["FC" + mul] if isinstance(mul, str) else []), [out], T[out][:], T[src][:, 0:cyc], col(mul) if isinstance(mul, str) else mul, 0.0, True)
    pa = T.PI[:, 2:3]
    V(1, ["P"], ["Pa"], lambda: v.tensor_scalar(pa, T.PI[:, 0:1], 15, None, A.bitwise_and))
    V(1, ["P"], ["Pg"], lambda: v.tensor_scalar(T.PI[:, 3:5], T.PI[:, 0:2], 112, None, A.bitwise_and))
    V(1, ["Pa", "Pg"], ["FCa", "FCg", "FCgs"], lambda: v.tensor_copy(T.FC[:, 1:4], T.PI[:, 2:5]))
    V(256, ["WI"], ["WF0_%d" % h for h in range(NC)], lambda: v.tensor_copy(T.WF0[:], T.WI[:]))
    COL("a0", pa, ["Pa"], 0.0, None, A.is_equal)
    ACOL("g15", "g", 1.0, 15.0)
    EQ("BLK", "GW", ["GW"], "g", 1.0, 64)
    if PAR["w0"] == "m":
        EQ("ZX", "X144", ["X144"], "g15", "a0", 72)
    else:
        SCALE("S0", "BLK", "a0", 128)
    EQ("ID", "CW", CWn, "0", 1.0, 64, (16, 144))
    EQ("NB", "K16", ["K16"], "a", -float(2 ** 24), 64, None, A.not_equal)
    V(1, ["wt0"], ["Ph"], lambda: v.tensor_scalar(T.PI[:, 5:6], T.wt0[:], 0xFC0, None, A.bitwise_and))
    V(1, ["wt0"], ["Pl"], lambda: v.tensor_scalar(T.PI[:, 6:7], T.wt0[:], 63, None, A.bitwise_and))
    V(1, ["Ph", "Pl"], ["FCwH", "FCwL"], lambda: v.tensor_copy(T.FC[:, cn["wH"]:cn["wH"] + 2], T.PI[:, 5:7]))
    SCALE("BH", "BLK", "wH", 128)
    SCALE("BL", "BLK", "wL", 128)
    SCALE("NID", "ID", -1.0, 128)
    EQ("ZD", "X144", ["X144"], "g15", 16384.0, 72)
    SCALE("KB", "K16", 1024.0, 128)
    EQ("EQ0", "E32", ["E32"], "0", 1.0, 128)
    for r in range(16):
        affine(128, ["EQ0"], ["R0_%d" % r], T.R0[:, r, :], T.EQ0[:, :, r:r + 16], 1.0, 0.0, True)
    affine(16, ["FCa"], ["II"], T.II[:], T.II[:], 1.0, col("a"))
    affine(1, ["FCa", "FCgs"], ["FCps"], col("ps"), col("gs"), 1.0, col("a"))
    ACOL("gs15", "gs", 1.0, 15.0)
    EQ("ZG", "X144", ["X144"], "gs15", 1.0, 72)
    COL("th", T.th0[:], ["th0"], -1.0, 2048.0, A.mult, A.add)
    EQ("THd", "K16", ["K16"], "a", "th", 64)
    EQ("BK1", "GW", ["GW"], "gs", 1.0, 64)
    pooled(n, ["THd", "BK1"], lambda P: [(P[:, 0:n], T.BK1[:], T.THd[:], True, True)], n, [], ["THn"], plus(T.THn[:], n, 0.0)[:1])
    SCALE("HID", "ID", 0.5, 128)
    V(64, [], ["ONE"], lambda: v.memset(T.ONE[:], 1.0))
    ACOL("a16", "a", 16.0, 0.0)
    affine(16, ["FCa16"], ["IW"], T.IW[:], T.IW[:], 1.0, col("a16"))
    V(64, [], ["D1"], lambda: v.memset(T.D1[:], 0.125))
    V(nb, ["J0", "FCa"], ["J0"], lambda: v.tensor_scalar(T.J0[:, 15::16], T.J0[:, 15::16], col("a"), 1.0 / (8 * n), A.subtract, A.mult))
    affine(nb, ["J0"], ["D1"], T.D1[:, 15::16], T.J0[:, 15::16], 1.0, 0.125)
    EQ("UN", "CU", ["CU0", "CU112"], "0", -8192.0, 64)
    EQ("SH", "CW", CWn, "0", 1.0, 64, (0, 128))
    EQ("SR", "T3", ["T30", "T316"], "0", 1.0, 64)
    EQ("EQ1", "E32", ["E32"], "ps", 1.0, 128)
    V(32, ["X144", "FCa"], ["GE"], lambda: v.tensor_scalar(T.GE[:], T.X144[:, 0:32], col("a"), None, A.is_le))
    ge = lambda k: T.GE[:, k:k + 1]
    for j in range(8):
        affine(128, ["SH", "GE"], ["SE%d" % j], T.SE[:, j, :], T.SH[:], ge(2 * j), 0.0, True)
        affine(128, ["SR", "GE"], ["SA%d" % (j + 1)], T.SA[:, j, :], T.SR[:], ge(15 - j), 0.0, True)
        affine(128, ["EQ1", "GE"], ["SW%d" % (j + 1)], T.SW[:, j, :], T.EQ1[:, :, 14 - 2 * j:30 - 2 * j], ge(15 - j), 0.0, True)
        if len(PAR["dt"]) < NC:
            affine(128, ["EQ1"], ["R1_%d" % (j + 1)], T.R1[:, j, :], T.EQ1[:, :, j + 1:j + 17], 1.0, 0.0, True)

    dst = T.cores[(rank + ST) % len(T.cores)]
    rid, pid, _se = topo.addr(dst)
    eng = topo.engines(core, dst)[:8]
    msk = sum(1 << e for e in eng)
    hs = list(range(NC))
    XV = T.X[:, 0:4096]

    def pcs(nm, h):
        return ["%s%d_%d" % (nm, h, w) for w in range(NP)]

    def two(nm, pn):
        return [nm + "a" + pn, nm + "b" + pn]

    def values(buf, lst, lstn, w0, pn, sp):
        for i in range(sp):
            lo, hi = w0 + i * H2 // sp, w0 + (i + 1) * H2 // sp
            gather(16 * (hi - lo), lstn + ["X"], two(buf, pn)[i::sp], T[buf][:, 16 * lo:16 * hi], XV.indirect(T[lst][:, lo:hi]))

    def diffs(src, srcn, sub, subn, w0, nm):
        for o in range(2):
            def calls(P, o=o):
                c = []
                for kk in range(8):
                    c.append((P[:, kk::8], T.ID[:], src(8 * o + kk), True, False))
                    c.append((P[:, kk::8], T.NID[:], sub(8 * o + kk), False, True))
                return c
            pooled(16 * H2, srcn + subn + ["ID", "NID"], calls, 8 * H2, [], ["%s_%d" % (nm, o)],
                   [("A", lambda P, o=o: a.activation(T.AB[:, w0:w0 + H2, 8 * o:8 * o + 8], P[:], AF.Abs))])

    def views(hh):
        lo, hi = hh[0], hh[-1] + 1
        cur[0] = lo
        return (lambda nm: T[nm][:, lo * n:hi * n]), (lambda nm: T[nm][:, lo * nb:hi * nb]), (lambda *nms: [x + str(h) for x in nms for h in hh])

    def table(h, js, rd, terms):
        def calls(P):
            return [(P[:, i * n:(i + 1) * n], m, x_, z == 0, z == len(terms(j)) - 1) for i, j in enumerate(js) for z, (m, x_) in enumerate(terms(j))]
        k = len(js)
        pooled(n * sum(len(terms(j)) for j in js), rd, calls, k * n, [], ["NT%d_%d" % (h, js[0])],
               plus(T.NT[:, (17 * h + js[0]) * n:(17 * h + js[0] + k) * n], k * n, 2048.0))

    def head(vis, h):
        N_, Wd, x = views([h])
        c0, c1 = h * n, (h + 1) * n
        PC, pc = T["PC%d" % h], "PC%d" % h
        wf, wfn = "WF%d" % vis, "WF%d_%d" % (vis, h)
        V(n / 2, [wfn], x("W16"), lambda: v.tensor_scalar(N_("W16"), N_(wf), -2048.0, None, A.add))
        if PAR["w0"] == "m":
            pooled(64 * 16, x("W16") + ["ZX"], lambda P: [(P[:, 0:nb], T.ZX[:, 15 - m:143 - m], T.W16[:, c0 + m:c1:16], m == 0, m == 15) for m in range(16)],
                   nb, [], x("W0u"), plus(Wd("W0u"), nb, 2048.0)[:1])
        else:
            pooled(2 * n, x("W16") + ["ID", "NB", "S0"], lambda P: [(P[:, 0:n], T.ID[:], T.NB[:], True, False), (P[:, 0:n], T.S0[:], N_("W16"), False, True)],
                   n, ["C0"], x("S1"), most(N_("S1"), n))
            V(nb, x("S1"), x("W0u"), lambda: v.tensor_scalar(Wd("W0u"), T.S1[:, c0 + 15:c1:16], 2048.0, None, A.add))
        gather(n, x("W0u") + ["X"], x("X0"), N_("X0"), XV.indirect(Wd("W0u")))
        pooled(3 * n, x("X0") + ["BH", "BL", "ID", "NB"],
               lambda P: [(P[:, 0:n], T.ID[:], T.NB[:], True, False), (P[:, 0:n], T.BH[:], N_("X0"), False, False), (P[:, 0:n], T.BL[:], N_("X0"), False, True)],
               n, ["C0"], x("SU"), most(N_("SU"), n))
        V(nb, x("SU"), x("U"), lambda: v.tensor_scalar(Wd("U"), T.SU[:, c0 + 15:c1:16], 4095, None, A.bitwise_and))
        V(nb, x("U"), x("vv"), lambda: v.tensor_scalar(Wd("vv"), Wd("U"), 592.0, None, A.add))
        V(nb, x("vv"), x("sq"), lambda: v.tensor_tensor(Wd("sq"), Wd("vv"), Wd("vv"), A.mult))
        V(nb, x("sq"), x("CC"), lambda: v.tensor_scalar(Wd("CC"), Wd("sq"), 5, 1023, A.arith_shift_right, A.bitwise_and))
        V(nb, x("CC"), x("c16"), lambda: v.tensor_copy(Wd("c16"), Wd("CC")))
        V(GA * n, x("c16") + ["RT"], x("Ro"), lambda: v.tensor_copy(N_("Ro"), T.RT2[:, 0:1024].indirect(Wd("c16"))))
        own = vis in PAR["rd"]
        rdn = ["RT", "RS"]
        if own:
            V(n / 2, x("Ro"), x("R16"), lambda: v.tensor_scalar(N_("R16"), N_("Ro"), -2048.0, None, A.add))
            rdn = ["RD%d_%d" % (h, r4) for r4 in range(4)]
            for r4 in range(4):
                pooled(4 * n, x("R16") + ["R0_%d" % r for r in range(4 * r4, 4 * r4 + 4)],
                       lambda P, r4=r4: [(P[:, i * n:(i + 1) * n], T.R0[:, 4 * r4 + i, :], N_("R16"), True, True) for i in range(4)],
                       4 * n, [], [rdn[r4]], plus(T.RD[:, (16 * h + 4 * r4) * n:(16 * h + 4 * r4 + 4) * n], 4 * n, 2048.0))
        for w in range(NP):
            w0 = c0 + w * H2
            pn = "%d_%d" % (h, w)
            values("XW", wf, [wfn], w0, pn, PAR["ws"][h * NP + w])
            values("XR", "Ro", x("Ro"), w0, pn, PAR["xs"][h * NP + w])
            diffs(lambda k, w0=w0: T.XR[:, 16 * w0 + k:16 * (w0 + H2):16], two("XR", pn), lambda k, w0=w0: T.X0[:, w0:w0 + H2], x("X0"), w0, "AB" + pn)
            keys = lambda o_, w=w, w0=w0: ([(o_, T.ID[:], T.KB[:, 0:H2], True, False)] +
                                           [(o_, T.ZD[:, 15 - m:143 - m], T.AB[:, w0 + m:w0 + H2:16, :], False, m == 15) for m in range(16)])
            rd = ["AB%s_0" % pn, "AB%s_1" % pn, "ZD", "KB", "ID"]
            if PAR["ps"][h]:
                pooled(17 * H2, rd, lambda P, keys=keys: keys(P[:, 0:H2]), H2, ["C1"], ["SK" + pn], least(T.SK[:, w0:w0 + H2], H2))
            else:
                PE(17 * H2, rd, [pc], keys(PC[:, w * H2:(w + 1) * H2]))
        if not PAR["ps"][h]:
            V(n, ["C1"], [pc] + pcs("SK", h), lambda: v.tensor_tensor_scan(N_("SK"), T.C1[:], PC[:, 0:n], 0.0, A.max, A.min))
        for ww in ([[w] for w in range(NP)] if PAR["ps"][h] else [list(range(NP))]):
            lo, hi = c0 + ww[0] * H2, c0 + (ww[-1] + 1) * H2
            y = lambda nm, ww=ww: ["%s%d_%d" % (nm, h, w) for w in ww]
            b = lambda nm, lo=lo, hi=hi: T[nm][:, lo // 16:hi // 16]
            sk = T.SK[:, lo + 15:hi:16]
            if own:
                V(nb, y("SK"), y("s10"), lambda b=b, sk=sk: v.tensor_scalar(b("s10"), sk, 0x3C00, 11 - n.bit_length(), A.bitwise_and, A.arith_shift_right))
                V(nb, y("s10") + ["II"], y("qi"), lambda b=b, lo=lo, hi=hi: v.tensor_tensor(b("qi"), b("s10"), T.II[:, (lo - c0) // 16:(hi - c0) // 16], A.add))
                win = T.RD[:, 16 * c0:16 * c1]
            else:
                V(nb, y("SK"), y("s10"), lambda b=b, sk=sk: v.tensor_scalar(b("s10"), sk, 0x3C00, None, A.bitwise_and))
                V(nb, y("s10") + x("CC"), y("qi"), lambda b=b: v.tensor_tensor(b("qi"), b("s10"), b("CC"), A.add))
                win = T.RT2[:]
            V(nb, y("qi"), y("qo"), lambda b=b: v.tensor_copy(b("qo"), b("qi")))
            V(GA * (hi - lo), y("qo") + rdn, y("Qo"), lambda b=b, lo=lo, hi=hi, win=win: v.tensor_copy(T.Qo[:, lo:hi], win.indirect(b("qo"))))
        if h in PAR["dt"]:
            D = T["sW%d" % h]
            V(n, [wfn], x("W32"), lambda: v.tensor_copy(N_("W32"), N_(wf)))
            DMA(3.0, x("W32"), x("sW"), [pr_ for par, lo in ((0, 8), (1, 0), (1, 16)) for pr_ in
                                         ((D[2 + par::2, lo:lo + 16, :], T.W32[0:112, c0:c1]), (D[par, lo:lo + 16, :], T.W32[112:128, c0:c1]))])
            DMA(4.0, x("sW"), ["NT%d_0" % h, "NT%d_4" % h], [(T.NT[k::8, 17 * c0:17 * c0 + 8 * n], D[:, 9 + k:17 + k, :]) for k in range(8)])
        else:
            for l4 in (0, 4):
                table(h, range(l4, l4 + 4), x("W16") + ["R1_%d" % (l + 1) for l in range(l4, l4 + 4)], lambda l: [(T.R1[:, l, :], N_("W16"))])

    def upart(vis, hh):
        N_, Wd, x = views(hh)
        V(1, x("U"), x("u16"), lambda: v.tensor_copy(Wd("u16"), Wd("U")))
        V(1, x("U"), x("u15"), lambda: v.tensor_scalar(Wd("u15"), Wd("U"), 15, None, A.bitwise_and))
        V(1, x("u15") + ["IW"], x("oT"), lambda: v.tensor_tensor(Wd("oT"), Wd("u15"), Wd("IW"), A.add))

    def qpart(vis, h):
        N_, Wd, x = views([h])
        V(n, pcs("Qo", h), x("Qi"), lambda: v.tensor_copy(N_("Qi"), N_("Qo")))
        V(GA * n, x("Qi", "u16") + IOTn, x("pr"), lambda: v.tensor_tensor(N_("pr"), T.IOT[:].indirect(Wd("u16")), N_("Qi"), A.mult))
        V(n, x("pr"), x("ps"), lambda: v.tensor_scalar(N_("ps"), N_("pr"), 5, None, A.arith_shift_right))
        V(2 * n, x("Qi", "ps"), x("pr"), lambda: v.tensor_tensor(N_("pr"), N_("ps"), N_("Qi"), A.add))
        V(n, x("pr"), x("ps"), lambda: v.tensor_scalar(N_("ps"), N_("pr"), 4095, None, A.bitwise_and))
        V(n, x("ps"), x("F16"), lambda: v.tensor_scalar(N_("F16"), N_("ps"), -2048.0, None, A.add))
        V(n, x("Qi"), x("q1"), lambda: v.tensor_scalar(N_("q1"), N_("Qi"), 1, None, A.bitwise_and))
        V(n, x("q1"), x("ee"), lambda: v.tensor_scalar(N_("ee"), N_("q1"), -2.0, -2047.0, A.mult, A.add))
        V(2 * n, x("ee", "Qi"), x("CQ"), lambda: v.tensor_tensor(N_("CQ"), N_("ee"), N_("Qi"), A.add))

        def terms(l):
            j = 16 - l
            return ([(T.SW[:, j - 1, :], N_("W16")), (T.SA[:, j - 1, :], N_("CQ"))] if j else []) + ([(T.SE[:, j, :], N_("F16"))] if j < 8 else [])
        for ls in ((8, 9, 10, 11), (12, 13, 14), (15, 16)):
            table(h, ls, x("W16", "CQ", "F16") + ["S%s%d" % (c, 16 - l) for l in ls for c in ("WA" if l < 16 else "") + ("E" if l > 8 else "")], terms)

    def gaps(vis, h):
        N_, Wd, x = views([h])
        c0, c1 = h * n, (h + 1) * n
        PC, pc = T["PC%d" % h], "PC%d" % h
        PE(n, ["ID", "THn"], [pc], [(PC[:, 0:n], T.ID[:], T.THn[:], True, False)])
        av = []
        for w in range(NP):
            w0 = h * n + w * H2
            pn = "%d_%d" % (h, w)
            way = PAR["way"][h * NP + w]
            win = XV.indirect(T.Qo[:, w0:w0 + H2])
            dd, ab = T.DD[:, 16 * w0:16 * (w0 + H2)], T.AB[:, w0:w0 + H2, :]
            abn = ["AB%s_0" % pn, "AB%s_1" % pn]
            at = lambda buf, k, w0=w0: T[buf][:, 16 * w0 + k:16 * (w0 + H2):16]
            if way == "A":
                ACT(GA * 16 * H2, ["Qo" + pn, "X"], ["DD" + pn], lambda dd=dd, win=win: a.activation(dd, win, AF.Identity))
                diffs(lambda k, at=at: at("DD", k), ["DD" + pn], lambda k, at=at: at("XW", k), two("XW", pn), w0, "AB" + pn)
            else:
                V(GA * 16 * H2, ["Qo" + pn, "X"] + two("XW", pn), ["DD" + pn],
                  lambda dd=dd, win=win, w0=w0: v.tensor_tensor(dd, win, T.XW[:, 16 * w0:16 * (w0 + H2)], A.subtract))
                ACT(16 * H2, ["DD" + pn], abn, lambda dd=dd, ab=ab: a.activation(ab, dd, AF.Abs))
            PE(16 * H2, abn + ["ZG"], [pc],
               [(PC[:, w * H2:(w + 1) * H2], T.ZG[:, 15 - m:143 - m], T.AB[:, w0 + m:w0 + H2:16, :], False, m == 15 and w == NP - 1) for m in range(16)], acc=True)
            av += [(w, at("DD", 15))] + ([(w, at("XW", 15))] if way != "A" else [])
        pooled(n + H2 * len(av), x("X0") + pcs("DD", h) + [y for w in range(NP) for y in two("XW", "%d_%d" % (h, w))] + ["HID"],
               lambda P: [(P[:, 0:n], T.HID[:], N_("X0"), True, False)] +
                         [(P[:, w * H2:(w + 1) * H2], T.HID[:], r_, False, i == len(av) - 1) for i, (w, r_) in enumerate(av)],
               n, [], x("AV"), plus(N_("AV"), n, -0.25)[:1])
        ACT(n, ["BA"] if vis else [], [pc] + x("Zs"), lambda: a.activation(N_("Zs"), PC[:, 0:n], AF.Sign, bias=T.BA[:] if vis else -2048.5))
        V(n, x("Zs") + ["D1"], x("LS"), lambda: v.tensor_tensor_scan(N_("LS"), N_("Zs"), T.D1[:], -8.0, A.max, A.add))
        V(nb, x("LS"), x("no"), lambda: v.tensor_scalar(Wd("no"), T.LS[:, c0 + 15:c1:16], -8.0 * n, -40.0 * n, A.mult, A.add))
        V(nb, x("LS"), x("rep"), lambda: v.tensor_scalar(Wd("rep"), T.LS[:, c0 + 15:c1:16], -5.9995, None, A.is_lt))
        pooled(128, x("rep") + ["UN", "ID", "II"], lambda P: [(P[:, 0:nb], T.ID[:], Wd("II"), True, False), (P[:, 0:nb], T.UN[:], Wd("rep"), False, True)],
               nb, x("oT"), x("of"), [("V", lambda P: v.tensor_tensor(Wd("of"), Wd("oT"), P[:, 0:nb], A.max))])
        V(nb, x("of"), x("oo"), lambda: v.tensor_scalar(Wd("oo"), Wd("of"), 4096.0, None, A.add))

    def tail(vis, h):
        N_, Wd, x = views([h])
        c0, c1 = h * n, (h + 1) * n
        last = vis == VIS - 1
        xn = "XO" if last and h == 0 else "X"
        V(SCA * n, x("AV", "oo"), [xn], lambda: v.tensor_copy(T[xn][:].indirect(Wd("oo")), N_("AV")))
        ntn = x("no") + ["NT%d_%d" % (h, j) for j in (0, 4, 8, 12, 15)]
        win = T.NT[:, 17 * c0:17 * c1].indirect(Wd("no"))
        if last:
            DMA(3.0, [xn], x("yx"), [(T.yx[:, 16 * c0:16 * c1], T[xn][:, 16 * c0:16 * c1])])
            gather(n, ntn, x("NF"), N_("NF"), win)
            DMA(2.0, x("NF"), x("yw"), [(T.yw[0:112, c0:c1], T.NF[16:128, c0:c1]), (T.yw[112:128, c0:c1], T.NF[0:16, c0:c1])], "D")
        else:
            st, nx = "ST%d" % (vis + 1), "WF%d" % (vis + 1)
            V(GA * n, ntn, ["%s_%d" % (st, h)], lambda: v.tensor_copy(N_(st), win))
            tag = "ar%d_%d" % (vis + 1, h)
            add([("R", 1.0, lambda: g.remote_dma(N_(nx), N_(st), T.sem[tag], T.sem.ls, pid, rid, msk))],
                ["%s_%d" % (st, h)], ["%s_%d" % (nx, h)], lat=PAR["rl"], tag=tag)

    for vis in range(VIS):
        cur[2] = vis
        for h in hs:
            head(vis, h)
        for hh in ([hs] if "u" in PAR["sh"] else [[h] for h in hs]):
            upart(vis, hh)
        for h in hs:
            qpart(vis, h)
        if vis == VIS - 1:
            DMA(3.0, ["X"], ["XO"], [(T.XO[:, 0:2048], T.X[:, 0:2048])])
        cur[1] = "g"
        for h in hs:
            gaps(vis, h)
        cur[1] = ""
        for h in hs:
            tail(vis, h)
        if vis < VIS - 1:
            cur[0] = 0
            pooled(64, ["grep%d" % h for h in ()] + ["rep%d" % h for h in hs] + ["ONE"], lambda P: [(P[:, 0:16], T.ONE[:], T.rep[:], True, True)],
                   40, [], ["AC", "AS"], [("A", lambda P: a.activation(T.AC[:], P[:, 0:16], AF.Identity, accum_out=T.AS[:]))])
            V(1, ["AS"], ["AI"], lambda: v.tensor_copy(T.AI[:, 0:1], T.AS[:]))
            V(1, ["AI"], ["AJ"], lambda: v.tensor_scalar(T.AI[:, 1:2], T.AI[:, 0:1], 31, None, A.bitwise_and))
            V(1, ["AJ"], ["BA"], lambda: v.tensor_scalar(T.BA[:], T.AI[:, 1:2], -8.0, -2048.5, A.mult, A.add))
    return ops, len(eng)


PHYS = {"V": "V", "A": "A", "D": "A", "T": "T", "G": "G", "R": "G", "S": "S"}


def name(o):
    return o["ph"] + ((o["pre"][-1] + "*") if o["take"] else o["rd"][0] + ">" if o["wr"][-1][:2] == "PC" else o["wr"][-1])


ORDER = """SU0* Ro0@ AS+ sq1@ SU0 R160@ IOT2048@ CC1@ rs2@ XRb0_0@=A XRa0_0@=V RD0_1*@ U0 NT1_4@ vv0 AI+ sq0 CC0 c161@ SE3@=V AB0_0_0*@ c160 Ro1@ AJ+ Ro0 R0_3@=V R161@ AB0_0_1*@ XRa0_1@=V XRa0_0=V XRb0_0=A R0_2@=A XRb0_1@=A IW@ AB0_0_0@ RD1_0*@ IOT3072@ XRb1_0@=V XRb0_1=V XRa0_1=A AB0_1_0*@ AB0_0_1* AB0_0_1@ RD1_1*@ AB0_0_0* R0_10@=A W161 XWb1_0=A AB0_1_0@ W320 RD0_2*@ sW0 AB0_1_1*@ SE4@=A RD1_1@=V W0u1* RD0_2@=A AB0_0_0 AB0_1_1* T316@ SK0_0*@ W0u1 RS@ X01=V u151@ AB0_1_1@ AB0_0_1 J0@ RD1_0@=V W321 AB1_0_1*@ BA+ SU1* T30@ sW1 XRb1_1@=A AB0_1_1 CU0@ SK0_0@ SU1 SW4@=V SK0_0* J0'@ RD0_0*@ u161@ U1 XWa1_0@=V CU112@ SK0_1*@ XWa1_0=A vv1 AB0_1_0* u151 sq1 u161 RD1_3*@ CC1 s100_0@ SK0_0 SK0_1@ c161 AB0_1_0 RD0_3*@ SR@ s100_0 s100_1@ RD0_1@=A Ro1 RD0_0@=V AB1_1_0*@ XWb0_1=V XRb1_0=A SK0_1* RD0_3@=A AB1_0_0*@ qi0_0@ qi0_1@ AB1_1_0@ SA1@=V AB1_1_1@ qo0_0@ XWb1_0@=A AB1_1_1 AB1_0_1 AB1_0_0 qo0_1@ AB1_1_1*@ Qo0_0@ Qo0_1@ SA7@=V SA8@=V SA4@=V RD1_2*@ SK0_1 Qi0@ D1'@=A qi0_0 XRb1_1=A gDD0_0@ SA6@=A s100_1 NT1_4 AB1_0_0* AB1_0_0@ qo0_0 qi0_1 Qo0_0 qo0_1 AB1_0_1* gDD0_0 NT0_4 AB1_0_1@ gDD0_1@ AB1_1_1* gAB0_0_1@ AB1_0_0>@ AB1_1_0* Qo0_1 pr0@ Qi0 gDD0_1 AB1_0_0> SA2@=V AB1_1_0 XWb1_1@=A q10@ AB1_1_0>@ ps0@ gAB0_0_1 AB1_1_0> pr0'@ gAV0*@ pr0 ee0@ gAB0_1_1@ gAV0* SK1_1 SK1_1@ ps0'@ ps0 UN@ gAB0_1_1 s101_1@ gID>1@ gAB0_0_0> s101_1 RD1_3@=V gAB0_0_0>@ pr0' qi1_1 SA3@=A RD1_2@=A qi1_1@ gAB0_1_0>@ ps0' F160@ q10 qo1_1 XWa1_1=A qo1_1@ F160 ee0 gAB0_1_0> CQ0@ XWa1_1@=A Qo1_1@ NT0_15*@ Qo1_1 SA5@=V CQ0 IW'@=V gDD1_0@ gZs0 NT0_8*@ gDD1_0 gDD1_1 gID>0- gZs0@ NT0_8* NT0_12@=A gDD1_1@ gLS0@ NT0_12*@ WI@- X0@- CW16@- D1@- RT@- th0@- ONE@- wt0@- NT0_15* P@- NT0_12* FC0@- oT1@ Pa@- GW@- gLS0 Pg@- NT0_8=A NT0_8@=V XWb1_1=V FCgs@- CW0@- FCa0@- FCg15@-=A E32@- gAB1_1_0*@ NT0_12=A FCps@-=A gno0@ SH@- NT0_15@=V FCa16@-=A BK1@- gAB1_1_0 ID@- gAB1_0_1@ FCgs15@-=V gAB1_0_1 Qi1@ NT0_15=V gAB1_1_0* HID@-=A gAB1_1_1*@ X144@- ST_0@ gno0 EQ1@- NID@-=A q11@ Qi1 WF_1@- ST_0 K16@- gAB1_1_1* q11 Pl@- gAV0@ WF_0@ gAB1_1_1@ ZD@- WF_0 pr1 C0@- GE@- gAB1_0_0>@ pr1@ KB@-=A EQ0@- gAV1* ee1 grep0@ W161@- SW8@-=A grep0 gID>1 ps1@ BLK@- gAB1_1_0@ oT1 R0_1@-=A C0'@- gof0* gAV1*@ ps1 ZX@- gAB1_1_1 Ph@- R0_9@-=A pr1'@ CQ1 SE2@-=V gof0*@ W0u1*@- gAB1_0_0> SE5@-=A R0_13@-=V IOT0@- W160@- gof0@ R0_15@-=A pr1' SW2@-=V ee1@ gAB1_1_0>@ NF0=A FCth@- SW6@-=A ps1'@ W0u0*@- NB@- gof0 gAB1_1_0> SE0@-=A W0u1@- ps1' W320@- F161@ R0_4@-=A gAV1 W321@- CQ1@ gZs1@ R0_12@-=A F161 sW0@- FCwL@- SW5@-=V SW3@-=A goo0 gZs1 NT1_8=A gAV0 gLS1@ NT1_8* R0_5@-=V BH@-=A NT1_15*@ goo0@ gLS1 R0_0@-=V sW1@- R0_8@-=A grep1@ AS*@ W0u0@- SW7@-=A R0_14@-=V SE6@-=V gof1*@ grep1 XO0 SW1@-=V SE7@-=A X0 R0_7@-=V NT1_8*@ R0_11@-=V gof1@ gof1* ZG@- R0_6@-=A AS@ C1@- X0'@ AS* NT1_12* NT1_15@=A XWb0_0@-=A THd@- gof1 yx0 BL@-=V X00@-=V THn*@- goo1@ goo1 C1'@- AI@ gno1 NT1_12*@ X01@-=V gno1@ X1 NT1_15* NT1_8@=A SU0*@- AJ@ NT1_12=A THn@- gAV1@ II@- SU1*@- IOT1024@- yx1 W160- XO1- gID>0@- XWb0_0-=A BA@ SE1@-=V NT1_12@=A NT1_15=V SU0@- X1@ SU1@- NF1=A W0u0*- U0@- XWb0_1@-=A ST_1 yw1 vv0@- ST_1@ yw0 sq0@- WF_1 W0u0- U1@- WF_1'@ CC0@- X00-=V vv1@- c160@- NT0_4@- II'@-=V"""
ORDER = """SU0* AJ@+ U0 c161@ SU0 Ro0@ rs2@ AS+ Ro1@ vv0 SA5@=V R160@ R161@ XRb0_1@=V sq0 sW0 RD0_3*@ BA@+ AI+ CC0 AJ+ RD0_2*@ IOT1024@ c160 BA+ XRb0_0=A NT1_4@ XRa0_0=V AB0_0_1@ XWb1_0@=A AB0_0_1*@ Ro0 SA1@=V XRa0_1@=V XRb1_1@=V W0u1* AB0_0_0* AB0_0_1* XRb0_1=V XRa0_1=A AB0_0_0*@ XWb1_0=A sW1 RD1_0@=V IOT2048@ RD1_0*@ RD0_3@=A W161 XWa1_0=V RD1_2*@ u161@ AB1_1_0*@ AB0_0_0@ AB0_0_1 AB0_1_0* RS@ W0u1 RD0_0*@ X01=V XRb1_0@=V SW5@=V W321 AB0_0_0 RD0_1*@ SK0_0*@ RD0_0@=A AB0_1_1*@ SU1* CU112@ XWb1_1=A SU1 SK0_0* CU0@ SK0_0@ U1 NT0_4 RD0_1@=A vv1 AB0_1_1* AB0_1_0 sq1 u151@ u151 II'@=A s100_0@ CC1 SA7@=V oT1 AB0_1_0*@ c161 AB0_1_1 IW'@=A AB0_1_1@ AB1_0_0*@ SK0_0 SE0@=V Ro1 RD1_1*@ qi0_0@ SW2@=V XWb0_1=V RD1_3*@ qo0_0@ XRb1_0=A AB0_1_0@ AB1_1_0@ AB1_0_0@ SK0_1* RD1_1@=A Qo0_0@ XWa1_0@=V AB1_1_1*@ AB1_0_1 gDD0_0@ SK0_1*@ SK0_1 s100_0 XRb1_1=A s100_1 NT1_4 qi0_0 AB1_1_1 AB1_0_1*@ qi0_1 SK0_1@ qo0_0 SW3@=V qo0_1 s100_1@ AB1_0_1* Qo0_0 RD1_3@=A Qo0_1 AB1_0_0* u161 gDD0_0 Qi0 AB1_0_0 AB1_0_1@ D1'@=A qi0_1@ AB1_1_1* AB1_1_1@ SA6@=V qo0_1@ SA2@=V AB1_0_0>@ Qo0_1@ AB1_1_0* SA4@=V SK1_1@ gDD0_1@ AB1_1_0>@ AB1_0_0> gDD0_1 pr0 AB1_1_0 gAB0_0_1@ RD1_2@=A gAB0_0_1 AB1_1_0> gAV0*@ Qi0@ s101_1@ gAB0_0_0>@ pr0@ q10@ ps0@ gAB0_0_0> q10 ps0 SK1_1 XWa1_1@=A SE4@=A gAB0_1_1@ pr0' qi1_1@ ee0@ gAB0_1_0>@ pr0'@ NT0_15=A gDD1_1 gDD1_1@ CQ0@ s101_1 ps0' gAB0_1_1 qo1_1@ gZs0 qi1_1 gID>1@ XWa1_1=A ee0 NT0_12*@ gAB0_1_0> ps0'@ NT0_8*@ qo1_1 F160 XWb1_1@=A gZs0@ Qo1_1@ Qo1_1 F160@ gAV0* CQ0 gDD1_0@ gDD1_0 FC0@- NT0_12* WI@- X0@- P@- ONE@- RT@- th0@- D1@- wt0@- NT0_12=A Pa@- NT0_8* FCa0@- Pg@- FCgs@- FCg15@-=A E32@- FCa16@-=A NT0_15*@ FCps@-=A NT0_12@=V NT0_15* gLS0 X144@- EQ0@- NT0_8@=A NT0_8=V gAB1_1_1* gLS0@ CW16@- gAB1_1_0*@ NT0_15@=V R0_6@-=A R0_11@-=V CW0@- R0_13@-=A GE@- C0@- gno0@ gAB1_0_1@ gno0 gID>1 SH@- gAB1_0_1 R0_14@-=A gAB1_1_1*@ gAB1_1_0* ST_0 WF_1@- R0_1@-=A K16@- Qi1@ R0_2@-=A Qi1 ST_0@ ID@- WF_0@ gID>0- WF_0 oT1@ gAV1*@ SE6@-=A ZX@- gAV1* GW@- grep0@ pr1 Ph@- gAV0 q11@ R0_7@-=V R0_0@-=A FCth@- pr1@ EQ1@- grep0 gAB1_1_1@ SE5@-=A gAB1_0_0>@ gAB1_0_0> R0_12@-=A FCgs15@-=A SE3@-=V ps1 ps1@ W320@- SW7@-=V HID@-=A q11 gAB1_1_0@ R0_10@-=A W160@- pr1' pr1'@ R0_3@-=A gof0* SE1@-=A Pl@- W0u0*@- IW@- J0@- ee1@ NID@-=A C0'@- ps1' IOT0@- UN@ SW1@-=A ee1 ps1'@ gAB1_1_0>@ SW4@-=V R0_9@-=V ZG@- gAB1_1_0> SE2@-=A sW0@- gof0 CQ1@ FCwL@- F161 THd@- W161@- gAB1_1_1 CQ1 F161@ BH@-=A gof0*@ gAB1_1_0 BLK@- W0u1*@- XO0 gAV0@ BK1@- R0_5@-=A NB@- SE7@-=A gZs1@ W0u0@- goo0 gZs1 NT1_8*@ SW6@-=V gAV1@ NT1_8* BL@-=V gLS1@ ZD@- KB@-=A gLS1 THn*@- yx0 gof0@ W0u1@- R0_15@-=V grep1@ grep1 goo0@ gAV1 THn@- gno1@ SW8@-=A R0_4@-=V NT1_15*@ NT1_8@=A XWb0_0@-=A gno1 NT1_15=A X01@-=V NT1_8=A AS*@ X0 gof1 J0'@- X0'@ gof1* X00@-=V gof1*@ SA8@-=A T30@- NT1_15* NT1_12* NT1_12*@ SU1*@- XWb0_1@-=A T316@- gof1@ AS@ RD0_2@-=A XRa0_0@-=A XRb0_0@-=A W321@- SU0*@- NT1_15@=A goo1@ goo1 SU1@- C1@- gID>0@- sW1@- AS* SR@- W160- X1@ SU0@- NT1_12=A NT1_12@=A X1 NF0=V W0u0*- U1@- yx1 C1'@- AI@ U0@- yw0 vv1@- XO1- XWb0_0-=A ST_1 SA3@-=V ST_1@ NF1=A vv0@- II@- sq1@- W0u0- IOT3072@- sq0@- WF_1 WF_1'@ yw1 X00-=V CC0@- NT0_4@- CC1@- R0_8@-=V W320- c160@-"""


def classes(ops):
    seen, out = {}, []
    for o in ops:
        c = name(o)
        if c[:2] in ("ST", "WF") and c[3:4] == "_":
            c = c[:2] + c[3:]
        if c in ("X", "gID>", "XO"):
            c += str(o["ch"])
        seen[c, o["v"]] = seen.get((c, o["v"]), -1) + 1
        out.append(c + "'" * seen[c, o["v"]] + ("@" if o["v"] == 0 else ""))
    return out


def places(text):
    words = text.split()
    out = {}
    for r, x in enumerate(words):
        x, _, q = x.partition("=")
        c = x.rstrip("+-")
        out[c] = (r + len(words) * (x.count("+") - x.count("-")), q)
    return out


def ordered(ops, bank):
    lastw, readers = {}, {}
    for i, o in enumerate(ops):
        d = set(lastw[r] for r in o["rd"] if r in lastw)
        for w in o["wr"] + o["pre"]:
            if w in lastw:
                d.add(lastw[w])
            d.update(readers.get(w, ()))
        o["dep"] = sorted(d - {i})
        for r in o["rd"]:
            readers.setdefault(r, []).append(i)
        for w in o["wr"]:
            lastw[w] = i
            readers[w] = []
    place = places(ORDER)
    key = []
    for o, c in zip(ops, classes(ops)):
        x = [y for y in o["alts"] if y[0] == place[c][1]] or o["alts"]
        o["q"], o["us"], o["fn"] = x[0]
        key.append(place[c][0] + len(place) * o["v"])
    free, fin, order = {q: 0.0 for q in "VATGS"}, {}, []
    rel = {b: (0.0, None) for b in POOL}
    todo = sorted(range(len(ops)), key=lambda i: (key[i], i))
    while todo:
        i = next(i for i in todo if all(d in fin for d in ops[i]["dep"]) and (rel or not ops[i]["take"]))
        o = ops[i]
        if o["take"]:
            b = min(rel, key=lambda k: (rel[k][0], k))
            if rel[b][1] is not None:
                o["dep"] = sorted(set(o["dep"] + [rel[b][1]]))
            bank[o["take"]] = b
            del rel[b]
        q = PHYS[o["q"]]
        o["start"] = max([free[q]] + [fin[d] + (0.0 if o["acc"] and ops[d]["q"] == "T" else HOP) for d in o["dep"]])
        free[q] = o["start"] + o["us"]
        fin[i] = free[q] + o["lat"]
        if o["give"]:
            rel[bank[o["give"]]] = (fin[i], i)
        todo.remove(i)
        order.append(i)
    return order, max(fin.values())


def rank_program(g, core, T, topo):
    rank = T.rank_of(core)
    if rank is None:
        return
    bank = {}
    ops, neng = build(g, core, rank, T, topo, bank)
    order, _ = ordered(ops, bank)
    S = T.sem
    handle = {"V": g.vector, "A": g.scalar, "T": g.tensor, "G": g, "S": g.sync}
    cnt = {"V": 0, "A": 0, "T": 0, "G": 0}
    known = {q: {} for q in handle}
    nd, nsend = 0, 0
    used = {}
    for i in order:
        o = ops[i]
        q = PHYS[o["q"]]
        kn = known[q]
        need = {}
        for d in o["dep"]:
            sm, val = ops[d]["done"]
            if o["acc"] and sm == "qT":
                continue
            if kn.get(sm, 0) < val:
                need[sm] = max(need.get(sm, 0), val)
        items = sorted(need.items(), key=lambda kv: -max(ops[d]["start"] for d in o["dep"] if ops[d]["done"][0] == kv[0]))
        for sm, val in items:
            if kn.get(sm, 0) >= val:
                continue
            handle[q].wait_ge(S[sm], val)
            kn[sm] = val
            for d in o["dep"]:
                if ops[d]["done"] == (sm, val):
                    for k2, v2 in ops[d]["kn"].items():
                        if kn.get(k2, 0) < v2:
                            kn[k2] = v2
        ins = o["fn"]()
        if o["q"] in ("S", "D"):
            sm = "d%d" % nd
            nd += 1
            for one in ins:
                one.then_inc(S[sm], 16)
            o["done"] = (sm, 16 * len(ins))
            used[sm] = 16 * len(ins)
        elif o["q"] == "R":
            nsend += 1
            o["done"] = (o["tag"], neng)
            used[o["tag"]] = neng
        else:
            cnt[q] += 1
            sm = "q" + q
            ins.then_inc(S[sm], 1)
            o["done"] = (sm, cnt[q])
            used[sm] = cnt[q]
        o["kn"] = {} if o["q"] == "R" else dict(kn)
    used["ls"] = nsend * neng
    for sm, val in used.items():
        if known["G"].get(sm, 0) < val:
            g.wait_ge(S[sm], val)
